import numpy as np, ml_dtypes
CORES = [10,34,74,98]
N = 4
import mx_ref
BF = ml_dtypes.bfloat16
def gentries(a):
    return np.ascontiguousarray(a.reshape(8, 16, -1).transpose(0, 2, 1)).reshape(8, -1)
def gtable(e):
    e = np.asarray(e); return np.ascontiguousarray(e.reshape(8, -1, 16).transpose(0, 2, 1)).reshape(128, -1).astype(np.int32)
def gcols(t, e):
    v = np.concatenate([t.reshape(8, 16, -1, 4), np.zeros((8, 16, 1, 4), BF)], axis=2)
    return np.ascontiguousarray(np.stack([v[g][:, e[g]] for g in range(8)])).reshape(128, -1)
def pick(q, e):
    c = np.concatenate([q[0].reshape(128, -1, 4), np.zeros((128, 1, 4), np.uint8)], axis=1); s = np.concatenate([q[1], np.ones((16, 1), np.uint8)], axis=1)
    return (np.ascontiguousarray(c[:, e].reshape(128, -1)), np.ascontiguousarray(s[:, e]))
def join(*qs):
    return (np.concatenate([q[0] for q in qs], axis=1), np.concatenate([q[1] for q in qs], axis=1))
def put(q, e, v):
    c, s = q[0].reshape(128, -1, 4).copy(), q[1].copy(); c[:, e] = v[0].reshape(128, -1, 4); s[:, e] = v[1]
    return (c.reshape(128, -1), s)
def pk(c, s):
    return (np.ascontiguousarray(c), mx_ref.live(s))
def emit(q):
    return q[0], q[1]
def packed(v, rng):
    q = [mx_ref.quantize(np.ascontiguousarray(v[r])) for r in range(N)]
    return np.stack([a for a, b in q]), np.stack([mx_ref.plane(b, rng) for a, b in q])
def values_of_codes():
    e, c = np.zeros((128, 128, 4), np.float32), np.zeros((128, 2, 4), np.uint8)
    e[np.arange(128), np.arange(128), 0] = 1
    c[:127, :, 0] = np.arange(256).reshape(2, 128).T[:127]
    return mx_ref.matmul(mx_ref.quantize(e.reshape(128, 512).astype(BF)), (c.reshape(128, 8), np.full((16, 2), 127, np.uint8))).T.reshape(-1).astype(np.float64)
CODE_VALUE, SCALE_VALUE = values_of_codes(), 2.0 ** (np.arange(256) - 127.0)
def decode(q):
    return (CODE_VALUE[q[0]].reshape(16, 8, -1, 4) * SCALE_VALUE[q[1]][:, None, :, None] + 0.0).reshape(128, -1).astype(np.float32)
def f(rng, *shape):
    return mx_ref.flush((rng.standard_normal(shape, dtype=np.float32) * np.exp2(rng.integers(-2, 3, shape[:-1] + (1,)))).astype(BF))
def wide(rng, *shape, cols=0):
    v = rng.standard_normal(shape, dtype=np.float32) * np.exp2(rng.integers(-12, 13, shape)).astype(np.float32)
    if cols: v *= np.repeat(np.exp2(rng.integers(-cols, cols + 1, shape[:-2] + (1, shape[-1] // 4))) * (rng.random(shape[:-2] + (1, shape[-1] // 4)) > 0.0625), 4, axis=-1).astype(np.float32)
    return mx_ref.flush(v.astype(BF))
C, M, R = 384, 160, 3
def numbers_of(rng):
    return {"x": np.array(f(rng, N, 128, 4 * C)), "u": np.array(f(rng, N, 128, 512)), "v": np.array(f(rng, N, 128, 512))}
def shuffled(rng):
    return np.argsort(rng.random((N, 8, C)), axis=2)
def stored(t):
    return {"cf": np.stack([gtable(t[r]) for r in range(N)])}
def weights(rng, w):
    c, p = packed(np.ascontiguousarray(w).reshape(N, 128, 2048), rng)
    return {"wc": c, "ws": p}
def layers(rng, still=[]):
    w = np.array(f(rng, N, 128, 2048)).reshape(N, 8, 16, 4, 8, 16, 4)
    for i in still:
        w[:, :, i] = 0
        w[:, :, :, :, :, i] = 0
    return weights(rng, w)
def setup_inputs(rng):
    return {**numbers_of(rng), **stored(shuffled(rng)), **layers(rng)}
def setup_inputs_ties(rng):
    d = numbers_of(rng)
    x = d["x"].reshape(N, 8, 16, C, 4)
    x[:, :, :2] = 0
    x[:, :, 0, :, 0] = rng.integers(0, 4, (N, 8, C)).astype(np.float32).astype(BF)
    x[:, :, 1, :, 0] = rng.integers(0, 3, (N, 8, C)).astype(np.float32).astype(BF)
    u = d["u"].reshape(N, 128, 128, 4)
    u[:, :, ::16] = 0
    u[:, :, 1] = 0
    o = rng.permutation(N)
    for r in range(N):
        s = 0.0 if r == o[0] else -1.0 if r == o[1] else 1.0
        for h in range(0, 128, 16): u[r, h, h, 0] = s
        u[r, 1, 1, 0] = s
    return {"x": x.reshape(N, 128, 4 * C), "u": u.reshape(N, 128, 512), "v": d["v"], **stored(shuffled(rng)), **layers(rng, [0, 1])}
def setup_inputs_near(rng):
    d = numbers_of(rng)
    o = rng.permutation(N) % 4
    c = np.where(o % 2 == 0, 1.0, -1.0)
    x = d["x"].astype(np.float32).reshape(N, 8, 16, C, 4)
    x[:, :, 0] = 0
    x[:, :, 8:] = 0
    x[:, :, 0, :, 0] = c[:, None, None]
    s = rng.integers(0, 16, (N, 8, C))
    x[:, :, 8] = ((s[:, :, :, None] >> np.arange(4)) & 1) * np.exp2(np.arange(4) - 23.0)
    x[:, :, 11, :, 0] = 2.0 ** -10
    u = d["u"].reshape(N, 128, 128, 4)
    u[:, :, ::16] = 0
    u[:, :, 1] = 0
    for r in range(N):
        for g in 1 + rng.permutation(7)[:4]: x[r, g, 0, rng.integers(C), 0] = c[r] * 2.0 ** 29
        if o[r] == 1: x[r, 0, 0, rng.integers(C), 0] = -2.0 ** 29
        if o[r] == 3:
            i = rng.integers(0, 2, (8, C))
            x[r, :, 8:] = 0
            x[r, :, 10, :, 0] = (1.0 + 0.125 * i) * 2.0 ** -30
            x[r, :, 12, :, 0] = (1.125 - 0.125 * i) * 2.0 ** -30
        k = 2.0 ** -30 if o[r] == 2 else 1.0
        for a, h in [(0, 1)] + [(h, h) for h in range(0, 128, 16)]:
            if o[r] == 3:
                u[r, a + 10, h, 0] = 1.125 * 2.0 ** -30
                u[r, a + 12, h, 0] = 2.0 ** -30
            else:
                u[r, a, h, 0] = k
                u[r, a + 8, h] = k
                u[r, a + 11, h, 0] = k
    return {"x": x.reshape(N, 128, 4 * C).astype(BF), "u": u.reshape(N, 128, 512), "v": d["v"], **stored(shuffled(rng)), **layers(rng, [0] + [8, 9, 10, 11, 12, 13, 14, 15])}
def swings(rng):
    h, j, a = np.zeros(C, int), 0, 200
    while j < C:
        i = np.arange(min(int(rng.integers(10, 25)), C - j))
        n = np.where((i > 8) & (rng.random(len(i)) < 0.25), rng.integers(2, np.maximum(i, 3)), i)
        h[j:j + len(i)] = (1 - 2 * (i % 2)) * (a - 8 * n)
        j, a = j + len(i), a + 1
    return h
def setup_inputs_deep(rng):
    d = numbers_of(rng)
    x = d["x"].reshape(N, 8, 16, C, 4)
    o = rng.permutation(N)
    t = np.arange(C) - C // 2
    small = (1.0 + (2 * rng.integers(0, 64, (N, 8, 8, C, 4)) + 1) * 2.0 ** -7) * np.exp2(-rng.integers(8, 15, (N, 8, 8, C, 4)).astype(np.float64))
    small = small * rng.choice([-1.0, 1.0], small.shape)
    small[:, :, 0, :, 0] = np.where(rng.random((N, 8, C)) < 0.5, 1.875, 1.96875)
    x[:, :, 8:] = small.astype(np.float32).astype(BF)
    x[:, 0, 0] = 0
    u = d["u"].reshape(N, 128, 128, 4)
    u[:, :, 1] = 0
    u[:, 0, 1, 0] = 16
    u[:, 0, 1, 1] = 1
    for r in range(N):
        h = t if r == o[0] else -t if r == o[1] else swings(rng)
        x[r, 0, 0, :, 0] = (np.sign(h) * (np.abs(h) // 16)).astype(np.float32).astype(BF)
        x[r, 0, 0, :, 1] = (np.sign(h) * (np.abs(h) % 16)).astype(np.float32).astype(BF)
    return {"x": x.reshape(N, 128, 4 * C), "u": u.reshape(N, 128, 512), "v": d["v"], **stored(shuffled(rng)), **layers(rng)}
def setup_inputs_ends(rng):
    d = numbers_of(rng)
    o = (np.arange(N) + int(rng.integers(N))) % 4
    x = np.zeros((N, 8, 16, C, 4))
    u = d["u"].reshape(N, 128, 128, 4)
    u[:, :, ::16] = 0
    t = shuffled(rng)
    w = np.zeros((N, 128, 4, 128, 4), np.float32)
    i = np.arange(128)
    for r in range(N):
        sign = rng.permutation(8) % 2 * 2.0 - 1.0
        wave = 2.0 ** 30 * (0.9 + 0.1 * rng.random((128, 8, 4)))
        u[r, :, 1] = 2.0 ** -30 if o[r] == 3 else 2.0 ** 30
        if o[r] == 0:
            x[r] = -2.0 ** 30 * (0.9 + 0.1 * rng.random((8, 16, C, 4)))
            u[r, :, ::16] = wave.astype(np.float32).astype(BF)
            t[r] = np.arange(C)
        if o[r] == 1:
            x[r] = 2.0 ** 30 * np.where(rng.random((8, 16, C, 4)) < 0.125, 0.8125, 0.875) * (rng.permutation(C) % 2 * 2.0 - 1.0)[:, None]
            u[r, :, ::16] = (wave * sign[:, None]).astype(np.float32).astype(BF)
            for b in range(4): w[r, i, b, i, b] = rng.choice([-1.0, 1.0], 128)
        if o[r] == 2:
            x[r] = 2.0 ** 30
            x[r, rng.permutation(8)[:4]] *= np.where(rng.random((4, 1, C, 1)) < 0.5, 0.875, 1.0)
            t[r] = np.arange(C)[::-1]
            for g in range(8): u[r, 16 * g:16 * g + 16, 16 * g] = sign[g] * 2.0 ** 30
        if o[r] == 3:
            x[r] = 2.0 ** -30 * (1.0 + 0.125 * rng.integers(0, 8, (8, 16, C, 4)))
            t[r, ::2] = np.arange(C)
            t[r, 1::2] = np.arange(C)[::-1]
            for g in range(8): u[r, 16 * g:16 * g + 16, 16 * g] = 2.0 ** -30
    d["v"] = (np.where(d["v"] < 0, -1.0, 1.0) * np.where(rng.permutation(N) % 2, 2.0 ** -30, 2.0 ** 30)[:, None, None]).astype(np.float32).astype(BF)
    return {"x": x.astype(np.float32).reshape(N, 128, 4 * C).astype(BF), "u": u.reshape(N, 128, 512), "v": d["v"], **stored(t), **weights(rng, w.astype(BF))}
def setup_inputs_spread(rng):
    d = setup_inputs(rng)
    d["x"] = wide(rng, N, 128, 4 * C, cols=6)
    return d
def check_inputs(d):
    b = []
    for k in ("x", "u", "v"):
        a = np.abs(d[k].astype(np.float32))
        if not (np.isfinite(a).all() and ((a == 0) | (a >= 2.0 ** -30) & (a <= 2.0 ** 30)).all()): b.append("a value of " + k)
    none, least, most = [emit(mx_ref.quantize(np.full((128, 16), k, np.float32).astype(BF)))[1][0, 0] for k in (0.0, 2.0 ** -30, 2.0 ** 30)]
    for r in range(N):
        if (np.sort(gentries(d["cf"][r]), axis=1) != np.arange(C)).any(): b.append("cf: a group hasn't every column once")
        if ((d["wc"][r] == 0x7F) | (d["wc"][r] == 0xFF)).any(): b.append("wc: a code that is no number")
        s = mx_ref.live(d["ws"][r])
        if ((s != none) & ((s < least) | (s > most))).any(): b.append("ws: a scale out of range")
    return b
def turning(h):
    t = np.arange(C)
    e, found = np.zeros(C, np.int64), []
    for i in range(7):
        inside = (t >= e[:, None]) & (t <= t[:, None])
        s = np.where(inside, h if i % 2 == 0 else -h, np.float32(-np.inf))
        e = C - 1 - np.argmax(s[:, ::-1], axis=1)
        found.append(e)
    found = np.stack(found + [t])
    return found, np.argmax(found == t, axis=0)
def reference(x, u, v, cf, wc, ws):
    qu = [mx_ref.quantize(u[r]) for r in range(N)]
    lay = [pk(wc[r], ws[r]) for r in range(N)]
    now = [x[r] for r in range(N)]
    reads = [gentries(cf[r]) for r in range(N)]
    for t in range(R):
        blend, low, sent = [], [], []
        for r in range(N):
            q = mx_ref.quantize(now[r])
            own = decode(q).astype(BF)
            s = mx_ref.matmul(qu[r], q) + np.float32(0.0)
            e, depth = turning(s[1])
            at = np.take_along_axis(e, np.maximum(depth - np.arange(9)[:, None], 0), axis=0)
            a = np.take_along_axis(reads[r], at[:8], axis=1)
            b = np.take_along_axis(reads[r], at[1:], axis=1)
            z = ((gcols(own, a).astype(np.float32) + gcols(own, b).astype(np.float32)) * np.float32(0.5)).astype(BF)
            o = np.argsort(-s[::16], axis=1, kind="stable")
            l, d = o[:, :M], o[:, C - M:]
            sent.append(mx_ref.quantize(gcols(z, l)))
            other = np.tile(np.arange(C), (8, 1))
            np.put_along_axis(other, l, d, axis=1)
            np.put_along_axis(other, d, l, axis=1)
            reads[r] = np.take_along_axis(other, reads[r], axis=1)
            blend.append(z)
            low.append(d)
        for r in range(N):
            came = sent[(r - 1) % N]
            made = np.stack([mx_ref.matmul(pick(lay[r], np.arange(128 * b, 128 * b + 128)), came) * np.float32(0.03125) for b in range(4)], axis=2).reshape(8, 16, M, 4)
            z = blend[r].astype(np.float32).reshape(8, 16, C, 4)
            for g in range(8): z[g][:, low[r][g]] = made[g] + z[g][:, low[r][g]]
            now[r] = z.reshape(128, 4 * C).astype(BF)
    y, op = np.zeros((N, 128, C), np.float32), np.zeros((N, 8, C), np.float32)
    oc, osc = np.zeros((N, 128, 4 * C), np.uint8), np.zeros((N, 16, C), np.uint8)
    for r in range(N):
        q = mx_ref.quantize(now[r])
        y[r] = mx_ref.matmul(mx_ref.quantize(v[r]), q)
        op[r] = reads[r]
        oc[r], osc[r] = emit(q)
    return {"y": y, "op": op, "oc": oc, "osc": osc}

@@ -1,0 +1,494 @@
+from concourse.mybir import dt, AluOpType, ActivationFunctionType
+
+C, M, ROUNDS = 384, 160, 3
+HALF = C // 2
+FIRST = 3
+WIDE = [max(128, 64 * (i + 1)) for i in range(6)]
+X4 = "float8_e4m3fn_x4"
+F32, BF = "float32", "bfloat16"
+SCRATCH = {}
+
+
+def _buf(name, cols, dtype, where="sbuf"):
+    SCRATCH[name] = (where, [128, cols], dtype)
+
+
+def _pair(name, cols):
+    _buf(name + "_q", cols, X4)
+    _buf(name + "_s", cols, "uint8")
+
+
+for _n, _c in (("xb", 4 * C), ("ub", 512), ("vb", 512), ("cb", 8 * 512), ("sig", 12 * C), ("hb", 512), ("dg", 4 * C), ("dr", C),
+               ("sgn", 3 * C), ("le", 4 * C), ("ge", 4 * C), ("mk", 8 * C), ("junk", 4 * C), ("eb", 4 * M), ("ones", C),
+               ("foldb", C)):
+    _buf(_n, _c, BF)
+for _n, _c in (("fp", BF), ("fc", BF), ("ag", BF), ("zp", BF), ("rz", F32)):
+    _buf(_n, 4 * C, _c)
+for _i in range(6):
+    _buf("cmp%d" % _i, 4 * WIDE[_i], BF)
+for _n, _c in (("iotaj", C), ("crow", C), ("jmod", C), ("g8", 512), ("ex", C), ("jt", 48), ("jg", 48), ("ct0", 24), ("qg", 10),
+               ("mask", C), ("fold0", C), ("pick", C), ("mbig", C), ("hs", 4), ("ka", C), ("win", 8 * C), ("u1", 48), ("kf", C),
+               ("ar", 2 * C), ("abf", 2 * C), ("sm", C), ("sf", C), ("smk", C), ("rs", 24), ("half", 4), ("rc", 24), ("cf2", C),
+               ("inv", C), ("wrow", C), ("swap", C), ("crm", C), ("crf", C), ("yb", C)):
+    _buf(_n, _c, F32)
+for _n, _c in (("cfi", 24), ("pcol", 4), ("us32", 32), ("ti", 48)):
+    _buf(_n, _c, "int32")
+for _n, _c in (("uso", 32), ("uho", 8), ("oab", 48), ("at", 48), ("pos", 24), ("lo", 10), ("cl", 24)):
+    _buf(_n, _c, "uint16")
+for _n, _c in (("u", 128), ("us", 128), ("uh", 128), ("v", 128), ("w", 512), ("x", C), ("k", 8 * 128), ("le", C), ("ge", C),
+               ("mk", 2 * C), ("dg", C)):
+    _pair(_n, _c)
+for _i in range(6):
+    _pair("cmp%d" % _i, WIDE[_i])
+for _r in range(ROUNDS):
+    _pair("e%d" % _r, M)
+    _pair("land%d" % _r, M)
+for _b in range(8):
+    _buf("ps%d" % _b, 512, F32, "psum")
+SEMAPHORES = ["vec", "act", "ten", "pool", "sent", "ldx", "ldu", "ldv", "ldw", "lds", "ldc", "sty", "sty2", "stp", "stc",
+              "sts0", "sts1", "sts2", "sts3", "arr0", "arr1", "arr2"]
+
+LE, GE, EQ = AluOpType.is_le, AluOpType.is_ge, AluOpType.is_equal
+ADD, SUB, MUL, MAX, MIN = AluOpType.add, AluOpType.subtract, AluOpType.mult, AluOpType.max, AluOpType.min
+COPY, SIGN = ActivationFunctionType.Copy, ActivationFunctionType.Sign
+ABS, RELU, IDENT = ActivationFunctionType.Abs, ActivationFunctionType.Relu, ActivationFunctionType.Identity
+SHIFT = 2.0 ** 18
+EB0, K512, K3, SG, SGH = 0, 4, 5, 6, 7
+
+
+def rank_program(g, core, T, topo):
+    rank = T.rank_of(core)
+    if rank is None:
+        return
+    queue = {"v": g.vector, "s": g.scalar, "t": g.tensor, "p": g, "y": g.sync}
+    own = {"v": "vec", "s": "act", "t": "ten", "p": "pool"}
+    count = {"vec": 0, "act": 0, "ten": 0, "pool": 0}
+    seen = {q: {} for q in queue}
+    clock, hist = {}, {}
+
+    def waits(q, reads, writes):
+        need = {}
+        for kind, regs in (("r", reads), ("w", writes)):
+            for key, lo, hi in regs:
+                for a, b, k, q2, ev in hist.get(key, []):
+                    if b <= lo or hi <= a:
+                        continue
+                    if kind == "r" and k == "r" and not (key[:2] == "ps" and q2 != q):
+                        continue
+                    if kind == "w" and q2 == q and (k == "r" or q == "t"):
+                        continue
+                    need[ev[0]] = max(need.get(ev[0], 0), ev[1])
+        need = {s: n for s, n in need.items() if seen[q].get(s, 0) < n}
+        for s in sorted(need):
+            if any(o != s and clock[(o, need[o])].get(s, 0) >= need[s] for o in need if need[o]):
+                need[s] = 0
+        for s, n in need.items():
+            if n and seen[q].get(s, 0) < n:
+                queue[q].wait_ge(T.sem[s], n)
+                for s2, n2 in clock[(s, n)].items():
+                    seen[q][s2] = max(seen[q].get(s2, 0), n2)
+
+    def note(q, ev, reads, writes):
+        clock[ev] = dict(seen[q] if q in seen else {})
+        clock[ev][ev[0]] = ev[1]
+        for key, lo, hi in writes:
+            hist[key] = [e for e in hist.get(key, []) if not (lo <= e[0] and e[1] <= hi)] + [(lo, hi, "w", q, ev)]
+        for key, lo, hi in reads:
+            hist[key] = [e for e in hist.get(key, []) if not (e[2] == "r" and e[3] == q and lo <= e[0] and e[1] <= hi)]
+            hist[key].append((lo, hi, "r", q, ev))
+
+    def full(regs):
+        return [(r, 0, 1 << 20) if not isinstance(r, tuple) else r for r in regs]
+
+    def run(q, reads, writes, call):
+        reads, writes = full(reads), full(writes)
+        waits(q, reads, writes)
+        s = own[q]
+        count[s] += 1
+        call().then_inc(T.sem[s], 1)
+        note(q, (s, count[s]), reads, writes)
+
+    def dma(q, sem, reads, writes, out, in_):
+        reads, writes = full(reads), full(writes)
+        waits(q, reads, writes)
+        queue[q].dma_start(out, in_).then_inc(T.sem[sem], 16)
+        saved = dict(seen[q])
+        note("d" + sem, (sem, 16), reads, writes)
+        clock[(sem, 16)].update(saved)
+
+    V, S, P = g.vector, g.scalar, g
+
+    def pl(buf, t):
+        return buf[:, C * t:C * t + C]
+
+    def codes(name, a, b):
+        return T[name + "_q"][:, a:b]
+
+    def plane(name, a, b):
+        return T[name + "_s"][:, a:b]
+
+    def quant(name, src, a=0, b=None, regs=None):
+        b = SCRATCH[name + "_q"][1][1] if b is None else b
+        run("v", [src] if regs is None else regs, [name + "_q"] if regs is None else [(name + "_q", a, b)],
+            lambda: V.quantize_mx(codes(name, a, b), plane(name, a, b), T[src][:, 4 * a:4 * b]))
+
+    def mm(bank, l, la, r, ra, rb, start=True, stop=True):
+        run("t", [(l + "_q", la, la + 128), (r + "_q", ra, rb)] + [l + "_s"] * (l[0] == "u"), ["ps%d" % bank],
+            lambda: g.tensor.matmul_mx(T["ps%d" % bank][:, 0:rb - ra], codes(l, la, la + 128), plane(l, la, la + 128),
+                                       codes(r, ra, rb), plane(r, ra, rb), start, stop))
+
+    def vts(reads, writes, out, in0, s1, s2, *ops):
+        run("v", reads, writes, lambda: V.tensor_scalar(out, in0, s1, s2, *ops))
+
+    def vtt(reads, writes, out, in0, in1, op):
+        run("v", reads, writes, lambda: V.tensor_tensor(out, in0, in1, op))
+
+    def vcp(reads, writes, out, in_):
+        run("v", reads, writes, lambda: V.tensor_copy(out, in_))
+
+    def act(reads, writes, out, in_, func=COPY, **kw):
+        run("s", reads, writes, lambda: S.activation(out, in_, func, **kw))
+
+    def scan(reads, writes, out, d0, d1, op0, op1):
+        run("v", reads, writes, lambda: V.tensor_tensor_scan(out, d0, d1, 0.0, op0, op1))
+
+    def cut(row, regs, dst, n=C):
+        scan(regs + ["pick"], [dst], T[dst][:, 0:n], T.pick[:, 0:n], row, ADD, MAX)
+
+    dma("y", "ldx", [], ["xb"], T.xb[:], T.x[:])
+    dma("s", "ldu", [], ["ub"], T.ub[:], T.u[:])
+    dma("s", "ldc", [], ["cfi"], T.cfi[:], T.cf[:])
+    dma("s", "ldw", [], ["w_q"], T.w_q[:, 0:512].bitcast(dt.uint8), T.wc[:])
+    dma("y", "lds", [], ["w_s"], T.w_s[:], T.ws[:])
+    dma("y", "ldv", [], ["vb"], T.vb[:], T.v[:])
+
+    def iota(name, a, b, pattern, base, cm, **kw):
+        run("p", [], [(name, a, b)], lambda: P.iota(T[name][:, a:b], pattern, base, cm, **kw))
+
+    def fill(name, a, b, value):
+        run("v", [], [(name, a, b)], lambda: V.memset(T[name][:, a:b], value))
+
+    def tile(k):
+        return "cb", 512 * k, 512 * k + 512
+
+    def const(k):
+        return T.cb[:, 512 * k:512 * k + 512]
+
+    ok = {"allow_small_or_imprecise_dtypes": True}
+    iota("us32", 0, 8, [[16, 8]], 0, 0)
+    iota("us32", 8, 32, [[16, 24]], 15, 0)
+    iota("pcol", 0, 1, [[1, 1]], 0, 1)
+    iota("jmod", 0, C, [[0, 24], [1, 16]], 0, 0, **ok)
+    iota("jt", 0, 24, [[16, 24]], 0, 0, **ok)
+    iota("jt", 24, 48, [[16, 24]], 0, 0, **ok)
+    fill("hb", 0, 512, 0.5)
+    for t in range(4):
+        run("p", ["hb"], [tile(EB0 + t)], lambda: P.affine_select(const(EB0 + t), T.hb[:], [[1, 512]], EQ, 0.0, -t, -4))
+    iota("g8", 0, 512, [[1, 8], [0, 64]], 0, 0, **ok)
+    iota("crow", 0, C, [[1, C]], -512, 0, **ok)
+    for i in (4, 3, 1, 0):
+        iota("cmp%d" % i, 256 * i, 4 * WIDE[i], [[0, 4 * WIDE[i] - 256 * i]], 0, 0, **ok)
+    iota("iotaj", 0, C, [[1, C]], 0, 0, **ok)
+
+    fill("uho", 0, 8, 1)
+    fill(*tile(K512), 512.0)
+    fill(*tile(K3), 3.0)
+    vcp(["us32"], ["uso"], T.uso[:], T.us32[:])
+    vts(["pcol"], [("pcol", 1, 2)], T.pcol[:, 1:2], T.pcol[:, 0:1], 15, None, AluOpType.bitwise_and)
+    vts(["pcol"], [("pcol", 2, 3)], T.pcol[:, 2:3], T.pcol[:, 0:1], 4, None, AluOpType.arith_shift_right)
+    fill("ones", 0, C, 1.0)
+    vcp([("pcol", 1, 3)], [("qg", 0, 2)], T.qg[:, 0:2], T.pcol[:, 1:3])
+    fill("half", 0, 4, 0.5)
+    vts([("qg", 0, 2)], [("qg", 4, 6)], T.qg[:, 4:6], T.qg[:, 0:2], -1.0, None, MUL)
+    q_of, g_of = T.qg[:, 0:1], T.qg[:, 1:2]
+    shift_of = T.qg[:, 7:8]
+    act(["jmod"], ["fold0"], T.fold0[:], T.jmod[:], SIGN)
+    act(["jmod", ("qg", 4, 6)], ["mask"], T.mask[:], T.jmod[:], ABS, bias=T.qg[:, 4:5])
+    act(["mask"], ["mask"], T.mask[:], T.mask[:], RELU, bias=1.0, scale=-1.0)
+
+    def blank(name, first):
+        act(["jmod"], [name], T[name][:, first:first + 4 * C - 3:4], T.jmod[:], scale=0.0)
+
+    act([("qg", 0, 2)], [("qg", 8, 9)], T.qg[:, 8:9], q_of, IDENT, bias=-0.5)
+    act(["jmod", ("qg", 8, 9)], ["mbig"], T.mbig[:], T.jmod[:], SIGN, bias=T.qg[:, 8:9], scale=-1.0)
+    act(["mbig"], ["mbig"], T.mbig[:], T.mbig[:], scale=1e29)
+    act([("qg", 0, 2)], [("qg", 6, 7)], T.qg[:, 6:7], q_of, IDENT, bias=1.0)
+    act([("qg", 0, 2)], [("qg", 7, 8)], shift_of, q_of, IDENT, bias=15.0 * SHIFT, scale=-SHIFT)
+    blank("le", 3)
+    blank("ge", 3)
+    for i in (5, 2):
+        fill("cmp%d" % i, 256 * i, 4 * WIDE[i], 0.0)
+    fill("dg", 0, 4 * C, 0.0)
+    quant("u", "ub")
+
+    def repeat(name, off):
+        run("v", ["u_q", off], [name + "_s"], lambda: V.tensor_copy(T[name + "_s"][:, 0:128], T.u_s[:, 0:128].indirect(T[off][:, 0:8])))
+        run("v", ["u_q", off], [name + "_q"],
+            lambda: V.tensor_copy(T[name + "_q"][:, 0:128].bitcast(dt.uint32), T.u_q[:, 0:128].bitcast(dt.uint32).indirect(T[off][:, 0:8])))
+
+    repeat("us", "uso")
+    quant("x", "xb", 0, HALF, ["xb"])
+    quant("x", "xb", HALF, C, ["xb"])
+    repeat("uh", "uho")
+    fill("rs", 0, 1, 0.0)
+
+    def packs():
+        quant("k", "cb", 512, 768, [("cb", 2048, 3072)])
+        quant("k", "cb", 0, 512, [("cb", 0, 2048)])
+        vcp(["cfi"], ["cl"], T.cl[:], T.cfi[:])
+        act(["jmod", ("qg", 6, 7)], ["pick"], T.pick[:], T.jmod[:], RELU, bias=T.qg[:, 6:7], scale=-1.0)
+        act(["pick"], ["pick"], T.pick[:], T.pick[:], IDENT, bias=SHIFT, scale=-256.0 * SHIFT)
+        act(["jmod"], ["foldb"], T.foldb[:], T.jmod[:], SIGN)
+        act(["g8", ("qg", 4, 6)], ["g8"], T.g8[:], T.g8[:], ABS, bias=T.qg[:, 5:6])
+        act(["g8"], [tile(SG)], const(SG), T.g8[:], RELU, bias=1.0, scale=-1.0)
+        act(["g8"], [tile(SGH)], const(SGH), T.g8[:], RELU, bias=0.5, scale=-0.5)
+
+    def tables():
+        lead = 4 * FIRST
+        blank("mk", 4 * C + 3)
+        for t in range(4):
+            act(["jmod"], [("rz%d" % t, 0, C - M)], T.rz[:, C * t:C * t + C - M], T.jmod[:, 0:C - M], scale=0.0)
+        vts(["jt", ("qg", 0, 2)], ["jt"], T.jt[:], T.jt[:], q_of, None, ADD)
+        vts([("qg", 0, 2)], [("qg", 2, 3)], T.qg[:, 2:3], g_of, 384.0, None, MUL)
+        vts([("qg", 0, 2)], [("qg", 3, 4)], T.qg[:, 3:4], g_of, 384.0, 384.0, MUL, ADD)
+        vts(["jt", ("qg", 2, 3)], [("jg", 0, 24)], T.jg[:, 0:24], T.jt[:, 0:24], T.qg[:, 2:3], None, SUB)
+        vts(["jt", ("qg", 3, 4)], [("jg", 24, 48)], T.jg[:, 24:48], T.jt[:, 24:48], T.qg[:, 3:4], None, SUB)
+        vts(["jt"], [("ct0", 0, lead)], T.ct0[:, 0:lead], T.jt[:, 0:lead], -1.0, 383.0 - 8 * (24 - lead), MUL, ADD)
+        vts(["jt", ("qg", 0, 2)], [("ct0", lead, 24)], T.ct0[:, lead:24], T.jt[:, lead:24], 0.0, q_of, MUL, SUB)
+        vts([("ct0", lead, 24)], [("ct0", lead, 24)], T.ct0[:, lead:24], T.ct0[:, lead:24], 199.0, None, ADD)
+        vts(["ct0", ("qg", 7, 8)], ["ct0"], T.ct0[:], T.ct0[:], shift_of, None, ADD)
+        vts(["jg", ("qg", 7, 8)], ["jg"], T.jg[:], T.jg[:], shift_of, None, SUB)
+
+    def products():
+        mm(0, "us", 0, "x", 0, HALF)
+        mm(7, "us", 0, "x", HALF, C)
+        for b in range(3):
+            mm(2 + b, "x", 128 * b, "u", 0, 128)
+        mm(1, "uh", 0, "x", 0, C)
+        mm(5, "us", 0, "x", 0, C)
+        for b in range(3):
+            act(["ps%d" % (2 + b)], [("hs", b, b + 1)], T.hs[:, b:b + 1], T["ps%d" % (2 + b)][:, 1:2])
+        for b in range(3):
+            act(["ps1", ("hs", b, b + 1)], [("sgn", C * b, C * b + C)], pl(T.sgn, b), T.ps1[:, 0:C], SIGN, bias=T.hs[:, b:b + 1], scale=-1.0)
+
+    def planes():
+        for t, bank in enumerate((6, 2, 1, 7)):
+            mm(bank, "k", 128 * (EB0 + t), "x", 0, C)
+        for t, bank in enumerate((6, 2, 1, 7)):
+            act(["ps%d" % bank], ["fp%d" % t], pl(T.fp, t), T["ps%d" % bank][:, 0:C])
+
+    def turning():
+        for name, op, bank in (("le", LE, 3), ("ge", GE, 4)):
+            for b in range(3):
+                vts([("sgn", C * b, C * b + C)], [name + "#%d" % b], T[name][:, b:4 * C:4], pl(T.sgn, b), 0.0, None, op)
+                yield
+            quant(name, name, 0, C, [name + "#%d" % b for b in range(3)] + [name])
+            mm(bank, "k", 128 * K512, name, 0, C)
+            yield
+        vtt(["ps3", "crow"], ["ka"], T.ka[:], T.ps3[:, 0:C], T.crow[:], ADD)
+        yield
+        for m in range(7):
+            even = m % 2 == 0
+            key = T.ka[:] if even else T.win[:, 7 * C:8 * C]
+            last = T.ones[:] if m == 0 else T.mk[:, mark:mark + 4 * (C - 1) + 1:4]
+            scan(["ka" if even else ("win", 7 * C, 8 * C), "ones" if m == 0 else "mk#%d" % (m - 1)], [("win", C * m, C * m + C)],
+                 pl(T.win, m), last, key, MUL, MAX)
+            yield
+            if m == 0:
+                vtt(["ps4", "crow"], [("win", 7 * C, 8 * C)], pl(T.win, 7), T.ps4[:, 0:C], T.crow[:], ADD)
+                yield
+            mark = m if m < 4 else 4 * C + m - 4
+            bank = 3 if even else 4
+            vtt(["ps%d" % bank, ("win", C * m, C * m + C)], ["mk#%d" % m], T.mk[:, mark:mark + 4 * (C - 1) + 1:4],
+                pl(T.win, m), T["ps%d" % bank][:, 0:C], GE)
+            yield
+            if m == 3:
+                quant("mk", "mk", 0, C, ["mk#%d" % i for i in range(4)])
+                mm(6, "k", 128 * K3, "mk", 0, C, True, False)
+                yield
+        quant("mk", "mk", C, 2 * C, ["mk#%d" % i for i in range(4, 7)] + ["mk"])
+        mm(6, "k", 128 * K3, "mk", C, 2 * C, False, True)
+        yield
+        yield
+        cut(T.ps6[:, 0:C], ["ps6"], "kf")
+        yield
+        for i in range(2):
+            a, b = 24 * i, 24 * i + 24
+            vtt(["kf", ("jg", a, b)], [("u1", a, b)], T.u1[:, a:b], T.kf[:, 15:C:16], T.jg[:, a:b], ADD)
+            yield
+        vtt(["u1", "jt"], ["u1"], T.u1[:], T.u1[:], T.jt[:], MAX)
+        yield
+        vcp(["u1"], ["oab"], T.oab[:], T.u1[:])
+        yield
+        for i in range(2):
+            act(["win", "oab"], ["ar#%d" % i], pl(T.ar, i), T.win[:, 0:8 * C].indirect(T.oab[:, 24 * i:24 * i + 24]))
+        yield
+        for i in range(2):
+            a, b, abf = 24 * i, 24 * i + 24, ("abf", C * i, C * i + C)
+            scan(["ar#%d" % i, "pick"], [abf], pl(T.abf, i), T.pick[:], pl(T.ar, i), ADD, MAX)
+            yield
+            vcp([abf], [("ti", a, b)], T.ti[:, a:b], T.abf[:, C * i + 15:C * i + C:16])
+            yield
+            vts([("ti", a, b)], [("ti", a, b)], T.ti[:, a:b], T.ti[:, a:b], 511, None, AluOpType.bitwise_and)
+            yield
+            vcp([("ti", a, b)], [("at", a, b)], T.at[:, a:b], T.ti[:, a:b])
+            if i == 0:
+                for t in range(4):
+                    act(["fc%d" % t, ("at", a, b)], ["ag%d" % t], pl(T.ag, t), pl(T.fc, t).indirect(T.at[:, a:b]))
+            yield
+
+    def orders(r):
+        for dst, by, op in (("sm", "mask", MUL), ("smk", "mbig", MIN)):
+            for a, bank in ((0, "ps0"), (HALF, "ps7")):
+                vtt([bank, by], [(dst, a, a + HALF)], T[dst][:, a:a + HALF], T[bank][:, 0:HALF], T[by][:, a:a + HALF], op)
+            yield
+        scan(["sm", "fold0"], ["sf"], T.sf[:], T.fold0[:], T.sm[:], MUL, ADD)
+        act(["sf", "uso"], ["ex"], T.ex[:], T.sf[:, 0:C].indirect(T.uso[:, 8:32]))
+        yield
+        score = [T.sf[:, 16 * c + 15:16 * c + 16] for c in range(24)]
+        for c in range(23, 4 * FIRST - 2, -1):
+            if c >= 4 * FIRST:
+                a = C * (c % 12)
+                act(["ps5", "sf"], [("sig", a, a + C)], T.sig[:, a:a + 16 * c], T.ps5[:, 0:16 * c], SIGN, bias=score[c], scale=-1.0)
+            if c < 23:
+                d = c + 1
+                i, t, a = d // 4, d % 4, C * (d % 12)
+                name = "cmp%d" % i
+                act([("sig", a, a + C), "half", name], [name + "#%d" % t, ("rs", d, d + 1)], T[name][:, t:64 * (d - 1) + 60 + t + 1:4],
+                    T.sig[:, a:a + 16 * d], SIGN, bias=T.half[:, 0:1], scale=-1.0, accum_out=T.rs[:, d:d + 1])
+                if d == 20:
+                    yield
+
+        def counts(name, half, cols, first=False, last=False):
+            mm(2, "k", 128 * (SGH if half else SG), name, 0, cols, first, last)
+
+        def pack(i):
+            name = "cmp%d" % i
+            quant(name, name, 0, WIDE[i], [name + "#%d" % t for t in range(4)] + [name])
+            counts(name, i >= FIRST, WIDE[i], i == 5, i == FIRST)
+
+        for i in range(FIRST - 1, -1, -1):
+            name = "cmp%d" % i
+            for t in range(3, -1, -1):
+                c = 4 * i + t
+                if c:
+                    part, end = name + "#%d" % t, 64 * (c - 1) + 60 + t + 1
+                    vts(["ps0", "sf", name], [part], T[name][:, t:end:4], T.ps0[:, 0:16 * c], score[c], None, GE)
+                    act([part], [("junk", C * t, C * t + C), ("rs", c, c + 1)], T.junk[:, C * t:C * t + 16 * c], T[name][:, t:end:4],
+                        accum_out=T.rs[:, c:c + 1])
+                    yield
+            if i == FIRST - 1:
+                vtt(["smk", "ex", "dg"], ["dg#0"], T.dg[:, 0:4 * C - 3:4], T.smk[:], T.ex[:], GE)
+                yield
+        if r == 0:
+            quant("k", "cb", 768, 1024, [("cb", 3072, 4096)])
+            yield
+        pack(5)
+        yield
+        quant("dg", "dg", 0, C, ["dg#0", "dg"])
+        counts("dg", False, C)
+        yield
+        scan(["dg#0", "foldb"], ["dr"], T.dr[:], T.foldb[:], T.dg[:, 0:4 * C - 3:4], MUL, ADD)
+        yield
+        vtt(["ct0", "dr"], ["rc"], T.rc[:], T.ct0[:], T.dr[:, 15:C:16], ADD)
+        yield
+        for i in range(FIRST - 1, -1, -1):
+            pack(i)
+            yield
+        for t in range(4):
+            act(["fp%d" % t, "cl"], ["fc%d" % t], pl(T.fc, t), pl(T.fp, t).indirect(T.cl[:, 0:24]))
+        for i in range(4, FIRST - 1, -1):
+            pack(i)
+            yield
+        vts([("rs", 4 * FIRST, 24)], [("rs", 4 * FIRST, 24)], T.rs[:, 4 * FIRST:24], T.rs[:, 4 * FIRST:24], 0.5, None, MUL)
+        yield
+        vtt(["rs", "rc"], ["rc"], T.rc[:], T.rs[:], T.rc[:], ADD)
+        yield
+        cut(T.ps2[:, 0:C], ["ps2"], "cf2")
+        yield
+        vtt(["rc", "cf2"], ["rc"], T.rc[:], T.rc[:], T.cf2[:, 15:C:16], SUB)
+        yield
+        vcp(["rc"], ["pos"], T.pos[:], T.rc[:])
+        yield
+        vcp(["iotaj", "pos"], ["inv"], T.inv[:, 0:C].indirect(T.pos[:, 0:24]), T.iotaj[:])
+        yield
+        cut(T.inv[:, 0:M], ["inv"], "cf2", M)
+        yield
+        vts(["cf2", ("qg", 7, 8)], ["lo"], T.lo[:], T.cf2[:, 15:M:16], shift_of, None, SUB)
+        yield
+
+    nxt = T.cores[(rank + 1) % len(T.cores)]
+    rid, pid = topo.addr(nxt)[:2]
+    engines = len(topo.engines(core, nxt))
+
+    for r in range(ROUNDS):
+        products()
+        chains = [[orders(r), 40, 0], [turning(), 48, 0]]
+        for _ in range(4):
+            next(chains[0][0])
+        if r == 0:
+            packs()
+        planes()
+        if r == 0:
+            tables()
+        while chains:
+            c = min(chains, key=lambda e: e[2] / e[1])
+            c[2] += 1
+            if next(c[0], 0) == 0:
+                chains.remove(c)
+        for t in range(4):
+            vtt(["fc%d" % t, ("at", 24, 48), "ag%d" % t], ["zp%d" % t], pl(T.zp, t), pl(T.fc, t).indirect(T.at[:, 24:48]), pl(T.ag, t), ADD)
+        for t in range(4):
+            out, in_ = T.eb[:, t:4 * M:4], pl(T.zp, t).indirect(T.lo[:, 0:10])
+            if t < 3:
+                act(["zp%d" % t, "lo"], ["eb#%d" % t], out, in_)
+            else:
+                vcp(["zp%d" % t, "lo"], ["eb#%d" % t], out, in_)
+        name, land, arr = "e%d" % r, "land%d" % r, "arr%d" % r
+        quant(name, "eb", 0, M, ["eb#%d" % t for t in range(4)])
+        waits("p", full([name + "_q"]), [])
+        g.remote_dma(T[land + "_q"][:, 0:M].bitcast(dt.uint8), T[name + "_q"][:, 0:M].bitcast(dt.uint8), T.sem[arr], T.sem.sent, pid, rid,
+                     topo.mask(core, nxt))
+        g.remote_dma(T[land + "_s"][:, 0:M], T[name + "_s"][:, 0:M], T.sem[arr], T.sem.sent, pid, rid, topo.mask(core, nxt))
+        note("d" + arr, (arr, 2 * engines), [], full([land + "_q"]))
+        for a, b, c in ((0, 224, 384), (160, 160, 224), (224, 0, 160)):
+            act(["inv"], [("wrow", a, a + c - b)], T.wrow[:, a:a + c - b], T.inv[:, b:c])
+        vcp(["wrow", "pos"], ["swap"], T.swap[:], T.wrow[:, 0:C].indirect(T.pos[:, 0:24]))
+        act(["swap", "cl"], ["crm"], T.crm[:], T.swap[:, 0:C].indirect(T.cl[:, 0:24]))
+        if r + 1 < ROUNDS:
+            cut(T.crm[:], ["crm"], "crf")
+            vts(["crf", ("qg", 7, 8)], ["cl"], T.cl[:], T.crf[:, 15:C:16], shift_of, None, SUB)
+        else:
+            dma("y", "stp", ["crm"], [], T.op[:], T.crm[0:128:16, :])
+        if r == 0:
+            quant("v", "vb")
+        banks = (1, 2, 6, 7)
+        for b in range(4):
+            run("t", ["w_q", "w_s", land + "_q"], ["ps%d" % banks[b]],
+                lambda: g.tensor.matmul_mx(T["ps%d" % banks[b]][:, 0:M], codes("w", 128 * b, 128 * b + 128), plane("w", 128 * b, 128 * b + 128),
+                                           codes(land, 0, M), plane(land, 0, M), True, True))
+        for b in range(4):
+            out, in_ = T.rz[:, C * b + C - M:C * b + C], T["ps%d" % banks[b]][:, 0:M]
+            if b == 0:
+                vts(["ps%d" % banks[b]], [("rz%d" % b, C - M, C)], out, in_, 0.03125, None, MUL)
+            else:
+                act(["ps%d" % banks[b]], [("rz%d" % b, C - M, C)], out, in_, scale=0.03125)
+        for b in range(4):
+            vtt(["rz%d" % b, "pos", "zp%d" % b], ["xb#%d" % b], T.xb[:, b:4 * C:4], pl(T.rz, b).indirect(T.pos[:, 0:24]), pl(T.zp, b), ADD)
+        for a in (0, HALF):
+            quant("x", "xb", a, a + HALF, ["xb#%d" % b for b in range(4)])
+
+    mm(0, "v", 0, "x", 0, HALF)
+    mm(5, "v", 0, "x", HALF, C)
+    dma("y", "stc", ["x_q"], [], T.oc[:], T.x_q[:, 0:C].bitcast(dt.uint8))
+    for k in range(4):
+        dma("y", "sts%d" % k, ["x_q"], [], T.osc[4 * k:4 * k + 4, :], T.x_s[32 * k:32 * k + 4, 0:C])
+    act(["ps0"], [("yb", 0, HALF)], T.yb[:, 0:HALF], T.ps0[:, 0:HALF])
+    dma("s", "sty", [("yb", 0, HALF)], [], T.y[:, 0:HALF], T.yb[:, 0:HALF])
+    vcp(["ps5"], [("yb", HALF, C)], T.yb[:, HALF:C], T.ps5[:, 0:HALF])
+    dma("s", "sty2", [("yb", HALF, C)], [], T.y[:, HALF:C], T.yb[:, HALF:C])
+    for s in ("vec", "act", "ten", "pool"):
+        g.wait_ge(T.sem[s], count[s])
+    for s in ("ldx", "ldu", "ldv", "ldw", "lds", "ldc", "sty", "sty2", "stp", "stc", "sts0", "sts1", "sts2", "sts3"):
+        g.wait_ge(T.sem[s], 16)
+    g.wait_ge(T.sem.sent, 2 * engines * ROUNDS)

@@ -1,8 +1,7 @@
 from concourse.mybir import dt, AluOpType, ActivationFunctionType
 
 C, M, ROUNDS = 384, 160, 3
-HALF = C // 2
-FIRST = 3
+HALF, REST = C // 2, C - M
 WIDE = [max(128, 64 * (i + 1)) for i in range(6)]
 X4 = "float8_e4m3fn_x4"
 F32, BF = "float32", "bfloat16"
@@ -18,25 +17,22 @@ def _pair(name, cols):
     _buf(name + "_s", cols, "uint8")
 
 
-for _n, _c in (("xb", 4 * C), ("ub", 512), ("vb", 512), ("cb", 8 * 512), ("sig", 12 * C), ("hb", 512), ("dg", 4 * C), ("dr", C),
-               ("sgn", 3 * C), ("le", 4 * C), ("ge", 4 * C), ("mk", 8 * C), ("junk", 4 * C), ("eb", 4 * M), ("ones", C),
-               ("foldb", C)):
+for _n, _c in (("xb", 4 * C), ("ub", 512), ("vb", 512), ("cb", 8 * 512), ("sig", 12 * C), ("c16", 512), ("ones", 512), ("dr", C),
+               ("t1", 4 * C), ("t2", 4 * C), ("su", C), ("mk", 8 * C), ("junk", 4 * C), ("eb", 4 * M), ("foldb", C),
+               ("fp", 4 * C), ("ag", 4 * C), ("zs", 4 * C)):
     _buf(_n, _c, BF)
-for _n, _c in (("fp", BF), ("fc", BF), ("ag", BF), ("zp", BF), ("rz", F32)):
-    _buf(_n, 4 * C, _c)
 for _i in range(6):
     _buf("cmp%d" % _i, 4 * WIDE[_i], BF)
-for _n, _c in (("iotaj", C), ("crow", C), ("jmod", C), ("g8", 512), ("ex", C), ("jt", 48), ("jg", 48), ("ct0", 24), ("qg", 10),
-               ("mask", C), ("fold0", C), ("pick", C), ("mbig", C), ("hs", 4), ("ka", C), ("win", 8 * C), ("u1", 48), ("kf", C),
-               ("ar", 2 * C), ("abf", 2 * C), ("sm", C), ("sf", C), ("smk", C), ("rs", 24), ("half", 4), ("rc", 24), ("cf2", C),
-               ("inv", C), ("wrow", C), ("swap", C), ("crm", C), ("crf", C), ("yb", C)):
+for _n, _c in (("iotaj", C), ("crow", C), ("jmod", 2 * REST), ("jt", 48), ("jg", 48), ("ct0", 24), ("qg", 10), ("mask", 2 * REST),
+               ("fold", C), ("pick", 2 * REST), ("mb", C), ("hs", 4), ("ka", C), ("win", 8 * C), ("u1", 48), ("kf", C), ("ar", 2 * C),
+               ("ab", 2 * C), ("abf", 2 * C), ("sm", C), ("sf", C), ("rs", 24), ("rc", 24), ("cf2", C), ("inv", C), ("itf", C),
+               ("wrow", C), ("swap", C), ("crf", C), ("yb", C)):
     _buf(_n, _c, F32)
-for _n, _c in (("cfi", 24), ("pcol", 4), ("us32", 32), ("ti", 48)):
+for _n, _c in (("cfi", 24), ("pcol", 4), ("us32", 8), ("ti", 48)):
     _buf(_n, _c, "int32")
-for _n, _c in (("uso", 32), ("uho", 8), ("oab", 48), ("at", 48), ("pos", 24), ("lo", 10), ("cl", 24)):
+for _n, _c in (("uso", 16), ("oab", 48), ("at", 48), ("pos", 24), ("it", 24), ("cl", 24)):
     _buf(_n, _c, "uint16")
-for _n, _c in (("u", 128), ("us", 128), ("uh", 128), ("v", 128), ("w", 512), ("x", C), ("k", 8 * 128), ("le", C), ("ge", C),
-               ("mk", 2 * C), ("dg", C)):
+for _n, _c in (("u", 128), ("uu", 256), ("v", 128), ("w", 512), ("x", C), ("k", 8 * 128), ("t1", C), ("t2", C), ("mk", 2 * C)):
     _pair(_n, _c)
 for _i in range(6):
     _pair("cmp%d" % _i, WIDE[_i])
@@ -45,450 +41,404 @@ for _r in range(ROUNDS):
     _pair("land%d" % _r, M)
 for _b in range(8):
     _buf("ps%d" % _b, 512, F32, "psum")
-SEMAPHORES = ["vec", "act", "ten", "pool", "sent", "ldx", "ldu", "ldv", "ldw", "lds", "ldc", "sty", "sty2", "stp", "stc",
-              "sts0", "sts1", "sts2", "sts3", "arr0", "arr1", "arr2"]
+MOVES = ["ldx0", "ldu", "ldx1", "ldc", "ldw", "lds", "ldv", "stp", "stc0", "stc1", "sts0", "sts1", "sts2", "sts3", "sty0", "sty1"]
+SEMAPHORES = ["vec", "act", "ten", "pool", "sent", "arr0", "arr1", "arr2"] + MOVES
 
-LE, GE, EQ = AluOpType.is_le, AluOpType.is_ge, AluOpType.is_equal
+LT, GE, EQ, NE = AluOpType.is_lt, AluOpType.is_ge, AluOpType.is_equal, AluOpType.not_equal
 ADD, SUB, MUL, MAX, MIN = AluOpType.add, AluOpType.subtract, AluOpType.mult, AluOpType.max, AluOpType.min
 COPY, SIGN = ActivationFunctionType.Copy, ActivationFunctionType.Sign
 ABS, RELU, IDENT = ActivationFunctionType.Abs, ActivationFunctionType.Relu, ActivationFunctionType.Identity
 SHIFT = 2.0 ** 18
-EB0, K512, K3, SG, SGH = 0, 4, 5, 6, 7
+BIG = 1e29
+KP, KN, K3, SG, EB0 = 0, 1, 2, 3, 4
+BY_VECTOR = 0
+WAIT, LOCAL, BYTE, REMOTE, GATHER, SCATTER = 120, 1600, 0.5, 3600, 1.6, 3.8
+PASSES, SLACK, LOOK = 4, 100, 150
 
 
 def rank_program(g, core, T, topo):
     rank = T.rank_of(core)
     if rank is None:
         return
-    queue = {"v": g.vector, "s": g.scalar, "t": g.tensor, "p": g, "y": g.sync}
-    own = {"v": "vec", "s": "act", "t": "ten", "p": "pool"}
-    count = {"vec": 0, "act": 0, "ten": 0, "pool": 0}
-    seen = {q: {} for q in queue}
-    clock, hist = {}, {}
-
-    def waits(q, reads, writes):
-        need = {}
-        for kind, regs in (("r", reads), ("w", writes)):
-            for key, lo, hi in regs:
-                for a, b, k, q2, ev in hist.get(key, []):
-                    if b <= lo or hi <= a:
-                        continue
-                    if kind == "r" and k == "r" and not (key[:2] == "ps" and q2 != q):
-                        continue
-                    if kind == "w" and q2 == q and (k == "r" or q == "t"):
-                        continue
-                    need[ev[0]] = max(need.get(ev[0], 0), ev[1])
-        need = {s: n for s, n in need.items() if seen[q].get(s, 0) < n}
-        for s in sorted(need):
-            if any(o != s and clock[(o, need[o])].get(s, 0) >= need[s] for o in need if need[o]):
-                need[s] = 0
-        for s, n in need.items():
-            if n and seen[q].get(s, 0) < n:
-                queue[q].wait_ge(T.sem[s], n)
-                for s2, n2 in clock[(s, n)].items():
-                    seen[q][s2] = max(seen[q].get(s2, 0), n2)
-
-    def note(q, ev, reads, writes):
-        clock[ev] = dict(seen[q] if q in seen else {})
-        clock[ev][ev[0]] = ev[1]
-        for key, lo, hi in writes:
-            hist[key] = [e for e in hist.get(key, []) if not (lo <= e[0] and e[1] <= hi)] + [(lo, hi, "w", q, ev)]
-        for key, lo, hi in reads:
-            hist[key] = [e for e in hist.get(key, []) if not (e[2] == "r" and e[3] == q and lo <= e[0] and e[1] <= hi)]
-            hist[key].append((lo, hi, "r", q, ev))
-
-    def full(regs):
-        return [(r, 0, 1 << 20) if not isinstance(r, tuple) else r for r in regs]
-
-    def run(q, reads, writes, call):
-        reads, writes = full(reads), full(writes)
-        waits(q, reads, writes)
-        s = own[q]
-        count[s] += 1
-        call().then_inc(T.sem[s], 1)
-        note(q, (s, count[s]), reads, writes)
-
-    def dma(q, sem, reads, writes, out, in_):
-        reads, writes = full(reads), full(writes)
-        waits(q, reads, writes)
-        queue[q].dma_start(out, in_).then_inc(T.sem[sem], 16)
-        saved = dict(seen[q])
-        note("d" + sem, (sem, 16), reads, writes)
-        clock[(sem, 16)].update(saved)
-
     V, S, P = g.vector, g.scalar, g
+    queue = {"v": V, "s": S, "t": g.tensor, "p": g, "y": g.sync}
+    own = {"v": "vec", "s": "act", "t": "ten", "p": "pool"}
+    calls = []
 
-    def pl(buf, t):
-        return buf[:, C * t:C * t + C]
+    def at(name, a=0, b=None, step=1):
+        b = SCRATCH[name][1][1] if b is None else b
+        return T[name][:, a:b:step] if step > 1 else T[name][:, a:b], len(range(a, b, step)), SCRATCH[name][2], [(name, a, b)], False
 
-    def codes(name, a, b):
-        return T[name + "_q"][:, a:b]
+    def slot(name, t, a=0, b=C):
+        return T[name][:, 4 * a + t:4 * (b - 1) + t + 1:4], b - a, BF, [(name + "#%d" % t, a, b)], False
 
-    def plane(name, a, b):
-        return T[name + "_s"][:, a:b]
+    def tile(name, a, b):
+        return T[name][:, 4 * a:4 * b], 4 * (b - a), BF, [(name + "#%d" % t, a, b) for t in range(4)], False
 
-    def quant(name, src, a=0, b=None, regs=None):
-        b = SCRATCH[name + "_q"][1][1] if b is None else b
-        run("v", [src] if regs is None else regs, [name + "_q"] if regs is None else [(name + "_q", a, b)],
-            lambda: V.quantize_mx(codes(name, a, b), plane(name, a, b), T[src][:, 4 * a:4 * b]))
+    def pl(name, t, a=0, b=C):
+        return at(name, C * t + a, C * t + b)
+
+    def by(win, off):
+        return win[0].indirect(off[0]), 16 * off[1], win[2], win[3] + off[3], True
+
+    def ps(bank, a=0, b=C):
+        return T["ps%d" % bank][:, a:b], b - a, "psum", [("ps%d" % bank, 0, 512)], False
+
+    def table(name, a=0, b=C):
+        return at(name, a + 15, b, 16)
+
+    def ap(x):
+        return x[0] if isinstance(x, tuple) else x
+
+    def regions(*xs):
+        return [r for x in xs if isinstance(x, tuple) for r in x[3]]
+
+    def add(q, reads, writes, call, cycles, late=0, sem=None, n=1):
+        calls.append((q, reads, writes, call, cycles, cycles + late, sem, n))
+
+    def cycles(out, in0, rate):
+        if out[4]:
+            return 60 + SCATTER * out[1]
+        if in0[4]:
+            return 70 + max(rate, GATHER) * in0[1]
+        return max(64, rate * in0[1])
+
+    def fast(*xs):
+        return 0.5 if all(x[2] in (BF, "uint16") for x in xs) else 1
+
+    def scattered(out):
+        return (out[3][1:], out[3][:1]) if out[4] else ([], out[3])
+
+    def vts(out, in0, s1, s2, *ops):
+        add("v", regions(in0, s1, s2), out[3], lambda: V.tensor_scalar(out[0], in0[0], ap(s1), ap(s2), *ops), cycles(out, in0, fast(out, in0)))
+
+    def vtt(out, in0, in1, op):
+        add("v", regions(in0, in1), out[3], lambda: V.tensor_tensor(out[0], in0[0], in1[0], op),
+            cycles(out, in0, 1 if "psum" in (in0[2], in1[2]) else 2))
+
+    def vcp(out, in_):
+        lists, window = scattered(out)
+        add("v", in_[3] + lists, window, lambda: V.tensor_copy(out[0], in_[0]), cycles(out, in_, fast(out, in_)))
+
+    def act(out, in_, func=COPY, **kw):
+        sums = regions(kw.get("accum_out"))
+        add("s", regions(in_, kw.get("bias")), out[3] + sums, lambda: S.activation(out[0], in_[0], func, **{k: ap(x) for k, x in kw.items()}),
+            cycles(out, in_, 1) + 24 * len(sums))
+
+    def scan(out, d0, d1, op0, op1):
+        add("v", regions(d0, d1), out[3], lambda: V.tensor_tensor_scan(out[0], d0[0], d1[0], 0.0, op0, op1), cycles(out, d0, fast(out, d0, d1)))
+
+    def fill(out, value):
+        add("v", [], out[3], lambda: V.memset(out[0], value), cycles(out, out, fast(out)))
+
+    def iota(out, pattern, base, cm):
+        kw = {"allow_small_or_imprecise_dtypes": True} if out[2] == F32 else {}
+        add("p", [], out[3], lambda: P.iota(out[0], pattern, base, cm, **kw), 160 + 2 * out[1])
+
+    def select(out, in_, *how):
+        add("p", in_[3], out[3], lambda: P.affine_select(out[0], in_[0], *how), 200 + 2 * out[1])
+
+    def quant(name, src, a, b):
+        add("v", tile(src, a, b)[3], [(name + "_q", a, b), (name + "_s", a, b)],
+            lambda: V.quantize_mx(T[name + "_q"][:, a:b], T[name + "_s"][:, a:b], tile(src, a, b)[0]), 15 + 1.06 * (b - a))
 
     def mm(bank, l, la, r, ra, rb, start=True, stop=True):
-        run("t", [(l + "_q", la, la + 128), (r + "_q", ra, rb)] + [l + "_s"] * (l[0] == "u"), ["ps%d" % bank],
-            lambda: g.tensor.matmul_mx(T["ps%d" % bank][:, 0:rb - ra], codes(l, la, la + 128), plane(l, la, la + 128),
-                                       codes(r, ra, rb), plane(r, ra, rb), start, stop))
+        reads = [(l + "_q", la, la + 128), (l + "_s", la, la + 128), (r + "_q", ra, rb), (r + "_s", ra, rb)]
+        add("t", reads, ps(bank)[3],
+            lambda: g.tensor.matmul_mx(ps(bank, 0, rb - ra)[0], T[l + "_q"][:, la:la + 128], T[l + "_s"][:, la:la + 128],
+                                       T[r + "_q"][:, ra:rb], T[r + "_s"][:, ra:rb], start, stop), rb - ra + 16)
 
-    def vts(reads, writes, out, in0, s1, s2, *ops):
-        run("v", reads, writes, lambda: V.tensor_scalar(out, in0, s1, s2, *ops))
+    def dma(q, sem, reads, writes, out, in_, ahead=0):
+        add(q, reads, writes, lambda: queue[q].dma_start(out, in_), 60, LOCAL + ahead * BYTE, sem, 16)
 
-    def vtt(reads, writes, out, in0, in1, op):
-        run("v", reads, writes, lambda: V.tensor_tensor(out, in0, in1, op))
-
-    def vcp(reads, writes, out, in_):
-        run("v", reads, writes, lambda: V.tensor_copy(out, in_))
-
-    def act(reads, writes, out, in_, func=COPY, **kw):
-        run("s", reads, writes, lambda: S.activation(out, in_, func, **kw))
-
-    def scan(reads, writes, out, d0, d1, op0, op1):
-        run("v", reads, writes, lambda: V.tensor_tensor_scan(out, d0, d1, 0.0, op0, op1))
-
-    def cut(row, regs, dst, n=C):
-        scan(regs + ["pick"], [dst], T[dst][:, 0:n], T.pick[:, 0:n], row, ADD, MAX)
-
-    dma("y", "ldx", [], ["xb"], T.xb[:], T.x[:])
-    dma("s", "ldu", [], ["ub"], T.ub[:], T.u[:])
-    dma("s", "ldc", [], ["cfi"], T.cfi[:], T.cf[:])
-    dma("s", "ldw", [], ["w_q"], T.w_q[:, 0:512].bitcast(dt.uint8), T.wc[:])
-    dma("y", "lds", [], ["w_s"], T.w_s[:], T.ws[:])
-    dma("y", "ldv", [], ["vb"], T.vb[:], T.v[:])
-
-    def iota(name, a, b, pattern, base, cm, **kw):
-        run("p", [], [(name, a, b)], lambda: P.iota(T[name][:, a:b], pattern, base, cm, **kw))
-
-    def fill(name, a, b, value):
-        run("v", [], [(name, a, b)], lambda: V.memset(T[name][:, a:b], value))
-
-    def tile(k):
-        return "cb", 512 * k, 512 * k + 512
+    def cut(dst, a, b, row):
+        scan(at(dst, a, b), at("pick", 0, b - a), row, ADD, MAX)
 
     def const(k):
-        return T.cb[:, 512 * k:512 * k + 512]
+        return tile("cb", 128 * k, 128 * k + 128)
 
-    ok = {"allow_small_or_imprecise_dtypes": True}
-    iota("us32", 0, 8, [[16, 8]], 0, 0)
-    iota("us32", 8, 32, [[16, 24]], 15, 0)
-    iota("pcol", 0, 1, [[1, 1]], 0, 1)
-    iota("jmod", 0, C, [[0, 24], [1, 16]], 0, 0, **ok)
-    iota("jt", 0, 24, [[16, 24]], 0, 0, **ok)
-    iota("jt", 24, 48, [[16, 24]], 0, 0, **ok)
-    fill("hb", 0, 512, 0.5)
+    dma("s", "ldu", [], tile("ub", 0, 128)[3], T.ub[:], T.u[:], 1024)
+    dma("y", "ldx0", [], tile("xb", 0, HALF)[3], T.xb[:, 0:2 * C], T.x[:, 0:2 * C], 2560)
+    dma("y", "ldx1", [], tile("xb", HALF, C)[3], T.xb[:, 2 * C:4 * C], T.x[:, 2 * C:4 * C], 4096)
+    dma("y", "ldc", [], at("cfi")[3], T.cfi[:], T.cf[:], 4192)
+    later = tile("xb", HALF, C)[3]
+    dma("y", "ldw", later, at("w_q")[3], T.w_q[:, 0:512].bitcast(dt.uint8), T.wc[:], 2048)
+    dma("y", "lds", later, at("w_s")[3], T.w_s[:], T.ws[:], 2560)
+    dma("y", "ldv", later, tile("vb", 0, 128)[3], T.vb[:], T.v[:], 3584)
+
+    iota(at("pcol", 0, 1), [[1, 1]], 0, 1)
+    iota(at("us32"), [[16, 8]], 0, 0)
+    iota(at("jmod"), [[0, 2 * REST // 16], [1, 16]], 0, 0)
+    iota(at("jt"), [[0, 2], [16, 24]], 0, 0)
+    iota(at("iotaj"), [[1, C]], 0, 0)
+    fill(at("ones"), 1.0)
+    fill(at("c16"), 16.0)
+    select(const(SG), at("ones"), [[-16, 8], [0, 64]], GE, 0.0, 0, 1)
+    select(const(SG), const(SG), [[16, 8], [0, 64]], GE, 0.0, 15, -1)
     for t in range(4):
-        run("p", ["hb"], [tile(EB0 + t)], lambda: P.affine_select(const(EB0 + t), T.hb[:], [[1, 512]], EQ, 0.0, -t, -4))
-    iota("g8", 0, 512, [[1, 8], [0, 64]], 0, 0, **ok)
-    iota("crow", 0, C, [[1, C]], -512, 0, **ok)
-    for i in (4, 3, 1, 0):
-        iota("cmp%d" % i, 256 * i, 4 * WIDE[i], [[0, 4 * WIDE[i] - 256 * i]], 0, 0, **ok)
-    iota("iotaj", 0, C, [[1, C]], 0, 0, **ok)
-
-    fill("uho", 0, 8, 1)
-    fill(*tile(K512), 512.0)
-    fill(*tile(K3), 3.0)
-    vcp(["us32"], ["uso"], T.uso[:], T.us32[:])
-    vts(["pcol"], [("pcol", 1, 2)], T.pcol[:, 1:2], T.pcol[:, 0:1], 15, None, AluOpType.bitwise_and)
-    vts(["pcol"], [("pcol", 2, 3)], T.pcol[:, 2:3], T.pcol[:, 0:1], 4, None, AluOpType.arith_shift_right)
-    fill("ones", 0, C, 1.0)
-    vcp([("pcol", 1, 3)], [("qg", 0, 2)], T.qg[:, 0:2], T.pcol[:, 1:3])
-    fill("half", 0, 4, 0.5)
-    vts([("qg", 0, 2)], [("qg", 4, 6)], T.qg[:, 4:6], T.qg[:, 0:2], -1.0, None, MUL)
-    q_of, g_of = T.qg[:, 0:1], T.qg[:, 1:2]
-    shift_of = T.qg[:, 7:8]
-    act(["jmod"], ["fold0"], T.fold0[:], T.jmod[:], SIGN)
-    act(["jmod", ("qg", 4, 6)], ["mask"], T.mask[:], T.jmod[:], ABS, bias=T.qg[:, 4:5])
-    act(["mask"], ["mask"], T.mask[:], T.mask[:], RELU, bias=1.0, scale=-1.0)
-
-    def blank(name, first):
-        act(["jmod"], [name], T[name][:, first:first + 4 * C - 3:4], T.jmod[:], scale=0.0)
-
-    act([("qg", 0, 2)], [("qg", 8, 9)], T.qg[:, 8:9], q_of, IDENT, bias=-0.5)
-    act(["jmod", ("qg", 8, 9)], ["mbig"], T.mbig[:], T.jmod[:], SIGN, bias=T.qg[:, 8:9], scale=-1.0)
-    act(["mbig"], ["mbig"], T.mbig[:], T.mbig[:], scale=1e29)
-    act([("qg", 0, 2)], [("qg", 6, 7)], T.qg[:, 6:7], q_of, IDENT, bias=1.0)
-    act([("qg", 0, 2)], [("qg", 7, 8)], shift_of, q_of, IDENT, bias=15.0 * SHIFT, scale=-SHIFT)
-    blank("le", 3)
-    blank("ge", 3)
-    for i in (5, 2):
-        fill("cmp%d" % i, 256 * i, 4 * WIDE[i], 0.0)
-    fill("dg", 0, 4 * C, 0.0)
-    quant("u", "ub")
-
-    def repeat(name, off):
-        run("v", ["u_q", off], [name + "_s"], lambda: V.tensor_copy(T[name + "_s"][:, 0:128], T.u_s[:, 0:128].indirect(T[off][:, 0:8])))
-        run("v", ["u_q", off], [name + "_q"],
-            lambda: V.tensor_copy(T[name + "_q"][:, 0:128].bitcast(dt.uint32), T.u_q[:, 0:128].bitcast(dt.uint32).indirect(T[off][:, 0:8])))
-
-    repeat("us", "uso")
-    quant("x", "xb", 0, HALF, ["xb"])
-    quant("x", "xb", HALF, C, ["xb"])
-    repeat("uh", "uho")
-    fill("rs", 0, 1, 0.0)
-
-    def packs():
-        quant("k", "cb", 512, 768, [("cb", 2048, 3072)])
-        quant("k", "cb", 0, 512, [("cb", 0, 2048)])
-        vcp(["cfi"], ["cl"], T.cl[:], T.cfi[:])
-        act(["jmod", ("qg", 6, 7)], ["pick"], T.pick[:], T.jmod[:], RELU, bias=T.qg[:, 6:7], scale=-1.0)
-        act(["pick"], ["pick"], T.pick[:], T.pick[:], IDENT, bias=SHIFT, scale=-256.0 * SHIFT)
-        act(["jmod"], ["foldb"], T.foldb[:], T.jmod[:], SIGN)
-        act(["g8", ("qg", 4, 6)], ["g8"], T.g8[:], T.g8[:], ABS, bias=T.qg[:, 5:6])
-        act(["g8"], [tile(SG)], const(SG), T.g8[:], RELU, bias=1.0, scale=-1.0)
-        act(["g8"], [tile(SGH)], const(SGH), T.g8[:], RELU, bias=0.5, scale=-0.5)
-
-    def tables():
-        lead = 4 * FIRST
-        blank("mk", 4 * C + 3)
-        for t in range(4):
-            act(["jmod"], [("rz%d" % t, 0, C - M)], T.rz[:, C * t:C * t + C - M], T.jmod[:, 0:C - M], scale=0.0)
-        vts(["jt", ("qg", 0, 2)], ["jt"], T.jt[:], T.jt[:], q_of, None, ADD)
-        vts([("qg", 0, 2)], [("qg", 2, 3)], T.qg[:, 2:3], g_of, 384.0, None, MUL)
-        vts([("qg", 0, 2)], [("qg", 3, 4)], T.qg[:, 3:4], g_of, 384.0, 384.0, MUL, ADD)
-        vts(["jt", ("qg", 2, 3)], [("jg", 0, 24)], T.jg[:, 0:24], T.jt[:, 0:24], T.qg[:, 2:3], None, SUB)
-        vts(["jt", ("qg", 3, 4)], [("jg", 24, 48)], T.jg[:, 24:48], T.jt[:, 24:48], T.qg[:, 3:4], None, SUB)
-        vts(["jt"], [("ct0", 0, lead)], T.ct0[:, 0:lead], T.jt[:, 0:lead], -1.0, 383.0 - 8 * (24 - lead), MUL, ADD)
-        vts(["jt", ("qg", 0, 2)], [("ct0", lead, 24)], T.ct0[:, lead:24], T.jt[:, lead:24], 0.0, q_of, MUL, SUB)
-        vts([("ct0", lead, 24)], [("ct0", lead, 24)], T.ct0[:, lead:24], T.ct0[:, lead:24], 199.0, None, ADD)
-        vts(["ct0", ("qg", 7, 8)], ["ct0"], T.ct0[:], T.ct0[:], shift_of, None, ADD)
-        vts(["jg", ("qg", 7, 8)], ["jg"], T.jg[:], T.jg[:], shift_of, None, SUB)
-
-    def products():
-        mm(0, "us", 0, "x", 0, HALF)
-        mm(7, "us", 0, "x", HALF, C)
-        for b in range(3):
-            mm(2 + b, "x", 128 * b, "u", 0, 128)
-        mm(1, "uh", 0, "x", 0, C)
-        mm(5, "us", 0, "x", 0, C)
-        for b in range(3):
-            act(["ps%d" % (2 + b)], [("hs", b, b + 1)], T.hs[:, b:b + 1], T["ps%d" % (2 + b)][:, 1:2])
-        for b in range(3):
-            act(["ps1", ("hs", b, b + 1)], [("sgn", C * b, C * b + C)], pl(T.sgn, b), T.ps1[:, 0:C], SIGN, bias=T.hs[:, b:b + 1], scale=-1.0)
-
-    def planes():
-        for t, bank in enumerate((6, 2, 1, 7)):
-            mm(bank, "k", 128 * (EB0 + t), "x", 0, C)
-        for t, bank in enumerate((6, 2, 1, 7)):
-            act(["ps%d" % bank], ["fp%d" % t], pl(T.fp, t), T["ps%d" % bank][:, 0:C])
+        select(const(EB0 + t), at("c16"), [[1, 512]], EQ, 0.0, -t, -4)
+    for k, value in ((KP, 256.0), (KN, -256.0), (K3, 3.0)):
+        fill(const(k), value)
+    for a, b in ((KP, K3), (K3, EB0), (EB0, EB0 + 4)):
+        quant("k", "cb", 128 * a, 128 * b)
+    vts(at("pcol", 1, 2), at("pcol", 0, 1), 15, None, AluOpType.bitwise_and)
+    vts(at("pcol", 2, 3), at("pcol", 0, 1), 4, None, AluOpType.arith_shift_right)
+    vcp(at("qg", 0, 2), at("pcol", 1, 3))
+    q_of, g_of, less_q, shift_of, group_at, place_at = [at("qg", k, k + 1) for k in range(6)]
+    act(less_q, q_of, scale=-1.0)
+    act(shift_of, q_of, IDENT, bias=15.0 * SHIFT, scale=-SHIFT)
+    act(group_at, g_of, IDENT, bias=shift_of, scale=384.0)
+    vts(place_at, q_of, -15.0, shift_of, ADD, ADD)
+    act(at("mask"), at("jmod"), ABS, bias=less_q)
+    act(at("mask"), at("mask"), RELU, bias=1.0, scale=-1.0)
+    act(at("mb"), at("mask", 0, C), IDENT, bias=-BIG, scale=2 * BIG)
+    act(at("foldb"), at("jmod", 0, C), SIGN)
+    act(at("fold"), at("foldb"), IDENT, bias=-BIG, scale=BIG)
+    act(at("pick"), at("mask"), IDENT, bias=SHIFT, scale=-256.0 * SHIFT)
+    act(at("ct0"), at("jt", 0, 24), IDENT, bias=place_at, scale=-1.0)
+    act(at("jt"), at("jt"), IDENT, bias=q_of)
+    vts(at("jg", 0, 24), at("jt", 0, 24), group_at, None, SUB)
+    vts(at("jg", 24, 48), at("jt", 24, 48), group_at, 384.0, SUB, SUB)
+    for i in range(6):
+        fill(tile("cmp%d" % i, 16 * (4 * i + 1), WIDE[i]), 0.0)
+    fill(slot("t1", 3), 0.0)
+    fill(slot("mk", 3, C, 2 * C), 0.0)
+    fill(at("rs", 0, 1), 0.0)
+    fill(at("uso", 8, 16), 1)
+    vcp(at("uso", 0, 8), at("us32"))
+    quant("u", "ub", 0, 128)
+    add("v", regions(at("u_q"), at("uso")), at("uu_q")[3],
+        lambda: V.tensor_copy(T.uu_q[:, 0:256].bitcast(dt.uint32), T.u_q[:, 0:128].bitcast(dt.uint32).indirect(T.uso[:, 0:16])), 70 + GATHER * 256)
+    act(at("uu_s"), by(at("u_s"), at("uso")))
+    quant("v", "vb", 0, 128)
+    vcp(at("cl"), at("cfi"))
+    act(at("crow"), by(at("iotaj"), at("cl")), IDENT, bias=-512.0)
+    for a in (0, HALF):
+        quant("x", "xb", a, a + HALF)
 
     def turning():
-        for name, op, bank in (("le", LE, 3), ("ge", GE, 4)):
-            for b in range(3):
-                vts([("sgn", C * b, C * b + C)], [name + "#%d" % b], T[name][:, b:4 * C:4], pl(T.sgn, b), 0.0, None, op)
-                yield
-            quant(name, name, 0, C, [name + "#%d" % b for b in range(3)] + [name])
-            mm(bank, "k", 128 * K512, name, 0, C)
-            yield
-        vtt(["ps3", "crow"], ["ka"], T.ka[:], T.ps3[:, 0:C], T.crow[:], ADD)
-        yield
+        mm(1, "uu", 128, "x", 0, C)
+        for b in range(3):
+            a, sign = 128 * b, slot("t1", b)
+            mm(2 + b, "x", a, "u", 0, 128)
+            act(at("hs", b, b + 1), ps(2 + b, 1, 2))
+            act(sign, ps(1), SIGN, bias=at("hs", b, b + 1), scale=-1.0)
+            select(at("su", a, a + 128), slot("t1", b, a, a + 128), [[1, 128]], GE, 1.0, 0, -1)
+            a += 128
+            vts(slot("t2", b, 0, a), slot("t1", b, 0, a), 0.0, None, NE)
+            if a < C:
+                vts(slot("t2", b, a, C), slot("t1", b, a, C), 0.0, 1.0, EQ, ADD)
+        vts(slot("t2", 3), at("su"), 0.0, 2.0, EQ, MUL)
+        quant("t1", "t1", 0, C)
+        quant("t2", "t2", 0, C)
+        for bank, k, key in ((3, KN, at("ka")), (4, KP, pl("win", 7))):
+            mm(bank, "k", 128 * k, "t1", 0, C, True, False)
+            mm(bank, "k", 128 * KP, "t2", 0, C, False, True)
+            vtt(key, ps(bank), at("crow"), ADD)
         for m in range(7):
-            even = m % 2 == 0
-            key = T.ka[:] if even else T.win[:, 7 * C:8 * C]
-            last = T.ones[:] if m == 0 else T.mk[:, mark:mark + 4 * (C - 1) + 1:4]
-            scan(["ka" if even else ("win", 7 * C, 8 * C), "ones" if m == 0 else "mk#%d" % (m - 1)], [("win", C * m, C * m + C)],
-                 pl(T.win, m), last, key, MUL, MAX)
-            yield
-            if m == 0:
-                vtt(["ps4", "crow"], [("win", 7 * C, 8 * C)], pl(T.win, 7), T.ps4[:, 0:C], T.crow[:], ADD)
-                yield
-            mark = m if m < 4 else 4 * C + m - 4
-            bank = 3 if even else 4
-            vtt(["ps%d" % bank, ("win", C * m, C * m + C)], ["mk#%d" % m], T.mk[:, mark:mark + 4 * (C - 1) + 1:4],
-                pl(T.win, m), T["ps%d" % bank][:, 0:C], GE)
-            yield
-            if m == 3:
-                quant("mk", "mk", 0, C, ["mk#%d" % i for i in range(4)])
-                mm(6, "k", 128 * K3, "mk", 0, C, True, False)
-                yield
-        quant("mk", "mk", C, 2 * C, ["mk#%d" % i for i in range(4, 7)] + ["mk"])
-        mm(6, "k", 128 * K3, "mk", C, 2 * C, False, True)
-        yield
-        yield
-        cut(T.ps6[:, 0:C], ["ps6"], "kf")
-        yield
+            key, mark = pl("win", 7) if m % 2 else at("ka"), slot("mk", m % 4, C * (m // 4), C * (m // 4) + C)
+            if m:
+                scan(pl("win", m), last, key, MUL, MAX)
+            else:
+                scan(pl("win", m), key, key, MAX, MAX)
+            vtt(mark, pl("win", m), ps(3 + m % 2), GE)
+            last = mark
+            if m % 3 == 0 and m:
+                quant("mk", "mk", C * (m // 4), C * (m // 4) + C)
+                mm(6, "k", 128 * K3, "mk", C * (m // 4), C * (m // 4) + C, m == 3, m == 6)
+        cut("kf", 0, C, ps(6))
+        for a in (0, 24):
+            vtt(at("u1", a, a + 24), table("kf"), at("jg", a, a + 24), ADD)
+        vtt(at("u1"), at("u1"), at("jt"), MAX)
+        vcp(at("oab"), at("u1"))
         for i in range(2):
-            a, b = 24 * i, 24 * i + 24
-            vtt(["kf", ("jg", a, b)], [("u1", a, b)], T.u1[:, a:b], T.kf[:, 15:C:16], T.jg[:, a:b], ADD)
-            yield
-        vtt(["u1", "jt"], ["u1"], T.u1[:], T.u1[:], T.jt[:], MAX)
-        yield
-        vcp(["u1"], ["oab"], T.oab[:], T.u1[:])
-        yield
-        for i in range(2):
-            act(["win", "oab"], ["ar#%d" % i], pl(T.ar, i), T.win[:, 0:8 * C].indirect(T.oab[:, 24 * i:24 * i + 24]))
-        yield
-        for i in range(2):
-            a, b, abf = 24 * i, 24 * i + 24, ("abf", C * i, C * i + C)
-            scan(["ar#%d" % i, "pick"], [abf], pl(T.abf, i), T.pick[:], pl(T.ar, i), ADD, MAX)
-            yield
-            vcp([abf], [("ti", a, b)], T.ti[:, a:b], T.abf[:, C * i + 15:C * i + C:16])
-            yield
-            vts([("ti", a, b)], [("ti", a, b)], T.ti[:, a:b], T.ti[:, a:b], 511, None, AluOpType.bitwise_and)
-            yield
-            vcp([("ti", a, b)], [("at", a, b)], T.at[:, a:b], T.ti[:, a:b])
-            if i == 0:
-                for t in range(4):
-                    act(["fc%d" % t, ("at", a, b)], ["ag%d" % t], pl(T.ag, t), pl(T.fc, t).indirect(T.at[:, a:b]))
-            yield
+            act(pl("ar", i), by(at("win"), at("oab", 24 * i, 24 * i + 24)))
 
-    def orders(r):
-        for dst, by, op in (("sm", "mask", MUL), ("smk", "mbig", MIN)):
-            for a, bank in ((0, "ps0"), (HALF, "ps7")):
-                vtt([bank, by], [(dst, a, a + HALF)], T[dst][:, a:a + HALF], T[bank][:, 0:HALF], T[by][:, a:a + HALF], op)
-            yield
-        scan(["sm", "fold0"], ["sf"], T.sf[:], T.fold0[:], T.sm[:], MUL, ADD)
-        act(["sf", "uso"], ["ex"], T.ex[:], T.sf[:, 0:C].indirect(T.uso[:, 8:32]))
-        yield
-        score = [T.sf[:, 16 * c + 15:16 * c + 16] for c in range(24)]
-        for c in range(23, 4 * FIRST - 2, -1):
-            if c >= 4 * FIRST:
-                a = C * (c % 12)
-                act(["ps5", "sf"], [("sig", a, a + C)], T.sig[:, a:a + 16 * c], T.ps5[:, 0:16 * c], SIGN, bias=score[c], scale=-1.0)
-            if c < 23:
-                d = c + 1
-                i, t, a = d // 4, d % 4, C * (d % 12)
-                name = "cmp%d" % i
-                act([("sig", a, a + C), "half", name], [name + "#%d" % t, ("rs", d, d + 1)], T[name][:, t:64 * (d - 1) + 60 + t + 1:4],
-                    T.sig[:, a:a + 16 * d], SIGN, bias=T.half[:, 0:1], scale=-1.0, accum_out=T.rs[:, d:d + 1])
-                if d == 20:
-                    yield
-
-        def counts(name, half, cols, first=False, last=False):
-            mm(2, "k", 128 * (SGH if half else SG), name, 0, cols, first, last)
-
-        def pack(i):
+    def orders():
+        for a, bank in ((0, 0), (HALF, 7)):
+            mm(bank, "uu", 0, "x", a, a + HALF)
+            vtt(at("sm", a, a + HALF), ps(bank, 0, HALF), at("mb", a, a + HALF), MIN)
+            scan(at("sf", a, a + HALF), at("fold", a, a + HALF), at("sm", a, a + HALF), ADD, MAX)
+            vtt(slot("cmp5", 3, a, a + HALF), at("sf", a, a + HALF), ps(bank, 0, HALF), GE)
+        mm(5, "uu", 0, "x", 0, C)
+        for c in range(23, 0, -1):
+            score, out, a = at("sf", 16 * c + 15, 16 * c + 16), slot("cmp%d" % ((c - 1) // 4), (c - 1) % 4, 0, 16 * c), C * (c % 12)
+            if c > BY_VECTOR:
+                act(at("sig", a, a + 16 * c), ps(5, 0, 16 * c), SIGN, bias=score, scale=-1.0)
+                act(out, at("sig", a, a + 16 * c), RELU, accum_out=at("rs", c, c + 1))
+            else:
+                vts(out, ps(0, 0, 16 * c), score, None, LT)
+                act(pl("junk", c % 4, 0, 16 * c), out, accum_out=at("rs", c, c + 1))
+        scan(at("dr"), at("foldb"), slot("cmp5", 3), MUL, ADD)
+        vtt(at("rc"), at("ct0"), table("dr"), ADD)
+        for i in range(5, -1, -1):
             name = "cmp%d" % i
-            quant(name, name, 0, WIDE[i], [name + "#%d" % t for t in range(4)] + [name])
-            counts(name, i >= FIRST, WIDE[i], i == 5, i == FIRST)
+            quant(name, name, 0, WIDE[i])
+            mm(2, "k", 128 * SG, name, 0, WIDE[i], i == 5, i == 0)
+        vtt(at("rc"), at("rs"), at("rc"), ADD)
+        cut("cf2", 0, C, ps(2))
+        vtt(at("rc"), table("cf2"), at("rc"), SUB)
+        vcp(at("pos"), at("rc"))
+        vcp(by(at("inv"), at("pos")), at("iotaj"))
 
-        for i in range(FIRST - 1, -1, -1):
-            name = "cmp%d" % i
-            for t in range(3, -1, -1):
-                c = 4 * i + t
-                if c:
-                    part, end = name + "#%d" % t, 64 * (c - 1) + 60 + t + 1
-                    vts(["ps0", "sf", name], [part], T[name][:, t:end:4], T.ps0[:, 0:16 * c], score[c], None, GE)
-                    act([part], [("junk", C * t, C * t + C), ("rs", c, c + 1)], T.junk[:, C * t:C * t + 16 * c], T[name][:, t:end:4],
-                        accum_out=T.rs[:, c:c + 1])
-                    yield
-            if i == FIRST - 1:
-                vtt(["smk", "ex", "dg"], ["dg#0"], T.dg[:, 0:4 * C - 3:4], T.smk[:], T.ex[:], GE)
-                yield
-        if r == 0:
-            quant("k", "cb", 768, 1024, [("cb", 3072, 4096)])
-            yield
-        pack(5)
-        yield
-        quant("dg", "dg", 0, C, ["dg#0", "dg"])
-        counts("dg", False, C)
-        yield
-        scan(["dg#0", "foldb"], ["dr"], T.dr[:], T.foldb[:], T.dg[:, 0:4 * C - 3:4], MUL, ADD)
-        yield
-        vtt(["ct0", "dr"], ["rc"], T.rc[:], T.ct0[:], T.dr[:, 15:C:16], ADD)
-        yield
-        for i in range(FIRST - 1, -1, -1):
-            pack(i)
-            yield
+    def planes():
+        for t, bank in enumerate((0, 7, 1, 5)):
+            mm(bank, "k", 128 * (EB0 + t), "x", 0, C)
+            act(pl("fp", t), ps(bank))
+
+    def blend(a, b, both):
+        n, k, it = b - a, (b - a) // 16, at("it", a // 16, b // 16)
+        cut("itf", a, b, at("inv", a, b))
+        vts(it, table("itf", a, b), shift_of, None, SUB)
+        for i in range(2):
+            (vcp if both and i else act)(at("ab", 2 * a + i * n, 2 * a + i * n + n), by(pl("ar", i), it))
+        cut("abf", 2 * a, 2 * b, at("ab", 2 * a, 2 * b))
+        ti, a8 = at("ti", a // 8, b // 8), a // 8
+        vcp(ti, table("abf", 2 * a, 2 * b))
+        vts(ti, ti, 511, None, AluOpType.bitwise_and)
+        vcp(at("at", a8, b // 8), ti)
         for t in range(4):
-            act(["fp%d" % t, "cl"], ["fc%d" % t], pl(T.fc, t), pl(T.fp, t).indirect(T.cl[:, 0:24]))
-        for i in range(4, FIRST - 1, -1):
-            pack(i)
-            yield
-        vts([("rs", 4 * FIRST, 24)], [("rs", 4 * FIRST, 24)], T.rs[:, 4 * FIRST:24], T.rs[:, 4 * FIRST:24], 0.5, None, MUL)
-        yield
-        vtt(["rs", "rc"], ["rc"], T.rc[:], T.rs[:], T.rc[:], ADD)
-        yield
-        cut(T.ps2[:, 0:C], ["ps2"], "cf2")
-        yield
-        vtt(["rc", "cf2"], ["rc"], T.rc[:], T.rc[:], T.cf2[:, 15:C:16], SUB)
-        yield
-        vcp(["rc"], ["pos"], T.pos[:], T.rc[:])
-        yield
-        vcp(["iotaj", "pos"], ["inv"], T.inv[:, 0:C].indirect(T.pos[:, 0:24]), T.iotaj[:])
-        yield
-        cut(T.inv[:, 0:M], ["inv"], "cf2", M)
-        yield
-        vts(["cf2", ("qg", 7, 8)], ["lo"], T.lo[:], T.cf2[:, 15:M:16], shift_of, None, SUB)
-        yield
+            act(pl("ag", t, a, b), by(pl("fp", t), at("at", a8, a8 + k)))
+            vtt(pl("zs", t, a, b), by(pl("fp", t), at("at", a8 + k, a8 + 2 * k)), pl("ag", t, a, b), ADD)
 
     nxt = T.cores[(rank + 1) % len(T.cores)]
     rid, pid = topo.addr(nxt)[:2]
     engines = len(topo.engines(core, nxt))
 
-    for r in range(ROUNDS):
-        products()
-        chains = [[orders(r), 40, 0], [turning(), 48, 0]]
-        for _ in range(4):
-            next(chains[0][0])
-        if r == 0:
-            packs()
-        planes()
-        if r == 0:
-            tables()
-        while chains:
-            c = min(chains, key=lambda e: e[2] / e[1])
-            c[2] += 1
-            if next(c[0], 0) == 0:
-                chains.remove(c)
-        for t in range(4):
-            vtt(["fc%d" % t, ("at", 24, 48), "ag%d" % t], ["zp%d" % t], pl(T.zp, t), pl(T.fc, t).indirect(T.at[:, 24:48]), pl(T.ag, t), ADD)
-        for t in range(4):
-            out, in_ = T.eb[:, t:4 * M:4], pl(T.zp, t).indirect(T.lo[:, 0:10])
-            if t < 3:
-                act(["zp%d" % t, "lo"], ["eb#%d" % t], out, in_)
-            else:
-                vcp(["zp%d" % t, "lo"], ["eb#%d" % t], out, in_)
-        name, land, arr = "e%d" % r, "land%d" % r, "arr%d" % r
-        quant(name, "eb", 0, M, ["eb#%d" % t for t in range(4)])
-        waits("p", full([name + "_q"]), [])
-        g.remote_dma(T[land + "_q"][:, 0:M].bitcast(dt.uint8), T[name + "_q"][:, 0:M].bitcast(dt.uint8), T.sem[arr], T.sem.sent, pid, rid,
+    def send(r):
+        name, land, arr = "e%d" % r, "land%d" % r, T.sem["arr%d" % r]
+        g.remote_dma(T[land + "_q"][:, 0:M].bitcast(dt.uint8), T[name + "_q"][:, 0:M].bitcast(dt.uint8), arr, T.sem.sent, pid, rid,
                      topo.mask(core, nxt))
-        g.remote_dma(T[land + "_s"][:, 0:M], T[name + "_s"][:, 0:M], T.sem[arr], T.sem.sent, pid, rid, topo.mask(core, nxt))
-        note("d" + arr, (arr, 2 * engines), [], full([land + "_q"]))
-        for a, b, c in ((0, 224, 384), (160, 160, 224), (224, 0, 160)):
-            act(["inv"], [("wrow", a, a + c - b)], T.wrow[:, a:a + c - b], T.inv[:, b:c])
-        vcp(["wrow", "pos"], ["swap"], T.swap[:], T.wrow[:, 0:C].indirect(T.pos[:, 0:24]))
-        act(["swap", "cl"], ["crm"], T.crm[:], T.swap[:, 0:C].indirect(T.cl[:, 0:24]))
-        if r + 1 < ROUNDS:
-            cut(T.crm[:], ["crm"], "crf")
-            vts(["crf", ("qg", 7, 8)], ["cl"], T.cl[:], T.crf[:, 15:C:16], shift_of, None, SUB)
-        else:
-            dma("y", "stp", ["crm"], [], T.op[:], T.crm[0:128:16, :])
-        if r == 0:
-            quant("v", "vb")
-        banks = (1, 2, 6, 7)
-        for b in range(4):
-            run("t", ["w_q", "w_s", land + "_q"], ["ps%d" % banks[b]],
-                lambda: g.tensor.matmul_mx(T["ps%d" % banks[b]][:, 0:M], codes("w", 128 * b, 128 * b + 128), plane("w", 128 * b, 128 * b + 128),
-                                           codes(land, 0, M), plane(land, 0, M), True, True))
-        for b in range(4):
-            out, in_ = T.rz[:, C * b + C - M:C * b + C], T["ps%d" % banks[b]][:, 0:M]
-            if b == 0:
-                vts(["ps%d" % banks[b]], [("rz%d" % b, C - M, C)], out, in_, 0.03125, None, MUL)
-            else:
-                act(["ps%d" % banks[b]], [("rz%d" % b, C - M, C)], out, in_, scale=0.03125)
-        for b in range(4):
-            vtt(["rz%d" % b, "pos", "zp%d" % b], ["xb#%d" % b], T.xb[:, b:4 * C:4], pl(T.rz, b).indirect(T.pos[:, 0:24]), pl(T.zp, b), ADD)
-        for a in (0, HALF):
-            quant("x", "xb", a, a + HALF, ["xb#%d" % b for b in range(4)])
+        g.remote_dma(T[land + "_s"][:, 0:M], T[name + "_s"][:, 0:M], arr, T.sem.sent, pid, rid, topo.mask(core, nxt))
 
-    mm(0, "v", 0, "x", 0, HALF)
-    mm(5, "v", 0, "x", HALF, C)
-    dma("y", "stc", ["x_q"], [], T.oc[:], T.x_q[:, 0:C].bitcast(dt.uint8))
+    for r in range(ROUNDS):
+        more, name, land = r + 1 < ROUNDS, "e%d" % r, "land%d" % r
+        turning()
+        orders()
+        planes()
+        blend(0, M, True)
+        for t in range(4):
+            vts(slot("eb", t, 0, M), pl("zs", t, 0, M), 0.03125, None, MUL)
+        quant(name, "eb", 0, M)
+        add("p", regions(at(name + "_q"), at(name + "_s")), regions(at(land + "_q"), at(land + "_s")), lambda r=r: send(r), 200, REMOTE,
+            "arr%d" % r, 2 * engines)
+        blend(M, C, False)
+        for a, b, c in ((0, REST, C), (M, M, REST), (REST, 0, M)):
+            act(at("wrow", a, a + c - b), at("inv", b, c))
+        act(at("swap"), by(at("wrow"), at("pos")))
+        act(at("crow"), by(at("swap"), at("cl")), IDENT, bias=-512.0 * more)
+        if more:
+            cut("crf", 0, C, at("crow"))
+            vts(at("cl"), table("crf"), shift_of, 512.0, SUB, ADD)
+        else:
+            dma("y", "stp", at("crow")[3], [], T.op[:], T.crow[0:128:16, :])
+        for b, bank in enumerate((1, 2, 6, 7)):
+            mm(bank, "w", 128 * b, land, 0, M)
+            vtt(pl("zs", b, REST, C), ps(bank, 0, M), pl("zs", b, REST, C), ADD)
+        for a in (0, HALF):
+            for b in range(4):
+                out, in_ = slot("xb", b, a, a + HALF), by(pl("zs", b), at("pos", a // 16, a // 16 + 12))
+                if b < 3 - a // HALF:
+                    act(out, in_, scale=0.03125)
+                else:
+                    vts(out, in_, 0.03125, None, MUL)
+            quant("x", "xb", a, a + HALF)
+
+    for i, a in enumerate((0, HALF)):
+        mm(5 * i, "v", 0, "x", a, a + HALF)
+        dma("y", "stc%d" % i, at("x_q", a, a + HALF)[3], [], T.oc[:, 4 * a:4 * a + 2 * C], T.x_q[:, a:a + HALF].bitcast(dt.uint8))
+        (vcp if i else act)(at("yb", a, a + HALF), ps(5 * i, 0, HALF))
+        dma("s", "sty%d" % i, at("yb", a, a + HALF)[3], [], T.y[:, a:a + HALF], T.yb[:, a:a + HALF])
     for k in range(4):
-        dma("y", "sts%d" % k, ["x_q"], [], T.osc[4 * k:4 * k + 4, :], T.x_s[32 * k:32 * k + 4, 0:C])
-    act(["ps0"], [("yb", 0, HALF)], T.yb[:, 0:HALF], T.ps0[:, 0:HALF])
-    dma("s", "sty", [("yb", 0, HALF)], [], T.y[:, 0:HALF], T.yb[:, 0:HALF])
-    vcp(["ps5"], [("yb", HALF, C)], T.yb[:, HALF:C], T.ps5[:, 0:HALF])
-    dma("s", "sty2", [("yb", HALF, C)], [], T.y[:, HALF:C], T.yb[:, HALF:C])
-    for s in ("vec", "act", "ten", "pool"):
-        g.wait_ge(T.sem[s], count[s])
-    for s in ("ldx", "ldu", "ldv", "ldw", "lds", "ldc", "sty", "sty2", "stp", "stc", "sts0", "sts1", "sts2", "sts3"):
+        dma("y", "sts%d" % k, at("x_s")[3], [], T.osc[4 * k:4 * k + 4, :], T.x_s[32 * k:32 * k + 4, 0:C])
+
+    def clash(q, kind, key, q2, kind2):
+        return kind == "w" or kind2 == "w" or (key[:2] == "ps" and q != q2)
+
+    def behind(hist, q, reads, writes):
+        return [e for kind, regs in (("r", reads), ("w", writes)) for key, lo, hi in regs for e in
+                [(e[4], kind, e[2], e[3]) for e in hist.get(key, []) if lo < e[1] and e[0] < hi and clash(q, kind, key, e[3], e[2])]]
+
+    def note(hist, q, who, reads, writes):
+        for key, lo, hi in writes:
+            hist[key] = [e for e in hist.get(key, []) if not (lo <= e[0] and e[1] <= hi)] + [(lo, hi, "w", q, who)]
+        for key, lo, hi in reads:
+            hist.setdefault(key, []).append((lo, hi, "r", q, who))
+
+    hist, needs = {}, []
+    for i, c in enumerate(calls):
+        needs.append({e[0]: WAIT * (not free(c[0], e)) for e in sorted(behind(hist, c[0], c[1], c[2]), key=lambda e: not free(c[0], e))})
+        note(hist, c[0], i, c[1], c[2])
+    late = [c[5] - c[4] for c in calls]
+    before = [{j: w + late[j] for j, w in n.items()} for n in needs]
+    after = [{} for _ in calls]
+    for i, n in enumerate(before):
+        for j, w in n.items():
+            after[j][i] = w
+
+    def walk(way, edges, back, first):
+        left, soonest = [len(n) for n in edges], list(first)
+        ready = {q: [i for i, c in enumerate(calls) if c[0] == q and not left[i]] for q in queue}
+        idle, end = {q: 0.0 for q in queue}, {}
+        for _ in calls:
+            soon, q = min((max(idle[q], min(soonest[i] for i in r)), q) for q, r in ready.items() if r)
+            start = {i: max(idle[q], soonest[i]) for i in ready[q]}
+            i = max((i for i in ready[q] if start[i] <= soon + SLACK), key=lambda i: (way[i], -i))
+            held = [h for h in ready[q] if start[h] + max(way[h], calls[h][4] + way[i]) + LOOK
+                    < max(start[i] + way[i], max(start[i] + calls[i][4], start[h]) + way[h]) and h != i]
+            i = min(held, key=lambda h: start[h] - way[h], default=i)
+            idle[q] = end[i] = start[i] + calls[i][4]
+            ready[q].remove(i)
+            for u, w in back[i].items():
+                left[u] -= 1
+                soonest[u] = max(soonest[u], end[i] + w)
+                if not left[u]:
+                    ready[calls[u][0]].append(u)
+        return end
+
+    way, walks = {}, []
+    for i in range(len(calls) - 1, -1, -1):
+        way[i] = calls[i][4] + max([late[i]] + [way[u] + w for u, w in after[i].items()])
+    for _ in range(PASSES):
+        end = walk(way, before, after, [0] * len(calls))
+        walks.append((max(end[i] + late[i] for i in end), sorted(end, key=lambda i: (end[i] - calls[i][4], i))))
+        back = walk(end, after, before, late)
+        way = {i: (way[i] + back[i]) / 2 for i in way}
+    order = min(walks)[1]
+
+    count = {s: 0 for s in own.values()}
+    seen, clock, event = {q: {} for q in queue}, {}, {}
+    for i in order:
+        q, _, _, call, _, _, sem, n = calls[i]
+        need = {}
+        for j, w in needs[i].items():
+            if w:
+                need[event[j][0]] = max(need.get(event[j][0], 0), event[j][1])
+        need = {s: k for s, k in need.items() if seen[q].get(s, 0) < k}
+        for s in sorted(need):
+            if any(o != s and clock[(o, need[o])].get(s, 0) >= need[s] for o in need if need[o]):
+                need[s] = 0
+        for s, k in need.items():
+            if k and seen[q].get(s, 0) < k:
+                queue[q].wait_ge(T.sem[s], k)
+                for s2, k2 in clock[(s, k)].items():
+                    seen[q][s2] = max(seen[q].get(s2, 0), k2)
+        made = call()
+        if sem is None:
+            sem = own[q]
+            count[sem] += 1
+            n = count[sem]
+            made.then_inc(T.sem[sem], 1)
+        elif made is not None:
+            made.then_inc(T.sem[sem], n)
+        event[i] = (sem, n)
+        clock[event[i]] = {**(seen[q] if made is not None else {}), sem: n}
+    for s, n in count.items():
+        g.wait_ge(T.sem[s], n)
+    for s in MOVES:
         g.wait_ge(T.sem[s], 16)
     g.wait_ge(T.sem.sent, 2 * engines * ROUNDS)
+
+
+def free(q, e):
+    return e[1] == "w" and e[3] == q == "t"

@@ -17,22 +17,22 @@ def _pair(name, cols):
     _buf(name + "_s", cols, "uint8")
 
 
-for _n, _c in (("xb", 4 * C), ("ub", 512), ("vb", 512), ("cb", 8 * 512), ("sig", 12 * C), ("c16", 512), ("ones", 512), ("dr", C),
-               ("t1", 4 * C), ("t2", 4 * C), ("su", C), ("mk", 8 * C), ("junk", 4 * C), ("eb", 4 * M), ("foldb", C),
+for _n, _c in (("xb", 4 * C), ("ub", 512), ("vb", 512), ("cb", 9 * 512), ("sig", 12 * C), ("ones", 512), ("dr", C), ("t1", 4 * C),
+               ("t2", 4 * C), ("mk", 8 * C), ("junk", 4 * C), ("eb", 4 * M), ("foldb", C), ("m6", C), ("m6f", C), ("pick2", C),
                ("fp", 4 * C), ("ag", 4 * C), ("zs", 4 * C)):
     _buf(_n, _c, BF)
 for _i in range(6):
     _buf("cmp%d" % _i, 4 * WIDE[_i], BF)
 for _n, _c in (("iotaj", C), ("crow", C), ("jmod", 2 * REST), ("jt", 48), ("jg", 48), ("ct0", 24), ("qg", 10), ("mask", 2 * REST),
-               ("fold", C), ("pick", 2 * REST), ("mb", C), ("hs", 4), ("ka", C), ("win", 8 * C), ("u1", 48), ("kf", C), ("ar", 2 * C),
-               ("ab", 2 * C), ("abf", 2 * C), ("sm", C), ("sf", C), ("rs", 24), ("rc", 24), ("cf2", C), ("inv", C), ("itf", C),
-               ("wrow", C), ("swap", C), ("crf", C), ("yb", C)):
+               ("fold", C), ("pick", 2 * REST), ("mb", C), ("hs", 4), ("ka", C), ("win", 8 * C), ("u1", 48), ("u2", 48), ("kf", C),
+               ("ar", 2 * C), ("ab", 2 * C), ("sm", C), ("sf", C), ("rs", 24), ("rc", 24), ("cf2", C), ("inv", C), ("itf", C),
+               ("wrow", C), ("swap", C), ("crf", C), ("yb", C), ("hm", C), ("later", C)):
     _buf(_n, _c, F32)
-for _n, _c in (("cfi", 24), ("pcol", 4), ("us32", 8), ("ti", 48)):
+for _n, _c in (("cfi", 24), ("pcol", 4), ("us32", 8), ("ti", 48), ("abf", 2 * C)):
     _buf(_n, _c, "int32")
 for _n, _c in (("uso", 16), ("oab", 48), ("at", 48), ("pos", 24), ("it", 24), ("cl", 24)):
     _buf(_n, _c, "uint16")
-for _n, _c in (("u", 128), ("uu", 256), ("v", 128), ("w", 512), ("x", C), ("k", 8 * 128), ("t1", C), ("t2", C), ("mk", 2 * C)):
+for _n, _c in (("u", 128), ("uu", 256), ("v", 128), ("w", 512), ("x", C), ("k", 9 * 128), ("t1", C), ("t2", C), ("mk", 2 * C)):
     _pair(_n, _c)
 for _i in range(6):
     _pair("cmp%d" % _i, WIDE[_i])
@@ -44,16 +44,20 @@ for _b in range(8):
 MOVES = ["ldx0", "ldu", "ldx1", "ldc", "ldw", "lds", "ldv", "stp", "stc0", "stc1", "sts0", "sts1", "sts2", "sts3", "sty0", "sty1"]
 SEMAPHORES = ["vec", "act", "ten", "pool", "sent", "arr0", "arr1", "arr2"] + MOVES
 
-LT, GE, EQ, NE = AluOpType.is_lt, AluOpType.is_ge, AluOpType.is_equal, AluOpType.not_equal
+LT, GT, GE, EQ, NE = AluOpType.is_lt, AluOpType.is_gt, AluOpType.is_ge, AluOpType.is_equal, AluOpType.not_equal
 ADD, SUB, MUL, MAX, MIN = AluOpType.add, AluOpType.subtract, AluOpType.mult, AluOpType.max, AluOpType.min
 COPY, SIGN = ActivationFunctionType.Copy, ActivationFunctionType.Sign
 ABS, RELU, IDENT = ActivationFunctionType.Abs, ActivationFunctionType.Relu, ActivationFunctionType.Identity
 SHIFT = 2.0 ** 18
 BIG = 1e29
-KP, KN, K3, SG, EB0 = 0, 1, 2, 3, 4
+KP, KX, KY, K3, SG, EB0 = 0, 1, 2, 3, 4, 5
 BY_VECTOR = 0
-WAIT, LOCAL, BYTE, REMOTE, GATHER, SCATTER = 120, 1600, 0.5, 3600, 1.6, 3.8
-PASSES, SLACK, LOOK = 4, 100, 150
+TILES = (5, 4, 3, 2, 1, 0)
+DIRECT = True
+MORE = 1
+TURNS = {"v": "fflfffffqlql" "agaggattattgttrtrcrcr" "tkktktktotototktcotdtootdtoododtoot" "ddtddottdocto" "ezezeeeezeeeezezezzzz",
+         "s": "fffff" "hhttht" "ss" + "so" * 21 + "oo" "pptptp" "ezzweeeeeweewwzzzzw",
+         "t": "ffff" "ahghtaah" "tttt" "ppoodoooodpp"}
 
 
 def rank_program(g, core, T, topo):
@@ -64,227 +68,263 @@ def rank_program(g, core, T, topo):
     queue = {"v": V, "s": S, "t": g.tensor, "p": g, "y": g.sync}
     own = {"v": "vec", "s": "act", "t": "ten", "p": "pool"}
     calls = []
+    chain, chains = ["", 0], {}
 
     def at(name, a=0, b=None, step=1):
         b = SCRATCH[name][1][1] if b is None else b
-        return T[name][:, a:b:step] if step > 1 else T[name][:, a:b], len(range(a, b, step)), SCRATCH[name][2], [(name, a, b)], False
+        return T[name][:, a:b:step] if step > 1 else T[name][:, a:b], len(range(a, b, step)), [(name, a, b)], False
 
     def slot(name, t, a=0, b=C):
-        return T[name][:, 4 * a + t:4 * (b - 1) + t + 1:4], b - a, BF, [(name + "#%d" % t, a, b)], False
+        return T[name][:, 4 * a + t:4 * (b - 1) + t + 1:4], b - a, [(name + "#%d" % t, a, b)], False
 
     def tile(name, a, b):
-        return T[name][:, 4 * a:4 * b], 4 * (b - a), BF, [(name + "#%d" % t, a, b) for t in range(4)], False
+        return T[name][:, 4 * a:4 * b], 4 * (b - a), [(name + "#%d" % t, a, b) for t in range(4)], False
 
     def pl(name, t, a=0, b=C):
         return at(name, C * t + a, C * t + b)
 
     def by(win, off):
-        return win[0].indirect(off[0]), 16 * off[1], win[2], win[3] + off[3], True
+        return win[0].indirect(off[0]), 16 * off[1], win[2] + off[2], True
 
     def ps(bank, a=0, b=C):
-        return T["ps%d" % bank][:, a:b], b - a, "psum", [("ps%d" % bank, 0, 512)], False
+        return T["ps%d" % bank][:, a:b], b - a, [("ps%d" % bank, 0, 512)], False
 
     def table(name, a=0, b=C):
         return at(name, a + 15, b, 16)
+
+    def const(k):
+        return tile("cb", 128 * k, 128 * k + 128)
 
     def ap(x):
         return x[0] if isinstance(x, tuple) else x
 
     def regions(*xs):
-        return [r for x in xs if isinstance(x, tuple) for r in x[3]]
+        return [r for x in xs if isinstance(x, tuple) for r in x[2]]
 
-    def add(q, reads, writes, call, cycles, late=0, sem=None, n=1):
-        calls.append((q, reads, writes, call, cycles, cycles + late, sem, n))
-
-    def cycles(out, in0, rate):
-        if out[4]:
-            return 60 + SCATTER * out[1]
-        if in0[4]:
-            return 70 + max(rate, GATHER) * in0[1]
-        return max(64, rate * in0[1])
-
-    def fast(*xs):
-        return 0.5 if all(x[2] in (BF, "uint16") for x in xs) else 1
-
-    def scattered(out):
-        return (out[3][1:], out[3][:1]) if out[4] else ([], out[3])
+    def add(q, reads, writes, call, sem=None, n=1):
+        chains.setdefault((q, chain[1], chain[0] if q in TURNS else ""), []).append(len(calls))
+        calls.append((q, reads, writes, call, sem, n))
 
     def vts(out, in0, s1, s2, *ops):
-        add("v", regions(in0, s1, s2), out[3], lambda: V.tensor_scalar(out[0], in0[0], ap(s1), ap(s2), *ops), cycles(out, in0, fast(out, in0)))
+        add("v", regions(in0, s1, s2), out[2], lambda: V.tensor_scalar(out[0], in0[0], ap(s1), ap(s2), *ops))
 
     def vtt(out, in0, in1, op):
-        add("v", regions(in0, in1), out[3], lambda: V.tensor_tensor(out[0], in0[0], in1[0], op),
-            cycles(out, in0, 1 if "psum" in (in0[2], in1[2]) else 2))
+        add("v", regions(in0, in1), out[2], lambda: V.tensor_tensor(out[0], in0[0], in1[0], op))
 
     def vcp(out, in_):
-        lists, window = scattered(out)
-        add("v", in_[3] + lists, window, lambda: V.tensor_copy(out[0], in_[0]), cycles(out, in_, fast(out, in_)))
+        lists, window = (out[2][1:], out[2][:1]) if out[3] else ([], out[2])
+        add("v", in_[2] + lists, window, lambda: V.tensor_copy(out[0], in_[0]))
 
     def act(out, in_, func=COPY, **kw):
-        sums = regions(kw.get("accum_out"))
-        add("s", regions(in_, kw.get("bias")), out[3] + sums, lambda: S.activation(out[0], in_[0], func, **{k: ap(x) for k, x in kw.items()}),
-            cycles(out, in_, 1) + 24 * len(sums))
+        add("s", regions(in_, kw.get("bias")), regions(out, kw.get("accum_out")),
+            lambda: S.activation(out[0], in_[0], func, **{k: ap(x) for k, x in kw.items()}))
 
     def scan(out, d0, d1, op0, op1):
-        add("v", regions(d0, d1), out[3], lambda: V.tensor_tensor_scan(out[0], d0[0], d1[0], 0.0, op0, op1), cycles(out, d0, fast(out, d0, d1)))
+        add("v", regions(d0, d1), out[2], lambda: V.tensor_tensor_scan(out[0], d0[0], d1[0], 0.0, op0, op1))
 
     def fill(out, value):
-        add("v", [], out[3], lambda: V.memset(out[0], value), cycles(out, out, fast(out)))
+        add("v", [], out[2], lambda: V.memset(out[0], value))
 
-    def iota(out, pattern, base, cm):
-        kw = {"allow_small_or_imprecise_dtypes": True} if out[2] == F32 else {}
-        add("p", [], out[3], lambda: P.iota(out[0], pattern, base, cm, **kw), 160 + 2 * out[1])
+    def iota(out, pattern, base, cm, whole=False):
+        kw = {} if whole else {"allow_small_or_imprecise_dtypes": True}
+        add("p", [], out[2], lambda: P.iota(out[0], pattern, base, cm, **kw))
 
     def select(out, in_, *how):
-        add("p", in_[3], out[3], lambda: P.affine_select(out[0], in_[0], *how), 200 + 2 * out[1])
+        add("p", in_[2], out[2], lambda: P.affine_select(out[0], in_[0], *how))
 
     def quant(name, src, a, b):
-        add("v", tile(src, a, b)[3], [(name + "_q", a, b), (name + "_s", a, b)],
-            lambda: V.quantize_mx(T[name + "_q"][:, a:b], T[name + "_s"][:, a:b], tile(src, a, b)[0]), 15 + 1.06 * (b - a))
+        add("v", tile(src, a, b)[2], [(name + "_q", a, b), (name + "_s", a, b)],
+            lambda: V.quantize_mx(T[name + "_q"][:, a:b], T[name + "_s"][:, a:b], tile(src, a, b)[0]))
 
     def mm(bank, l, la, r, ra, rb, start=True, stop=True):
         reads = [(l + "_q", la, la + 128), (l + "_s", la, la + 128), (r + "_q", ra, rb), (r + "_s", ra, rb)]
-        add("t", reads, ps(bank)[3],
+        add("t", reads, ps(bank)[2],
             lambda: g.tensor.matmul_mx(ps(bank, 0, rb - ra)[0], T[l + "_q"][:, la:la + 128], T[l + "_s"][:, la:la + 128],
-                                       T[r + "_q"][:, ra:rb], T[r + "_s"][:, ra:rb], start, stop), rb - ra + 16)
+                                       T[r + "_q"][:, ra:rb], T[r + "_s"][:, ra:rb], start, stop))
 
-    def dma(q, sem, reads, writes, out, in_, ahead=0):
-        add(q, reads, writes, lambda: queue[q].dma_start(out, in_), 60, LOCAL + ahead * BYTE, sem, 16)
+    def dma(q, sem, reads, writes, out, in_):
+        add(q, reads, writes, lambda: queue[q].dma_start(out, in_), sem, 16)
 
     def cut(dst, a, b, row):
         scan(at(dst, a, b), at("pick", 0, b - a), row, ADD, MAX)
 
-    def const(k):
-        return tile("cb", 128 * k, 128 * k + 128)
+    def last(out, x, y, op, turned=False):
+        if DIRECT:
+            vtt(out, *((y, x) if turned else (x, y)), op)
+        else:
+            vtt(x, *((y, x) if turned else (x, y)), op)
+            vcp(out, x)
 
-    dma("s", "ldu", [], tile("ub", 0, 128)[3], T.ub[:], T.u[:], 1024)
-    dma("y", "ldx0", [], tile("xb", 0, HALF)[3], T.xb[:, 0:2 * C], T.x[:, 0:2 * C], 2560)
-    dma("y", "ldx1", [], tile("xb", HALF, C)[3], T.xb[:, 2 * C:4 * C], T.x[:, 2 * C:4 * C], 4096)
-    dma("y", "ldc", [], at("cfi")[3], T.cfi[:], T.cf[:], 4192)
-    later = tile("xb", HALF, C)[3]
-    dma("y", "ldw", later, at("w_q")[3], T.w_q[:, 0:512].bitcast(dt.uint8), T.wc[:], 2048)
-    dma("y", "lds", later, at("w_s")[3], T.w_s[:], T.ws[:], 2560)
-    dma("y", "ldv", later, tile("vb", 0, 128)[3], T.vb[:], T.v[:], 3584)
+    def parts(n):
+        return ((0, n // 2), (n // 2, n)) if n >= 256 else ((0, n),)
 
-    iota(at("pcol", 0, 1), [[1, 1]], 0, 1)
-    iota(at("us32"), [[16, 8]], 0, 0)
+    dma("s", "ldu", [], tile("ub", 0, 128)[2], T.ub[:], T.u[:])
+    dma("s", "ldc", [], at("cfi")[2], T.cfi[:], T.cf[:])
+    for i, (a, b) in enumerate(parts(C)):
+        dma("y", "ldx%d" % i, [], tile("xb", a, b)[2], T.xb[:, 4 * a:4 * b], T.x[:, 4 * a:4 * b])
+    there = tile("xb", HALF, C)[2]
+    dma("y", "ldw", there, at("w_q")[2], T.w_q[:, 0:512].bitcast(dt.uint8), T.wc[:])
+    dma("y", "lds", there, at("w_s")[2], T.w_s[:], T.ws[:])
+    dma("y", "ldv", there, tile("vb", 0, 128)[2], T.vb[:], T.v[:])
+
+    q_of, g_of, less_q, shift_of, place_at, twos_of, *rest = [at("qg", k, k + 1) for k in range(10)]
+    row_at, further = rest[:2], rest[2:]
+    iota(at("pcol", 0, 1), [[1, 1]], 0, 1, True)
+    iota(at("us32"), [[16, 8]], 0, 0, True)
     iota(at("jmod"), [[0, 2 * REST // 16], [1, 16]], 0, 0)
-    iota(at("jt"), [[0, 2], [16, 24]], 0, 0)
-    iota(at("iotaj"), [[1, C]], 0, 0)
+    fill(at("m6"), -BIG)
     fill(at("ones"), 1.0)
-    fill(at("c16"), 16.0)
-    select(const(SG), at("ones"), [[-16, 8], [0, 64]], GE, 0.0, 0, 1)
-    select(const(SG), const(SG), [[16, 8], [0, 64]], GE, 0.0, 15, -1)
-    for t in range(4):
-        select(const(EB0 + t), at("c16"), [[1, 512]], EQ, 0.0, -t, -4)
-    for k, value in ((KP, 256.0), (KN, -256.0), (K3, 3.0)):
-        fill(const(k), value)
-    for a, b in ((KP, K3), (K3, EB0), (EB0, EB0 + 4)):
-        quant("k", "cb", 128 * a, 128 * b)
     vts(at("pcol", 1, 2), at("pcol", 0, 1), 15, None, AluOpType.bitwise_and)
     vts(at("pcol", 2, 3), at("pcol", 0, 1), 4, None, AluOpType.arith_shift_right)
-    vcp(at("qg", 0, 2), at("pcol", 1, 3))
-    q_of, g_of, less_q, shift_of, group_at, place_at = [at("qg", k, k + 1) for k in range(6)]
-    act(less_q, q_of, scale=-1.0)
-    act(shift_of, q_of, IDENT, bias=15.0 * SHIFT, scale=-SHIFT)
-    act(group_at, g_of, IDENT, bias=shift_of, scale=384.0)
-    vts(place_at, q_of, -15.0, shift_of, ADD, ADD)
-    act(at("mask"), at("jmod"), ABS, bias=less_q)
-    act(at("mask"), at("mask"), RELU, bias=1.0, scale=-1.0)
-    act(at("mb"), at("mask", 0, C), IDENT, bias=-BIG, scale=2 * BIG)
-    act(at("foldb"), at("jmod", 0, C), SIGN)
-    act(at("fold"), at("foldb"), IDENT, bias=-BIG, scale=BIG)
-    act(at("pick"), at("mask"), IDENT, bias=SHIFT, scale=-256.0 * SHIFT)
-    act(at("ct0"), at("jt", 0, 24), IDENT, bias=place_at, scale=-1.0)
-    act(at("jt"), at("jt"), IDENT, bias=q_of)
-    vts(at("jg", 0, 24), at("jt", 0, 24), group_at, None, SUB)
-    vts(at("jg", 24, 48), at("jt", 24, 48), group_at, 384.0, SUB, SUB)
-    for i in range(6):
-        fill(tile("cmp%d" % i, 16 * (4 * i + 1), WIDE[i]), 0.0)
-    fill(slot("t1", 3), 0.0)
-    fill(slot("mk", 3, C, 2 * C), 0.0)
-    fill(at("rs", 0, 1), 0.0)
     fill(at("uso", 8, 16), 1)
     vcp(at("uso", 0, 8), at("us32"))
+    vcp(at("qg", 0, 2), at("pcol", 1, 3))
+    fill(tile("cb", 128 * KP, 128 * K3), 256.0)
+    fill(const(K3), 3.0)
+    for k, t in ((KX, 0), (KX, 1), (KY, 0)):
+        fill(slot("cb", t, 128 * k, 128 * k + 128), -256.0)
+    select(at("later"), at("m6"), [[0, 3], [1, 128]], GE, BIG, 0, -1)
+    iota(at("iotaj"), [[1, C]], 0, 0)
+    iota(at("jt"), [[0, 2], [16, 24]], 0, 0)
+    select(const(SG), at("ones"), [[-16, 8], [0, 64]], GE, 0.0, 0, 1)
+    select(const(SG), const(SG), [[16, 8], [0, 64]], GE, 0.0, 15, -1)
+    for t in (2, 3):
+        iota(slot("mk", t, C, 2 * C), [[0, C]], 0, 0)
+    for t in range(4):
+        select(const(EB0 + t), at("ones"), [[1, 512]], EQ, 0.0, -t, -4)
+    act(less_q, q_of, scale=-1.0)
+    act(shift_of, q_of, IDENT, bias=15.0 * SHIFT, scale=-SHIFT)
+    act(twos_of, q_of, IDENT, bias=30.0, scale=-2.0)
+    for i in TILES:
+        fill(tile("cmp%d" % i, 16 * (4 * i + 1), WIDE[i]), 0.0)
+    fill(slot("t2", 3), 0.0)
+    fill(at("rs", 0, 1), 0.0)
+    vts(place_at, q_of, -15.0, shift_of, ADD, ADD)
+    for i in range(2):
+        vts(further[i], g_of, 6.5 - i, 384.0, LT, MUL)
+        vts(row_at[i], g_of, -384.0, -384.0 * i, MUL, ADD)
     quant("u", "ub", 0, 128)
-    add("v", regions(at("u_q"), at("uso")), at("uu_q")[3],
-        lambda: V.tensor_copy(T.uu_q[:, 0:256].bitcast(dt.uint32), T.u_q[:, 0:128].bitcast(dt.uint32).indirect(T.uso[:, 0:16])), 70 + GATHER * 256)
-    act(at("uu_s"), by(at("u_s"), at("uso")))
-    quant("v", "vb", 0, 128)
+    vts(at("qg", 6, 8), at("qg", 6, 8), shift_of, None, SUB)
+    add("v", regions(at("u_q"), at("uso")), at("uu_q")[2],
+        lambda: V.tensor_copy(T.uu_q[:, 0:256].bitcast(dt.uint32), T.u_q[:, 0:128].bitcast(dt.uint32).indirect(T.uso[:, 0:16])))
     vcp(at("cl"), at("cfi"))
+    quant("k", "cb", 128 * KP, 128 * SG)
+    act(at("mask"), at("jmod"), ABS, bias=less_q)
+    act(at("foldb"), at("jmod", 0, C), SIGN)
+    act(at("mask"), at("mask"), RELU, bias=1.0, scale=-1.0)
+    act(at("fold"), at("foldb"), IDENT, bias=-BIG, scale=BIG)
+    act(at("uu_s"), by(at("u_s"), at("uso")))
+    act(at("mb"), at("mask", 0, C), IDENT, bias=-BIG, scale=2 * BIG)
+    act(at("ct0"), at("jt", 0, 24), IDENT, bias=place_at, scale=-1.0)
     act(at("crow"), by(at("iotaj"), at("cl")), IDENT, bias=-512.0)
-    for a in (0, HALF):
-        quant("x", "xb", a, a + HALF)
+    act(at("jt"), at("jt"), IDENT, bias=q_of)
+    act(at("pick"), at("mask"), IDENT, bias=SHIFT, scale=-256.0 * SHIFT)
+    for i in range(2):
+        act(at("jg", 24 * i, 24 * i + 24), at("jt", 0, 24), IDENT, bias=row_at[i])
+    act(at("pick2"), at("mask", 0, C), IDENT, bias=2.0, scale=-64.0)
+    chain[0] = "c"
+    quant("k", "cb", 128 * SG, 128 * EB0)
+    quant("v", "vb", 0, 128)
+    for a, b in parts(512):
+        quant("k", "cb", 128 * EB0 + a, 128 * EB0 + b)
+    chain[0] = "q"
+    for a, b in parts(C):
+        quant("x", "xb", a, b)
 
     def turning():
+        chain[0] = "t"
         mm(1, "uu", 128, "x", 0, C)
-        for b in range(3):
-            a, sign = 128 * b, slot("t1", b)
-            mm(2 + b, "x", a, "u", 0, 128)
-            act(at("hs", b, b + 1), ps(2 + b, 1, 2))
-            act(sign, ps(1), SIGN, bias=at("hs", b, b + 1), scale=-1.0)
-            select(at("su", a, a + 128), slot("t1", b, a, a + 128), [[1, 128]], GE, 1.0, 0, -1)
-            a += 128
-            vts(slot("t2", b, 0, a), slot("t1", b, 0, a), 0.0, None, NE)
+        chain[0] = "g"
+        mm(6, "uu", 128, "x", 0, C)
+        vtt(at("hm"), ps(6), at("later"), MAX)
+        for b, (name, t, u) in enumerate((("t1", 0, 2), ("t1", 1, 3), ("t2", 0, 1))):
+            a, hs = 128 * b + 128, at("hs", b, b + 1)
+            chain[0] = "h"
+            mm(2 + b, "x", a - 128, "u", 0, 128)
+            act(hs, ps(2 + b, 1, 2))
+            chain[0] = "g"
+            vts(slot("t2", 2, a - 128, a), at("hm", a - 128, a), hs, 2.0, EQ, MUL)
+            chain[0] = "t"
+            act(slot(name, t), ps(1), SIGN, bias=hs, scale=-1.0)
+            if b == 2:
+                quant("t1", "t1", 0, C)
+            vts(slot(name, u, 0, a), slot(name, t, 0, a), 0.0, None, NE)
             if a < C:
-                vts(slot("t2", b, a, C), slot("t1", b, a, C), 0.0, 1.0, EQ, ADD)
-        vts(slot("t2", 3), at("su"), 0.0, 2.0, EQ, MUL)
-        quant("t1", "t1", 0, C)
+                vts(slot(name, u, a, C), slot(name, t, a, C), 0.0, 1.0, EQ, ADD)
         quant("t2", "t2", 0, C)
-        for bank, k, key in ((3, KN, at("ka")), (4, KP, pl("win", 7))):
-            mm(bank, "k", 128 * k, "t1", 0, C, True, False)
-            mm(bank, "k", 128 * KP, "t2", 0, C, False, True)
-            vtt(key, ps(bank), at("crow"), ADD)
-        for m in range(7):
-            key, mark = pl("win", 7) if m % 2 else at("ka"), slot("mk", m % 4, C * (m // 4), C * (m // 4) + C)
-            if m:
-                scan(pl("win", m), last, key, MUL, MAX)
-            else:
-                scan(pl("win", m), key, key, MAX, MAX)
-            vtt(mark, pl("win", m), ps(3 + m % 2), GE)
-            last = mark
-            if m % 3 == 0 and m:
-                quant("mk", "mk", C * (m // 4), C * (m // 4) + C)
-                mm(6, "k", 128 * K3, "mk", C * (m // 4), C * (m // 4) + C, m == 3, m == 6)
-        cut("kf", 0, C, ps(6))
+        for name, ks in (("t1", (KX, KP)), ("t2", (KY, KP))):
+            for bank, k in zip((3, 4), ks):
+                mm(bank, "k", 128 * k, name, 0, C, name == "t1", name == "t2")
+        marks = [slot("mk", m % 4, C * (m // 4), C * (m // 4) + C) for m in range(6)] + [at("m6")]
+        chain[0] = "k"
+        for name, lo, bank in (("win", 7 * C, 4), ("ka", 0, 3)):
+            for a, b in parts(C):
+                vtt(at(name, lo + a, lo + b), ps(bank, a, b), at("crow", a, b), ADD)
+        scan(pl("win", 0), at("ka"), at("ka"), MAX, MAX)
+        chain[0] = "t"
+        scan(at("hm"), at("fold"), ps(3), MAX, MAX)
+        vtt(marks[0], at("hm"), ps(3), GT)
+        for m in range(1, 7):
+            scan(pl("win", m), marks[m - 1], pl("win", 7) if m % 2 else at("ka"), MUL, MAX)
+            vtt(marks[m], pl("win", m), ps(3 + m % 2), GE)
+        chain[0] = "d"
+        for a in (0, C):
+            for b, c in parts(C):
+                quant("mk", "mk", a + b, a + c)
+            mm(6, "k", 128 * K3, "mk", a, a + C, not a, a > 0)
+        for a, b in parts(C):
+            cut("kf", a, b, ps(6, a, b))
         for a in (0, 24):
             vtt(at("u1", a, a + 24), table("kf"), at("jg", a, a + 24), ADD)
         vtt(at("u1"), at("u1"), at("jt"), MAX)
-        vcp(at("oab"), at("u1"))
+        chain[0] = "t"
+        scan(at("m6f"), at("pick2"), at("m6"), ADD, MAX)
+        for i in range(2):
+            vts(at("u2", 24 * i, 24 * i + 24), table("m6f"), twos_of, further[i], SUB, MUL)
+        last(at("oab"), at("u2"), at("u1"), ADD)
         for i in range(2):
             act(pl("ar", i), by(at("win"), at("oab", 24 * i, 24 * i + 24)))
 
     def orders():
         for a, bank in ((0, 0), (HALF, 7)):
+            chain[0] = "a"
             mm(bank, "uu", 0, "x", a, a + HALF)
             vtt(at("sm", a, a + HALF), ps(bank, 0, HALF), at("mb", a, a + HALF), MIN)
             scan(at("sf", a, a + HALF), at("fold", a, a + HALF), at("sm", a, a + HALF), ADD, MAX)
+            chain[0] = "r"
             vtt(slot("cmp5", 3, a, a + HALF), at("sf", a, a + HALF), ps(bank, 0, HALF), GE)
+        scan(at("dr"), at("foldb"), slot("cmp5", 3), MUL, ADD)
+        vtt(at("rc"), at("ct0"), table("dr"), ADD)
+        chain[0] = "a"
         mm(5, "uu", 0, "x", 0, C)
         for c in range(23, 0, -1):
             score, out, a = at("sf", 16 * c + 15, 16 * c + 16), slot("cmp%d" % ((c - 1) // 4), (c - 1) % 4, 0, 16 * c), C * (c % 12)
             if c > BY_VECTOR:
+                chain[0] = "s"
                 act(at("sig", a, a + 16 * c), ps(5, 0, 16 * c), SIGN, bias=score, scale=-1.0)
+                chain[0] = "o"
                 act(out, at("sig", a, a + 16 * c), RELU, accum_out=at("rs", c, c + 1))
             else:
+                chain[0] = "j"
                 vts(out, ps(0, 0, 16 * c), score, None, LT)
                 act(pl("junk", c % 4, 0, 16 * c), out, accum_out=at("rs", c, c + 1))
-        scan(at("dr"), at("foldb"), slot("cmp5", 3), MUL, ADD)
-        vtt(at("rc"), at("ct0"), table("dr"), ADD)
-        for i in range(5, -1, -1):
+        chain[0] = "o"
+        for i in TILES:
             name = "cmp%d" % i
-            quant(name, name, 0, WIDE[i])
-            mm(2, "k", 128 * SG, name, 0, WIDE[i], i == 5, i == 0)
+            for a, b in parts(WIDE[i]):
+                quant(name, name, a, b)
+            mm(2, "k", 128 * SG, name, 0, WIDE[i], i == TILES[0], i == TILES[-1])
         vtt(at("rc"), at("rs"), at("rc"), ADD)
-        cut("cf2", 0, C, ps(2))
-        vtt(at("rc"), table("cf2"), at("rc"), SUB)
-        vcp(at("pos"), at("rc"))
+        for a, b in parts(C):
+            cut("cf2", a, b, ps(2, a, b))
+        last(at("pos"), at("rc"), table("cf2"), SUB, True)
         vcp(by(at("inv"), at("pos")), at("iotaj"))
 
     def planes():
-        for t, bank in enumerate((0, 7, 1, 5)):
+        chain[0] = "p"
+        for t, bank in enumerate((7, 1, 0, 5)):
             mm(bank, "k", 128 * (EB0 + t), "x", 0, C)
-            act(pl("fp", t), ps(bank))
+            act(pl("fp", t), ps(bank), scale=16.0)
 
     def blend(a, b, both):
         n, k, it = b - a, (b - a) // 16, at("it", a // 16, b // 16)
@@ -294,8 +334,7 @@ def rank_program(g, core, T, topo):
             (vcp if both and i else act)(at("ab", 2 * a + i * n, 2 * a + i * n + n), by(pl("ar", i), it))
         cut("abf", 2 * a, 2 * b, at("ab", 2 * a, 2 * b))
         ti, a8 = at("ti", a // 8, b // 8), a // 8
-        vcp(ti, table("abf", 2 * a, 2 * b))
-        vts(ti, ti, 511, None, AluOpType.bitwise_and)
+        vts(ti, table("abf", 2 * a, 2 * b), 511, None, AluOpType.bitwise_and)
         vcp(at("at", a8, b // 8), ti)
         for t in range(4):
             act(pl("ag", t, a, b), by(pl("fp", t), at("at", a8, a8 + k)))
@@ -316,104 +355,82 @@ def rank_program(g, core, T, topo):
         turning()
         orders()
         planes()
+        chain[0] = "e"
         blend(0, M, True)
         for t in range(4):
-            vts(slot("eb", t, 0, M), pl("zs", t, 0, M), 0.03125, None, MUL)
+            if t < 3:
+                act(slot("eb", t, 0, M), pl("zs", t, 0, M), scale=0.03125)
+            else:
+                vts(slot("eb", t, 0, M), pl("zs", t, 0, M), 0.03125, None, MUL)
         quant(name, "eb", 0, M)
-        add("p", regions(at(name + "_q"), at(name + "_s")), regions(at(land + "_q"), at(land + "_s")), lambda r=r: send(r), 200, REMOTE,
+        add("p", regions(at(name + "_q"), at(name + "_s")), regions(at(land + "_q"), at(land + "_s")), lambda r=r: send(r),
             "arr%d" % r, 2 * engines)
+        chain[0] = "z"
         blend(M, C, False)
+        chain[0] = "w"
         for a, b, c in ((0, REST, C), (M, M, REST), (REST, 0, M)):
             act(at("wrow", a, a + c - b), at("inv", b, c))
         act(at("swap"), by(at("wrow"), at("pos")))
         act(at("crow"), by(at("swap"), at("cl")), IDENT, bias=-512.0 * more)
+        chain[:] = "l", r + 1
         if more:
-            cut("crf", 0, C, at("crow"))
+            for a, b in parts(C):
+                cut("crf", a, b, at("crow", a, b))
             vts(at("cl"), table("crf"), shift_of, 512.0, SUB, ADD)
         else:
-            dma("y", "stp", at("crow")[3], [], T.op[:], T.crow[0:128:16, :])
+            dma("y", "stp", at("crow")[2], [], T.op[:], T.crow[0:128:16, :])
+        chain[0] = "f"
         for b, bank in enumerate((1, 2, 6, 7)):
             mm(bank, "w", 128 * b, land, 0, M)
             vtt(pl("zs", b, REST, C), ps(bank, 0, M), pl("zs", b, REST, C), ADD)
-        for a in (0, HALF):
+        for a, c in parts(C):
             for b in range(4):
-                out, in_ = slot("xb", b, a, a + HALF), by(pl("zs", b), at("pos", a // 16, a // 16 + 12))
-                if b < 3 - a // HALF:
+                out, in_ = slot("xb", b, a, c), by(pl("zs", b), at("pos", a // 16, c // 16))
+                if b < 2 + (a > 0) * MORE:
                     act(out, in_, scale=0.03125)
                 else:
                     vts(out, in_, 0.03125, None, MUL)
-            quant("x", "xb", a, a + HALF)
+        chain[0] = "q"
+        for a, c in parts(C):
+            quant("x", "xb", a, c)
 
-    for i, a in enumerate((0, HALF)):
-        mm(5 * i, "v", 0, "x", a, a + HALF)
-        dma("y", "stc%d" % i, at("x_q", a, a + HALF)[3], [], T.oc[:, 4 * a:4 * a + 2 * C], T.x_q[:, a:a + HALF].bitcast(dt.uint8))
-        (vcp if i else act)(at("yb", a, a + HALF), ps(5 * i, 0, HALF))
-        dma("s", "sty%d" % i, at("yb", a, a + HALF)[3], [], T.y[:, a:a + HALF], T.yb[:, a:a + HALF])
+    chain[:] = "", ROUNDS + 1
+    for i, (a, b) in enumerate(parts(C)):
+        mm(5 * i, "v", 0, "x", a, b)
+        dma("y", "stc%d" % i, at("x_q", a, b)[2], [], T.oc[:, 4 * a:4 * b], T.x_q[:, a:b].bitcast(dt.uint8))
+        (vcp if i else act)(at("yb", a, b), ps(5 * i, 0, HALF))
+        dma("s", "sty%d" % i, at("yb", a, b)[2], [], T.y[:, a:b], T.yb[:, a:b])
     for k in range(4):
-        dma("y", "sts%d" % k, at("x_s")[3], [], T.osc[4 * k:4 * k + 4, :], T.x_s[32 * k:32 * k + 4, 0:C])
-
-    def clash(q, kind, key, q2, kind2):
-        return kind == "w" or kind2 == "w" or (key[:2] == "ps" and q != q2)
-
-    def behind(hist, q, reads, writes):
-        return [e for kind, regs in (("r", reads), ("w", writes)) for key, lo, hi in regs for e in
-                [(e[4], kind, e[2], e[3]) for e in hist.get(key, []) if lo < e[1] and e[0] < hi and clash(q, kind, key, e[3], e[2])]]
-
-    def note(hist, q, who, reads, writes):
-        for key, lo, hi in writes:
-            hist[key] = [e for e in hist.get(key, []) if not (lo <= e[0] and e[1] <= hi)] + [(lo, hi, "w", q, who)]
-        for key, lo, hi in reads:
-            hist.setdefault(key, []).append((lo, hi, "r", q, who))
+        dma("y", "sts%d" % k, at("x_s")[2], [], T.osc[4 * k:4 * k + 4, :], T.x_s[32 * k:32 * k + 4, 0:C])
 
     hist, needs = {}, []
-    for i, c in enumerate(calls):
-        needs.append({e[0]: WAIT * (not free(c[0], e)) for e in sorted(behind(hist, c[0], c[1], c[2]), key=lambda e: not free(c[0], e))})
-        note(hist, c[0], i, c[1], c[2])
-    late = [c[5] - c[4] for c in calls]
-    before = [{j: w + late[j] for j, w in n.items()} for n in needs]
-    after = [{} for _ in calls]
-    for i, n in enumerate(before):
-        for j, w in n.items():
-            after[j][i] = w
+    for i, (q, reads, writes, *_) in enumerate(calls):
+        needs.append(set())
+        for kind, regs in (("r", reads), ("w", writes)):
+            for key, lo, hi in regs:
+                for a, b, kind2, q2, j in hist.get(key, []):
+                    if lo < b and a < hi and ("w" in (kind, kind2) or (key[:2] == "ps" and q != q2)) and not q == q2 == "t":
+                        needs[i].add(j)
+        for key, lo, hi in writes:
+            hist[key] = [e for e in hist.get(key, []) if not (lo <= e[0] and e[1] <= hi)] + [(lo, hi, "w", q, i)]
+        for key, lo, hi in reads:
+            hist.setdefault(key, []).append((lo, hi, "r", q, i))
 
-    def walk(way, edges, back, first):
-        left, soonest = [len(n) for n in edges], list(first)
-        ready = {q: [i for i, c in enumerate(calls) if c[0] == q and not left[i]] for q in queue}
-        idle, end = {q: 0.0 for q in queue}, {}
-        for _ in calls:
-            soon, q = min((max(idle[q], min(soonest[i] for i in r)), q) for q, r in ready.items() if r)
-            start = {i: max(idle[q], soonest[i]) for i in ready[q]}
-            i = max((i for i in ready[q] if start[i] <= soon + SLACK), key=lambda i: (way[i], -i))
-            held = [h for h in ready[q] if start[h] + max(way[h], calls[h][4] + way[i]) + LOOK
-                    < max(start[i] + way[i], max(start[i] + calls[i][4], start[h]) + way[h]) and h != i]
-            i = min(held, key=lambda h: start[h] - way[h], default=i)
-            idle[q] = end[i] = start[i] + calls[i][4]
-            ready[q].remove(i)
-            for u, w in back[i].items():
-                left[u] -= 1
-                soonest[u] = max(soonest[u], end[i] + w)
-                if not left[u]:
-                    ready[calls[u][0]].append(u)
-        return end
-
-    way, walks = {}, []
-    for i in range(len(calls) - 1, -1, -1):
-        way[i] = calls[i][4] + max([late[i]] + [way[u] + w for u, w in after[i].items()])
-    for _ in range(PASSES):
-        end = walk(way, before, after, [0] * len(calls))
-        walks.append((max(end[i] + late[i] for i in end), sorted(end, key=lambda i: (end[i] - calls[i][4], i))))
-        back = walk(end, after, before, late)
-        way = {i: (way[i] + back[i]) / 2 for i in way}
-    order = min(walks)[1]
+    line = {q: [] for q in queue}
+    for r in range(ROUNDS + 2):
+        for q in queue:
+            line[q] += chains.pop((q, r, ""), [])
+            line[q] += [chains[q, r, c].pop(0) for c in TURNS.get(q, "") if chains.get((q, r, c))]
+    assert not any(chains.values())
 
     count = {s: 0 for s in own.values()}
     seen, clock, event = {q: {} for q in queue}, {}, {}
-    for i in order:
-        q, _, _, call, _, _, sem, n = calls[i]
+    while any(line.values()):
+        i = next(line[q].pop(0) for q in queue if line[q] and all(j in event for j in needs[line[q][0]]))
+        q, _, _, call, sem, n = calls[i]
         need = {}
-        for j, w in needs[i].items():
-            if w:
-                need[event[j][0]] = max(need.get(event[j][0], 0), event[j][1])
+        for j in needs[i]:
+            need[event[j][0]] = max(need.get(event[j][0], 0), event[j][1])
         need = {s: k for s, k in need.items() if seen[q].get(s, 0) < k}
         for s in sorted(need):
             if any(o != s and clock[(o, need[o])].get(s, 0) >= need[s] for o in need if need[o]):
@@ -438,7 +455,3 @@ def rank_program(g, core, T, topo):
     for s in MOVES:
         g.wait_ge(T.sem[s], 16)
     g.wait_ge(T.sem.sent, 2 * engines * ROUNDS)
-
-
-def free(q, e):
-    return e[1] == "w" and e[3] == q == "t"

@@ -19,30 +19,32 @@ def _pair(name, cols):
 
 for _n, _c in (("xb", 4 * C), ("ub", 512), ("vb", 512), ("cb", 9 * 512), ("sig", 12 * C), ("ones", 512), ("dr", C), ("t1", 4 * C),
                ("t2", 4 * C), ("mk", 8 * C), ("junk", 4 * C), ("eb", 4 * M), ("foldb", C), ("m6", C), ("m6f", C), ("pick2", C),
-               ("fp", 4 * C), ("ag", 4 * C), ("zs", 4 * C)):
+               ("fp", 4 * C), ("fq", 4 * C), ("ag", 4 * C), ("ah", 4 * C), ("zs", 4 * C)):
     _buf(_n, _c, BF)
 for _i in range(6):
     _buf("cmp%d" % _i, 4 * WIDE[_i], BF)
-for _n, _c in (("iotaj", C), ("crow", C), ("jmod", 2 * REST), ("jt", 48), ("jg", 48), ("ct0", 24), ("qg", 10), ("mask", 2 * REST),
-               ("fold", C), ("pick", 2 * REST), ("mb", C), ("hs", 4), ("ka", C), ("win", 8 * C), ("u1", 48), ("u2", 48), ("kf", C),
+for _n, _c in (("jmod", 2 * REST), ("mask", 2 * REST), ("fold", C), ("pick", 2 * REST), ("mb", C)):
+    _buf(_n, _c, BF)
+for _n, _c in (("iotaj", C), ("crow", C), ("jt", 48), ("jg", 48), ("ct0", 24), ("qg", 10), ("hs", 4), ("ka", C), ("win", 8 * C), ("u1", 48), ("u2", 48), ("kf", C),
                ("ar", 2 * C), ("ab", 2 * C), ("sm", C), ("sf", C), ("rs", 24), ("rc", 24), ("cf2", C), ("inv", C), ("itf", C),
                ("wrow", C), ("swap", C), ("crf", C), ("yb", C), ("hm", C), ("later", C)):
     _buf(_n, _c, F32)
-for _n, _c in (("cfi", 24), ("pcol", 4), ("us32", 8), ("ti", 48), ("abf", 2 * C)):
+for _n, _c in (("cfi", 24), ("pcol", 4), ("us32", 8), ("ti", 48), ("te", 20), ("abf", 2 * C)):
     _buf(_n, _c, "int32")
-for _n, _c in (("uso", 16), ("oab", 48), ("at", 48), ("pos", 24), ("it", 24), ("cl", 24)):
+for _n, _c in (("uso", 16), ("ae", 20), ("oab", 48), ("at", 48), ("pos", 24), ("it", 24), ("cl", 24)):
     _buf(_n, _c, "uint16")
-for _n, _c in (("u", 128), ("uu", 256), ("v", 128), ("w", 512), ("x", C), ("k", 9 * 128), ("t1", C), ("t2", C), ("mk", 2 * C)):
+for _n, _c in (("u", 128), ("uu", 256), ("v", 128), ("w", 512), ("x", C), ("k", 9 * 128), ("t1", C), ("t2", C), ("mk", 2 * C),
+               ("e", M)):
     _pair(_n, _c)
 for _i in range(6):
     _pair("cmp%d" % _i, WIDE[_i])
 for _r in range(ROUNDS):
-    _pair("e%d" % _r, M)
-    _pair("land%d" % _r, M)
+    _pair("land%d" % _r, C)
+    _buf("lists%d" % _r, M // 8, "uint16")
 for _b in range(8):
     _buf("ps%d" % _b, 512, F32, "psum")
 MOVES = ["ldx0", "ldu", "ldx1", "ldc", "ldw", "lds", "ldv", "stp", "stc0", "stc1", "sts0", "sts1", "sts2", "sts3", "sty0", "sty1"]
-SEMAPHORES = ["vec", "act", "ten", "pool", "sent", "arr0", "arr1", "arr2"] + MOVES
+SEMAPHORES = ["vec", "act", "ten", "pool"] + MOVES + [w + n + str(r) for w in ("in", "out") for n in "xl" for r in range(ROUNDS)]
 
 LT, GT, GE, EQ, NE = AluOpType.is_lt, AluOpType.is_gt, AluOpType.is_ge, AluOpType.is_equal, AluOpType.not_equal
 ADD, SUB, MUL, MAX, MIN = AluOpType.add, AluOpType.subtract, AluOpType.mult, AluOpType.max, AluOpType.min
@@ -55,9 +57,18 @@ BY_VECTOR = 0
 TILES = (5, 4, 3, 2, 1, 0)
 DIRECT = True
 MORE = 1
-TURNS = {"v": "fflfffffqlql" "agaggattattgttrtrcrcr" "tkktktktotototktcotdtootdtoododtoot" "ddtddottdocto" "ezezeeeezeeeezezezzzz",
-         "s": "fffff" "hhttht" "ss" + "so" * 21 + "oo" "pptptp" "ezzweeeeeweewwzzzzw",
-         "t": "ffff" "ahghtaah" "tttt" "ppoodoooodpp"}
+LAST = ((0, 256), (256, C))
+END = "fffffffjfj"
+BOTH = False
+COUNTS = True
+POOL = True
+SHARE = True
+AND = AluOpType.bitwise_and
+TURNS = {"v": "fffffcff" "ucuqcqca" "lclaagtt" "attggtti" "grtcclrr" "tkktktkt" "ototktor" "tccotdto" "otdctotd" "dtootddo" "oddotdto"
+              "toezezee" "eezmzyzy" "yyzzzbbb" "bbz",
+         "s": "lccfcffm" "fflucccm" "chmhhwmw" "tttcssss" "coomosoo" "sssossom" "sososoos" "oocsocss" "ssosssos" "opoooooo" "mpcpnnnp"
+              "ttnezzyy" "yyzzzbbb" "bz",
+         "t": "ffffahhh" "wtagattt" "tpopoodo" "pdnoonnp" "n"}
 
 
 def rank_program(g, core, T, topo):
@@ -159,10 +170,10 @@ def rank_program(g, core, T, topo):
         return ((0, n // 2), (n // 2, n)) if n >= 256 else ((0, n),)
 
     dma("s", "ldu", [], tile("ub", 0, 128)[2], T.ub[:], T.u[:])
-    dma("s", "ldc", [], at("cfi")[2], T.cfi[:], T.cf[:])
-    for i, (a, b) in enumerate(parts(C)):
+    for i, (a, b) in enumerate(LAST):
         dma("y", "ldx%d" % i, [], tile("xb", a, b)[2], T.xb[:, 4 * a:4 * b], T.x[:, 4 * a:4 * b])
-    there = tile("xb", HALF, C)[2]
+    dma("y", "ldc", [], at("cfi")[2], T.cfi[:], T.cf[:])
+    there = tile("xb", *LAST[1])[2]
     dma("y", "ldw", there, at("w_q")[2], T.w_q[:, 0:512].bitcast(dt.uint8), T.wc[:])
     dma("y", "lds", there, at("w_s")[2], T.w_s[:], T.ws[:])
     dma("y", "ldv", there, tile("vb", 0, 128)[2], T.vb[:], T.v[:])
@@ -170,102 +181,142 @@ def rank_program(g, core, T, topo):
     q_of, g_of, less_q, shift_of, place_at, twos_of, *rest = [at("qg", k, k + 1) for k in range(10)]
     row_at, further = rest[:2], rest[2:]
     iota(at("pcol", 0, 1), [[1, 1]], 0, 1, True)
-    iota(at("us32"), [[16, 8]], 0, 0, True)
     iota(at("jmod"), [[0, 2 * REST // 16], [1, 16]], 0, 0)
-    fill(at("m6"), -BIG)
+    iota(at("us32"), [[16, 8]], 0, 0, True)
     fill(at("ones"), 1.0)
-    vts(at("pcol", 1, 2), at("pcol", 0, 1), 15, None, AluOpType.bitwise_and)
+    vts(at("pcol", 1, 2), at("pcol", 0, 1), 15, None, AND)
     vts(at("pcol", 2, 3), at("pcol", 0, 1), 4, None, AluOpType.arith_shift_right)
     fill(at("uso", 8, 16), 1)
-    vcp(at("uso", 0, 8), at("us32"))
     vcp(at("qg", 0, 2), at("pcol", 1, 3))
-    fill(tile("cb", 128 * KP, 128 * K3), 256.0)
-    fill(const(K3), 3.0)
-    for k, t in ((KX, 0), (KX, 1), (KY, 0)):
-        fill(slot("cb", t, 128 * k, 128 * k + 128), -256.0)
+    act(const(KP), at("ones"), scale=256.0)
+    for k, less in ((KX, 2), (KY, 1)):
+        for t in range(4):
+            act(slot("cb", t, 128 * k, 128 * k + 128), at("ones", 0, 128), scale=-256.0 if t < less else 256.0)
+    fill(at("m6"), -BIG)
     select(at("later"), at("m6"), [[0, 3], [1, 128]], GE, BIG, 0, -1)
     iota(at("iotaj"), [[1, C]], 0, 0)
     iota(at("jt"), [[0, 2], [16, 24]], 0, 0)
-    select(const(SG), at("ones"), [[-16, 8], [0, 64]], GE, 0.0, 0, 1)
-    select(const(SG), const(SG), [[16, 8], [0, 64]], GE, 0.0, 15, -1)
+    fill(const(K3), 3.0)
     for t in (2, 3):
-        iota(slot("mk", t, C, 2 * C), [[0, C]], 0, 0)
-    for t in range(4):
-        select(const(EB0 + t), at("ones"), [[1, 512]], EQ, 0.0, -t, -4)
-    act(less_q, q_of, scale=-1.0)
-    act(shift_of, q_of, IDENT, bias=15.0 * SHIFT, scale=-SHIFT)
-    act(twos_of, q_of, IDENT, bias=30.0, scale=-2.0)
-    for i in TILES:
-        fill(tile("cmp%d" % i, 16 * (4 * i + 1), WIDE[i]), 0.0)
-    fill(slot("t2", 3), 0.0)
+        fill(slot("mk", t, C, 2 * C), 0.0)
     fill(at("rs", 0, 1), 0.0)
-    vts(place_at, q_of, -15.0, shift_of, ADD, ADD)
-    for i in range(2):
-        vts(further[i], g_of, 6.5 - i, 384.0, LT, MUL)
-        vts(row_at[i], g_of, -384.0, -384.0 * i, MUL, ADD)
+    vts(at("mask"), at("jmod"), q_of, None, EQ)
+    vcp(at("uso", 0, 8), at("us32"))
+    vts(at("fold"), at("jmod", 0, C), 0.0, -BIG, EQ, MUL)
+    vts(at("mb"), at("mask", 0, C), 2 * BIG, -BIG, MUL, ADD)
+    chain[0] = "u"
     quant("u", "ub", 0, 128)
-    vts(at("qg", 6, 8), at("qg", 6, 8), shift_of, None, SUB)
     add("v", regions(at("u_q"), at("uso")), at("uu_q")[2],
         lambda: V.tensor_copy(T.uu_q[:, 0:256].bitcast(dt.uint32), T.u_q[:, 0:128].bitcast(dt.uint32).indirect(T.uso[:, 0:16])))
-    vcp(at("cl"), at("cfi"))
-    quant("k", "cb", 128 * KP, 128 * SG)
-    act(at("mask"), at("jmod"), ABS, bias=less_q)
-    act(at("foldb"), at("jmod", 0, C), SIGN)
-    act(at("mask"), at("mask"), RELU, bias=1.0, scale=-1.0)
-    act(at("fold"), at("foldb"), IDENT, bias=-BIG, scale=BIG)
     act(at("uu_s"), by(at("u_s"), at("uso")))
-    act(at("mb"), at("mask", 0, C), IDENT, bias=-BIG, scale=2 * BIG)
-    act(at("ct0"), at("jt", 0, 24), IDENT, bias=place_at, scale=-1.0)
+    chain[0] = "c"
+    for out in [slot("t2", 3)] + [tile("cmp%d" % i, 16 * (4 * i + 1), WIDE[i]) for i in TILES]:
+        act(out, at("ones", 0, out[1]), scale=0.0)
+    quant("k", "cb", 128 * KP, 128 * SG)
+    vts(at("foldb"), at("jmod", 0, C), 0.0, None, NE)
+    vts(at("pick"), at("mask"), -256.0 * SHIFT, SHIFT, MUL, ADD)
+    vts(at("pick2"), at("mask", 0, C), -64.0, 2.0, MUL, ADD)
+    vcp(at("cl"), at("cfi"))
+    for i in range(2):
+        vts(further[i], g_of, 6.5 - i, 384.0, LT, MUL)
+    chain[0] = "m"
+    act(shift_of, q_of, IDENT, bias=15.0 * SHIFT, scale=-SHIFT)
+    act(twos_of, q_of, IDENT, bias=30.0, scale=-2.0)
+    act(place_at, q_of, IDENT, bias=15.0 * SHIFT - 15.0, scale=1.0 - SHIFT)
+    for i in range(2):
+        act(row_at[i], q_of, IDENT, bias=-15.0 * SHIFT - 384.0 * i, scale=SHIFT)
+    for i in range(2):
+        act(row_at[i], g_of, IDENT, bias=row_at[i], scale=-384.0)
+    chain[0] = "c"
     act(at("crow"), by(at("iotaj"), at("cl")), IDENT, bias=-512.0)
+    act(at("ct0"), at("jt", 0, 24), IDENT, bias=place_at, scale=-1.0)
     act(at("jt"), at("jt"), IDENT, bias=q_of)
-    act(at("pick"), at("mask"), IDENT, bias=SHIFT, scale=-256.0 * SHIFT)
     for i in range(2):
         act(at("jg", 24 * i, 24 * i + 24), at("jt", 0, 24), IDENT, bias=row_at[i])
-    act(at("pick2"), at("mask", 0, C), IDENT, bias=2.0, scale=-64.0)
-    chain[0] = "c"
-    quant("k", "cb", 128 * SG, 128 * EB0)
-    quant("v", "vb", 0, 128)
-    for a, b in parts(512):
-        quant("k", "cb", 128 * EB0 + a, 128 * EB0 + b)
     chain[0] = "q"
-    for a, b in parts(C):
+    for a, b in LAST:
         quant("x", "xb", a, b)
 
-    def turning():
+    def late_constants():
+        chain[0] = "c"
+        select(const(SG), at("ones"), [[-16, 8], [0, 64]], GE, 0.0, 0, 1)
+        select(const(SG), const(SG), [[16, 8], [0, 64]], GE, 0.0, 15, -1)
+        for t in range(4):
+            select(const(EB0 + t), at("ones"), [[1, 512]], EQ, 0.0, -t, -4)
+        quant("k", "cb", 128 * SG, 128 * EB0)
+        for a, b in parts(512):
+            quant("k", "cb", 128 * EB0 + a, 128 * EB0 + b)
+        chain[0] = "m"
+        quant("v", "vb", 0, 128)
+
+    def turning(POOL):
         chain[0] = "t"
         mm(1, "uu", 128, "x", 0, C)
         chain[0] = "g"
-        mm(6, "uu", 128, "x", 0, C)
-        vtt(at("hm"), ps(6), at("later"), MAX)
-        for b, (name, t, u) in enumerate((("t1", 0, 2), ("t1", 1, 3), ("t2", 0, 1))):
-            a, hs = 128 * b + 128, at("hs", b, b + 1)
-            chain[0] = "h"
-            mm(2 + b, "x", a - 128, "u", 0, 128)
-            act(hs, ps(2 + b, 1, 2))
-            chain[0] = "g"
-            vts(slot("t2", 2, a - 128, a), at("hm", a - 128, a), hs, 2.0, EQ, MUL)
+        if not POOL:
+            mm(6, "uu", 128, "x", 0, C)
+            vtt(at("hm"), ps(6), at("later"), MAX)
+        homes, hs = (("t1", 0, 2), ("t1", 1, 3), ("t2", 0, 1)), [at("hs", b, b + 1) for b in range(3)]
+
+        def signs(b, bank, lo, hi):
+            act(slot(*homes[b][:2], lo, hi), ps(bank, lo, hi), SIGN, bias=hs[b], scale=-1.0)
+            if POOL and lo <= 128 * b:
+                select(at("m6", 128 * b, 128 * b + 128), slot(*homes[b][:2], 128 * b, 128 * b + 128), [[1, 128]], GE, 1.0, 0, -1)
+
+        def unlike(b):
+            name, t, u = homes[b]
+            vts(slot(name, u, 0, 128 * b + 128), slot(name, t, 0, 128 * b + 128), 0.0, None, NE)
+
+        def alike(b):
+            name, t, u = homes[b]
+            vts(slot(name, u, 128 * b + 128, C), slot(name, t, 128 * b + 128, C), 0.0, 1.0, EQ, ADD)
+
+        chain[0] = "h"
+        for b in range(3):
+            mm(2 + b, "x", 128 * b, "u", 0, 128)
+            act(hs[b], ps(2 + b, 1, 2))
+        if POOL:
+            chain[0] = "w"
+            mm(6, "uu", 128, "x", 0, 256)
+            for b in range(2):
+                signs(b, 6, 0, 256)
             chain[0] = "t"
-            act(slot(name, t), ps(1), SIGN, bias=hs, scale=-1.0)
-            if b == 2:
-                quant("t1", "t1", 0, C)
-            vts(slot(name, u, 0, a), slot(name, t, 0, a), 0.0, None, NE)
-            if a < C:
-                vts(slot(name, u, a, C), slot(name, t, a, C), 0.0, 1.0, EQ, ADD)
+            for b, lo in ((2, 0), (0, 256), (1, 256)):
+                signs(b, 1, lo, C)
+            chain[0] = "i"
+            vts(slot("t2", 2), at("m6"), 0.0, 2.0, EQ, MUL)
+            chain[0] = "t"
+            for step, b in ((unlike, 0), (unlike, 1), (unlike, 2), (alike, 0), (alike, 1)):
+                step(b)
+            quant("t1", "t1", 0, C)
+        else:
+            chain[0] = "g"
+            for b in range(3):
+                vts(slot("t2", 2, 128 * b, 128 * b + 128), at("hm", 128 * b, 128 * b + 128), hs[b], 2.0, EQ, MUL)
+            chain[0] = "t"
+            for b in range(3):
+                signs(b, 1, 0, C)
+            for step, b in ((unlike, 0), (alike, 0), (unlike, 1), (alike, 1)):
+                step(b)
+            quant("t1", "t1", 0, C)
+            unlike(2)
         quant("t2", "t2", 0, C)
         for name, ks in (("t1", (KX, KP)), ("t2", (KY, KP))):
             for bank, k in zip((3, 4), ks):
                 mm(bank, "k", 128 * k, name, 0, C, name == "t1", name == "t2")
         marks = [slot("mk", m % 4, C * (m // 4), C * (m // 4) + C) for m in range(6)] + [at("m6")]
         chain[0] = "k"
-        for name, lo, bank in (("win", 7 * C, 4), ("ka", 0, 3)):
+        for name, lo, bank in (("win", 7 * C, 4), ("ka", 0, 3))[::1 if COUNTS else -1]:
             for a, b in parts(C):
                 vtt(at(name, lo + a, lo + b), ps(bank, a, b), at("crow", a, b), ADD)
-        scan(pl("win", 0), at("ka"), at("ka"), MAX, MAX)
+        if COUNTS:
+            scan(pl("win", 0), at("ka"), at("ka"), MAX, MAX)
+            chain[0] = "t"
+            scan(at("hm"), at("fold"), ps(3), MAX, MAX)
+            vtt(marks[0], at("hm"), ps(3), GT)
         chain[0] = "t"
-        scan(at("hm"), at("fold"), ps(3), MAX, MAX)
-        vtt(marks[0], at("hm"), ps(3), GT)
-        for m in range(1, 7):
-            scan(pl("win", m), marks[m - 1], pl("win", 7) if m % 2 else at("ka"), MUL, MAX)
+        for m in range(1 if COUNTS else 0, 7):
+            scan(pl("win", m), marks[m - 1] if m else at("ones", 0, C), pl("win", 7) if m % 2 else at("ka"), MUL, MAX)
             vtt(marks[m], pl("win", m), ps(3 + m % 2), GE)
         chain[0] = "d"
         for a in (0, C):
@@ -286,13 +337,13 @@ def rank_program(g, core, T, topo):
             act(pl("ar", i), by(at("win"), at("oab", 24 * i, 24 * i + 24)))
 
     def orders():
-        for a, bank in ((0, 0), (HALF, 7)):
+        for (a, b), bank in zip(LAST, (0, 7)):
             chain[0] = "a"
-            mm(bank, "uu", 0, "x", a, a + HALF)
-            vtt(at("sm", a, a + HALF), ps(bank, 0, HALF), at("mb", a, a + HALF), MIN)
-            scan(at("sf", a, a + HALF), at("fold", a, a + HALF), at("sm", a, a + HALF), ADD, MAX)
+            mm(bank, "uu", 0, "x", a, b)
+            vtt(at("sm", a, b), ps(bank, 0, b - a), at("mb", a, b), MIN)
+            scan(at("sf", a, b), at("fold", a, b), at("sm", a, b), ADD, MAX)
             chain[0] = "r"
-            vtt(slot("cmp5", 3, a, a + HALF), at("sf", a, a + HALF), ps(bank, 0, HALF), GE)
+            vtt(slot("cmp5", 3, a, b), at("sf", a, b), ps(bank, 0, b - a), GE)
         scan(at("dr"), at("foldb"), slot("cmp5", 3), MUL, ADD)
         vtt(at("rc"), at("ct0"), table("dr"), ADD)
         chain[0] = "a"
@@ -320,59 +371,67 @@ def rank_program(g, core, T, topo):
         last(at("pos"), at("rc"), table("cf2"), SUB, True)
         vcp(by(at("inv"), at("pos")), at("iotaj"))
 
-    def planes():
-        chain[0] = "p"
+    def planes(dst, src, scale):
         for t, bank in enumerate((7, 1, 0, 5)):
-            mm(bank, "k", 128 * (EB0 + t), "x", 0, C)
-            act(pl("fp", t), ps(bank), scale=16.0)
+            mm(bank, "k", 128 * (EB0 + t), src, 0, C)
+            act(pl(dst, t), ps(bank), scale=scale)
 
-    def blend(a, b, both):
+    def reads(a, b, both):
         n, k, it = b - a, (b - a) // 16, at("it", a // 16, b // 16)
         cut("itf", a, b, at("inv", a, b))
         vts(it, table("itf", a, b), shift_of, None, SUB)
         for i in range(2):
             (vcp if both and i else act)(at("ab", 2 * a + i * n, 2 * a + i * n + n), by(pl("ar", i), it))
         cut("abf", 2 * a, 2 * b, at("ab", 2 * a, 2 * b))
-        ti, a8 = at("ti", a // 8, b // 8), a // 8
-        vts(ti, table("abf", 2 * a, 2 * b), 511, None, AluOpType.bitwise_and)
-        vcp(at("at", a8, b // 8), ti)
+        ti = at("ti", a // 8, b // 8)
+        vts(ti, table("abf", 2 * a, 2 * b), 511, None, AND)
+        vcp(at("at", 0, 2 * k) if a else at("ae"), ti)
+
+    def blend(out, src, half, lists, a, b):
+        k = (b - a) // 16
         for t in range(4):
-            act(pl("ag", t, a, b), by(pl("fp", t), at("at", a8, a8 + k)))
-            vtt(pl("zs", t, a, b), by(pl("fp", t), at("at", a8 + k, a8 + 2 * k)), pl("ag", t, a, b), ADD)
+            act(pl(half, t, a, b), by(pl(src, t), at(lists, 0, k)))
+            vtt(out(t), by(pl(src, t), at(lists, k, 2 * k)), pl(half, t, a, b), ADD)
 
     nxt = T.cores[(rank + 1) % len(T.cores)]
     rid, pid = topo.addr(nxt)[:2]
     engines = len(topo.engines(core, nxt))
 
-    def send(r):
-        name, land, arr = "e%d" % r, "land%d" % r, T.sem["arr%d" % r]
-        g.remote_dma(T[land + "_q"][:, 0:M].bitcast(dt.uint8), T[name + "_q"][:, 0:M].bitcast(dt.uint8), arr, T.sem.sent, pid, rid,
-                     topo.mask(core, nxt))
-        g.remote_dma(T[land + "_s"][:, 0:M], T[name + "_s"][:, 0:M], arr, T.sem.sent, pid, rid, topo.mask(core, nxt))
+    def send(name, *pairs):
+        def call():
+            for dst, src in pairs:
+                out, in_ = [x[0].bitcast(dt.uint8) if x[2][0][0][-2:] == "_q" else x[0] for x in (dst, src)]
+                g.remote_dma(out, in_, T.sem["in" + name], T.sem["out" + name], pid, rid, topo.mask(core, nxt))
+        add("p", regions(*[src for _, src in pairs]), [], call, "out" + name, len(pairs) * engines)
+        add("p", [], regions(*[dst for dst, _ in pairs]), lambda: None, "in" + name, len(pairs) * engines)
 
     for r in range(ROUNDS):
-        more, name, land = r + 1 < ROUNDS, "e%d" % r, "land%d" % r
-        turning()
+        more, land, lists = r + 1 < ROUNDS, "land%d" % r, "lists%d" % r
+        send("x%d" % r, (at(land + "_q", 0, C), at("x_q", 0, C)), (at(land + "_s", 0, C), at("x_s", 0, C)))
+        if not r:
+            late_constants()
+        turning(POOL and r > 0)
         orders()
-        planes()
+        chain[0] = "p"
+        planes("fp", "x", 16.0)
+        chain[0] = "n"
+        planes("fq", land, 0.5)
         chain[0] = "e"
-        blend(0, M, True)
-        for t in range(4):
-            if t < 3:
-                act(slot("eb", t, 0, M), pl("zs", t, 0, M), scale=0.03125)
-            else:
-                vts(slot("eb", t, 0, M), pl("zs", t, 0, M), 0.03125, None, MUL)
-        quant(name, "eb", 0, M)
-        add("p", regions(at(name + "_q"), at(name + "_s")), regions(at(land + "_q"), at(land + "_s")), lambda r=r: send(r),
-            "arr%d" % r, 2 * engines)
+        reads(0, M, SHARE)
+        send("l%d" % r, (at(lists), at("ae")))
+        chain[0] = "y"
+        blend(lambda t: pl("zs", t, 0, M), "fp", "ag", "ae", 0, M)
         chain[0] = "z"
-        blend(M, C, False)
-        chain[0] = "w"
-        for a, b, c in ((0, REST, C), (M, M, REST), (REST, 0, M)):
-            act(at("wrow", a, a + c - b), at("inv", b, c))
+        reads(M, C, BOTH)
+        blend(lambda t: pl("zs", t, M, C), "fp", "ag", "at", M, C)
+        chain[0] = "b"
+        blend(lambda t: slot("eb", t, 0, M), "fq", "ah", lists, 0, M)
+        quant("e", "eb", 0, M)
+        chain[:] = "l" * more, r + 1
+        for i, (a, b, c) in enumerate(((0, REST, C), (M, M, REST), (REST, 0, M))):
+            select(at("wrow", a, a + c - b), at("inv", b, c), [[1, c - b]], GE, 0.0, 0, 0)
         act(at("swap"), by(at("wrow"), at("pos")))
         act(at("crow"), by(at("swap"), at("cl")), IDENT, bias=-512.0 * more)
-        chain[:] = "l", r + 1
         if more:
             for a, b in parts(C):
                 cut("crf", a, b, at("crow", a, b))
@@ -381,24 +440,24 @@ def rank_program(g, core, T, topo):
             dma("y", "stp", at("crow")[2], [], T.op[:], T.crow[0:128:16, :])
         chain[0] = "f"
         for b, bank in enumerate((1, 2, 6, 7)):
-            mm(bank, "w", 128 * b, land, 0, M)
+            mm(bank, "w", 128 * b, "e", 0, M)
             vtt(pl("zs", b, REST, C), ps(bank, 0, M), pl("zs", b, REST, C), ADD)
-        for a, c in parts(C):
+        for a, c in LAST:
             for b in range(4):
                 out, in_ = slot("xb", b, a, c), by(pl("zs", b), at("pos", a // 16, c // 16))
                 if b < 2 + (a > 0) * MORE:
                     act(out, in_, scale=0.03125)
                 else:
                     vts(out, in_, 0.03125, None, MUL)
-        chain[0] = "q"
-        for a, c in parts(C):
+            chain[0] = "q" if more else "j"
             quant("x", "xb", a, c)
+            chain[0] = "f"
 
     chain[:] = "", ROUNDS + 1
-    for i, (a, b) in enumerate(parts(C)):
+    for i, (a, b) in enumerate(LAST):
         mm(5 * i, "v", 0, "x", a, b)
         dma("y", "stc%d" % i, at("x_q", a, b)[2], [], T.oc[:, 4 * a:4 * b], T.x_q[:, a:b].bitcast(dt.uint8))
-        (vcp if i else act)(at("yb", a, b), ps(5 * i, 0, HALF))
+        (vcp if i else act)(at("yb", a, b), ps(5 * i, 0, b - a))
         dma("s", "sty%d" % i, at("yb", a, b)[2], [], T.y[:, a:b], T.yb[:, a:b])
     for k in range(4):
         dma("y", "sts%d" % k, at("x_s")[2], [], T.osc[4 * k:4 * k + 4, :], T.x_s[32 * k:32 * k + 4, 0:C])
@@ -420,7 +479,7 @@ def rank_program(g, core, T, topo):
     for r in range(ROUNDS + 2):
         for q in queue:
             line[q] += chains.pop((q, r, ""), [])
-            line[q] += [chains[q, r, c].pop(0) for c in TURNS.get(q, "") if chains.get((q, r, c))]
+            line[q] += [chains[q, r, c].pop(0) for c in (TURNS.get(q, "") if r < ROUNDS else END) if chains.get((q, r, c))]
     assert not any(chains.values())
 
     count = {s: 0 for s in own.values()}
@@ -454,4 +513,6 @@ def rank_program(g, core, T, topo):
         g.wait_ge(T.sem[s], n)
     for s in MOVES:
         g.wait_ge(T.sem[s], 16)
-    g.wait_ge(T.sem.sent, 2 * engines * ROUNDS)
+    for r in range(ROUNDS):
+        g.wait_ge(T.sem["outx%d" % r], 2 * engines)
+        g.wait_ge(T.sem["outl%d" % r], engines)

from concourse.mybir import dt, AluOpType, ActivationFunctionType

C, M, ROUNDS = 384, 160, 3
HALF, REST = C // 2, C - M
WIDE = [max(128, 64 * (i + 1)) for i in range(6)]
X4 = "float8_e4m3fn_x4"
F32, BF = "float32", "bfloat16"
SCRATCH = {}


def _buf(name, cols, dtype, where="sbuf"):
    SCRATCH[name] = (where, [128, cols], dtype)


def _pair(name, cols):
    _buf(name + "_q", cols, X4)
    _buf(name + "_s", cols, "uint8")


for _n, _c in (("xb", 4 * C), ("ub", 512), ("vb", 512), ("cb", 9 * 512), ("sig", 12 * C), ("ones", 512), ("dr", C), ("t1", 4 * C),
               ("t2", 4 * C), ("mk", 8 * C), ("junk", 4 * C), ("eb", 4 * M), ("foldb", C), ("m6", C), ("m6f", C), ("pick2", C),
               ("fp", 4 * C), ("fq", 4 * C), ("ag", 4 * C), ("ah", 4 * C), ("zs", 4 * C)):
    _buf(_n, _c, BF)
for _i in range(6):
    _buf("cmp%d" % _i, 4 * WIDE[_i], BF)
for _n, _c in (("jmod", 2 * REST), ("mask", 2 * REST), ("fold", C), ("pick", 2 * REST), ("mb", C)):
    _buf(_n, _c, BF)
for _n, _c in (("iotaj", C), ("crow", C), ("jt", 48), ("jg", 48), ("ct0", 24), ("qg", 10), ("hs", 4), ("ka", C), ("win", 8 * C), ("u1", 48), ("u2", 48), ("kf", C),
               ("ar", 2 * C), ("ab", 2 * C), ("sm", C), ("sf", C), ("rs", 24), ("rc", 24), ("cf2", C), ("inv", C), ("itf", C),
               ("wrow", C), ("swap", C), ("crf", C), ("yb", C), ("hm", C), ("later", C)):
    _buf(_n, _c, F32)
for _n, _c in (("cfi", 24), ("pcol", 4), ("us32", 8), ("ti", 48), ("te", 20), ("abf", 2 * C)):
    _buf(_n, _c, "int32")
for _n, _c in (("uso", 16), ("ae", 20), ("oab", 48), ("at", 48), ("pos", 24), ("it", 24), ("cl", 24)):
    _buf(_n, _c, "uint16")
for _n, _c in (("u", 128), ("uu", 256), ("v", 128), ("w", 512), ("x", C), ("k", 9 * 128), ("t1", C), ("t2", C), ("mk", 2 * C),
               ("e", M)):
    _pair(_n, _c)
for _i in range(6):
    _pair("cmp%d" % _i, WIDE[_i])
for _r in range(ROUNDS):
    _pair("land%d" % _r, C)
    _buf("lists%d" % _r, M // 8, "uint16")
for _b in range(8):
    _buf("ps%d" % _b, 512, F32, "psum")
MOVES = ["ldx0", "ldu", "ldx1", "ldc", "ldw", "lds", "ldv", "stp", "stc0", "stc1", "sts0", "sts1", "sts2", "sts3", "sty0", "sty1"]
SEMAPHORES = ["vec", "act", "ten", "pool"] + MOVES + [w + n + str(r) for w in ("in", "out") for n in "xl" for r in range(ROUNDS)]

LT, GT, GE, EQ, NE = AluOpType.is_lt, AluOpType.is_gt, AluOpType.is_ge, AluOpType.is_equal, AluOpType.not_equal
ADD, SUB, MUL, MAX, MIN = AluOpType.add, AluOpType.subtract, AluOpType.mult, AluOpType.max, AluOpType.min
COPY, SIGN = ActivationFunctionType.Copy, ActivationFunctionType.Sign
ABS, RELU, IDENT = ActivationFunctionType.Abs, ActivationFunctionType.Relu, ActivationFunctionType.Identity
SHIFT = 2.0 ** 18
BIG = 1e29
KP, KX, KY, K3, SG, EB0 = 0, 1, 2, 3, 4, 5
BY_VECTOR = 0
TILES = (5, 4, 3, 2, 1, 0)
DIRECT = True
MORE = 1
LAST = ((0, 256), (256, C))
END = "fffffffjfj"
BOTH = False
COUNTS = True
POOL = True
SHARE = True
AND = AluOpType.bitwise_and
TURNS = {"v": "fffffcff" "ucuqcqca" "lclaagtt" "attggtti" "grtcclrr" "tkktktkt" "ototktor" "tccotdto" "otdctotd" "dtootddo" "oddotdto"
              "toezezee" "eezmzyzy" "yyzzzbbb" "bbz",
         "s": "lccfcffm" "fflucccm" "chmhhwmw" "tttcssss" "coomosoo" "sssossom" "sososoos" "oocsocss" "ssosssos" "opoooooo" "mpcpnnnp"
              "ttnezzyy" "yyzzzbbb" "bz",
         "t": "ffffahhh" "wtagattt" "tpopoodo" "pdnoonnp" "n"}


def rank_program(g, core, T, topo):
    rank = T.rank_of(core)
    if rank is None:
        return
    V, S, P = g.vector, g.scalar, g
    queue = {"v": V, "s": S, "t": g.tensor, "p": g, "y": g.sync}
    own = {"v": "vec", "s": "act", "t": "ten", "p": "pool"}
    calls = []
    chain, chains = ["", 0], {}

    def at(name, a=0, b=None, step=1):
        b = SCRATCH[name][1][1] if b is None else b
        return T[name][:, a:b:step] if step > 1 else T[name][:, a:b], len(range(a, b, step)), [(name, a, b)], False

    def slot(name, t, a=0, b=C):
        return T[name][:, 4 * a + t:4 * (b - 1) + t + 1:4], b - a, [(name + "#%d" % t, a, b)], False

    def tile(name, a, b):
        return T[name][:, 4 * a:4 * b], 4 * (b - a), [(name + "#%d" % t, a, b) for t in range(4)], False

    def pl(name, t, a=0, b=C):
        return at(name, C * t + a, C * t + b)

    def by(win, off):
        return win[0].indirect(off[0]), 16 * off[1], win[2] + off[2], True

    def ps(bank, a=0, b=C):
        return T["ps%d" % bank][:, a:b], b - a, [("ps%d" % bank, 0, 512)], False

    def table(name, a=0, b=C):
        return at(name, a + 15, b, 16)

    def const(k):
        return tile("cb", 128 * k, 128 * k + 128)

    def ap(x):
        return x[0] if isinstance(x, tuple) else x

    def regions(*xs):
        return [r for x in xs if isinstance(x, tuple) for r in x[2]]

    def add(q, reads, writes, call, sem=None, n=1):
        chains.setdefault((q, chain[1], chain[0] if q in TURNS else ""), []).append(len(calls))
        calls.append((q, reads, writes, call, sem, n))

    def vts(out, in0, s1, s2, *ops):
        add("v", regions(in0, s1, s2), out[2], lambda: V.tensor_scalar(out[0], in0[0], ap(s1), ap(s2), *ops))

    def vtt(out, in0, in1, op):
        add("v", regions(in0, in1), out[2], lambda: V.tensor_tensor(out[0], in0[0], in1[0], op))

    def vcp(out, in_):
        lists, window = (out[2][1:], out[2][:1]) if out[3] else ([], out[2])
        add("v", in_[2] + lists, window, lambda: V.tensor_copy(out[0], in_[0]))

    def act(out, in_, func=COPY, **kw):
        add("s", regions(in_, kw.get("bias")), regions(out, kw.get("accum_out")),
            lambda: S.activation(out[0], in_[0], func, **{k: ap(x) for k, x in kw.items()}))

    def scan(out, d0, d1, op0, op1):
        add("v", regions(d0, d1), out[2], lambda: V.tensor_tensor_scan(out[0], d0[0], d1[0], 0.0, op0, op1))

    def fill(out, value):
        add("v", [], out[2], lambda: V.memset(out[0], value))

    def iota(out, pattern, base, cm, whole=False):
        kw = {} if whole else {"allow_small_or_imprecise_dtypes": True}
        add("p", [], out[2], lambda: P.iota(out[0], pattern, base, cm, **kw))

    def select(out, in_, *how):
        add("p", in_[2], out[2], lambda: P.affine_select(out[0], in_[0], *how))

    def quant(name, src, a, b):
        add("v", tile(src, a, b)[2], [(name + "_q", a, b), (name + "_s", a, b)],
            lambda: V.quantize_mx(T[name + "_q"][:, a:b], T[name + "_s"][:, a:b], tile(src, a, b)[0]))

    def mm(bank, l, la, r, ra, rb, start=True, stop=True):
        reads = [(l + "_q", la, la + 128), (l + "_s", la, la + 128), (r + "_q", ra, rb), (r + "_s", ra, rb)]
        add("t", reads, ps(bank)[2],
            lambda: g.tensor.matmul_mx(ps(bank, 0, rb - ra)[0], T[l + "_q"][:, la:la + 128], T[l + "_s"][:, la:la + 128],
                                       T[r + "_q"][:, ra:rb], T[r + "_s"][:, ra:rb], start, stop))

    def dma(q, sem, reads, writes, out, in_):
        add(q, reads, writes, lambda: queue[q].dma_start(out, in_), sem, 16)

    def cut(dst, a, b, row):
        scan(at(dst, a, b), at("pick", 0, b - a), row, ADD, MAX)

    def last(out, x, y, op, turned=False):
        if DIRECT:
            vtt(out, *((y, x) if turned else (x, y)), op)
        else:
            vtt(x, *((y, x) if turned else (x, y)), op)
            vcp(out, x)

    def parts(n):
        return ((0, n // 2), (n // 2, n)) if n >= 256 else ((0, n),)

    dma("s", "ldu", [], tile("ub", 0, 128)[2], T.ub[:], T.u[:])
    for i, (a, b) in enumerate(LAST):
        dma("y", "ldx%d" % i, [], tile("xb", a, b)[2], T.xb[:, 4 * a:4 * b], T.x[:, 4 * a:4 * b])
    dma("y", "ldc", [], at("cfi")[2], T.cfi[:], T.cf[:])
    there = tile("xb", *LAST[1])[2]
    dma("y", "ldw", there, at("w_q")[2], T.w_q[:, 0:512].bitcast(dt.uint8), T.wc[:])
    dma("y", "lds", there, at("w_s")[2], T.w_s[:], T.ws[:])
    dma("y", "ldv", there, tile("vb", 0, 128)[2], T.vb[:], T.v[:])

    q_of, g_of, less_q, shift_of, place_at, twos_of, *rest = [at("qg", k, k + 1) for k in range(10)]
    row_at, further = rest[:2], rest[2:]
    iota(at("pcol", 0, 1), [[1, 1]], 0, 1, True)
    iota(at("jmod"), [[0, 2 * REST // 16], [1, 16]], 0, 0)
    iota(at("us32"), [[16, 8]], 0, 0, True)
    fill(at("ones"), 1.0)
    vts(at("pcol", 1, 2), at("pcol", 0, 1), 15, None, AND)
    vts(at("pcol", 2, 3), at("pcol", 0, 1), 4, None, AluOpType.arith_shift_right)
    fill(at("uso", 8, 16), 1)
    vcp(at("qg", 0, 2), at("pcol", 1, 3))
    act(const(KP), at("ones"), scale=256.0)
    for k, less in ((KX, 2), (KY, 1)):
        for t in range(4):
            act(slot("cb", t, 128 * k, 128 * k + 128), at("ones", 0, 128), scale=-256.0 if t < less else 256.0)
    fill(at("m6"), -BIG)
    select(at("later"), at("m6"), [[0, 3], [1, 128]], GE, BIG, 0, -1)
    iota(at("iotaj"), [[1, C]], 0, 0)
    iota(at("jt"), [[0, 2], [16, 24]], 0, 0)
    fill(const(K3), 3.0)
    for t in (2, 3):
        fill(slot("mk", t, C, 2 * C), 0.0)
    fill(at("rs", 0, 1), 0.0)
    vts(at("mask"), at("jmod"), q_of, None, EQ)
    vcp(at("uso", 0, 8), at("us32"))
    vts(at("fold"), at("jmod", 0, C), 0.0, -BIG, EQ, MUL)
    vts(at("mb"), at("mask", 0, C), 2 * BIG, -BIG, MUL, ADD)
    chain[0] = "u"
    quant("u", "ub", 0, 128)
    add("v", regions(at("u_q"), at("uso")), at("uu_q")[2],
        lambda: V.tensor_copy(T.uu_q[:, 0:256].bitcast(dt.uint32), T.u_q[:, 0:128].bitcast(dt.uint32).indirect(T.uso[:, 0:16])))
    act(at("uu_s"), by(at("u_s"), at("uso")))
    chain[0] = "c"
    for out in [slot("t2", 3)] + [tile("cmp%d" % i, 16 * (4 * i + 1), WIDE[i]) for i in TILES]:
        act(out, at("ones", 0, out[1]), scale=0.0)
    quant("k", "cb", 128 * KP, 128 * SG)
    vts(at("foldb"), at("jmod", 0, C), 0.0, None, NE)
    vts(at("pick"), at("mask"), -256.0 * SHIFT, SHIFT, MUL, ADD)
    vts(at("pick2"), at("mask", 0, C), -64.0, 2.0, MUL, ADD)
    vcp(at("cl"), at("cfi"))
    for i in range(2):
        vts(further[i], g_of, 6.5 - i, 384.0, LT, MUL)
    chain[0] = "m"
    act(shift_of, q_of, IDENT, bias=15.0 * SHIFT, scale=-SHIFT)
    act(twos_of, q_of, IDENT, bias=30.0, scale=-2.0)
    act(place_at, q_of, IDENT, bias=15.0 * SHIFT - 15.0, scale=1.0 - SHIFT)
    for i in range(2):
        act(row_at[i], q_of, IDENT, bias=-15.0 * SHIFT - 384.0 * i, scale=SHIFT)
    for i in range(2):
        act(row_at[i], g_of, IDENT, bias=row_at[i], scale=-384.0)
    chain[0] = "c"
    act(at("crow"), by(at("iotaj"), at("cl")), IDENT, bias=-512.0)
    act(at("ct0"), at("jt", 0, 24), IDENT, bias=place_at, scale=-1.0)
    act(at("jt"), at("jt"), IDENT, bias=q_of)
    for i in range(2):
        act(at("jg", 24 * i, 24 * i + 24), at("jt", 0, 24), IDENT, bias=row_at[i])
    chain[0] = "q"
    for a, b in LAST:
        quant("x", "xb", a, b)

    def late_constants():
        chain[0] = "c"
        select(const(SG), at("ones"), [[-16, 8], [0, 64]], GE, 0.0, 0, 1)
        select(const(SG), const(SG), [[16, 8], [0, 64]], GE, 0.0, 15, -1)
        for t in range(4):
            select(const(EB0 + t), at("ones"), [[1, 512]], EQ, 0.0, -t, -4)
        quant("k", "cb", 128 * SG, 128 * EB0)
        for a, b in parts(512):
            quant("k", "cb", 128 * EB0 + a, 128 * EB0 + b)
        chain[0] = "m"
        quant("v", "vb", 0, 128)

    def turning(POOL):
        chain[0] = "t"
        mm(1, "uu", 128, "x", 0, C)
        chain[0] = "g"
        if not POOL:
            mm(6, "uu", 128, "x", 0, C)
            vtt(at("hm"), ps(6), at("later"), MAX)
        homes, hs = (("t1", 0, 2), ("t1", 1, 3), ("t2", 0, 1)), [at("hs", b, b + 1) for b in range(3)]

        def signs(b, bank, lo, hi):
            act(slot(*homes[b][:2], lo, hi), ps(bank, lo, hi), SIGN, bias=hs[b], scale=-1.0)
            if POOL and lo <= 128 * b:
                select(at("m6", 128 * b, 128 * b + 128), slot(*homes[b][:2], 128 * b, 128 * b + 128), [[1, 128]], GE, 1.0, 0, -1)

        def unlike(b):
            name, t, u = homes[b]
            vts(slot(name, u, 0, 128 * b + 128), slot(name, t, 0, 128 * b + 128), 0.0, None, NE)

        def alike(b):
            name, t, u = homes[b]
            vts(slot(name, u, 128 * b + 128, C), slot(name, t, 128 * b + 128, C), 0.0, 1.0, EQ, ADD)

        chain[0] = "h"
        for b in range(3):
            mm(2 + b, "x", 128 * b, "u", 0, 128)
            act(hs[b], ps(2 + b, 1, 2))
        if POOL:
            chain[0] = "w"
            mm(6, "uu", 128, "x", 0, 256)
            for b in range(2):
                signs(b, 6, 0, 256)
            chain[0] = "t"
            for b, lo in ((2, 0), (0, 256), (1, 256)):
                signs(b, 1, lo, C)
            chain[0] = "i"
            vts(slot("t2", 2), at("m6"), 0.0, 2.0, EQ, MUL)
            chain[0] = "t"
            for step, b in ((unlike, 0), (unlike, 1), (unlike, 2), (alike, 0), (alike, 1)):
                step(b)
            quant("t1", "t1", 0, C)
        else:
            chain[0] = "g"
            for b in range(3):
                vts(slot("t2", 2, 128 * b, 128 * b + 128), at("hm", 128 * b, 128 * b + 128), hs[b], 2.0, EQ, MUL)
            chain[0] = "t"
            for b in range(3):
                signs(b, 1, 0, C)
            for step, b in ((unlike, 0), (alike, 0), (unlike, 1), (alike, 1)):
                step(b)
            quant("t1", "t1", 0, C)
            unlike(2)
        quant("t2", "t2", 0, C)
        for name, ks in (("t1", (KX, KP)), ("t2", (KY, KP))):
            for bank, k in zip((3, 4), ks):
                mm(bank, "k", 128 * k, name, 0, C, name == "t1", name == "t2")
        marks = [slot("mk", m % 4, C * (m // 4), C * (m // 4) + C) for m in range(6)] + [at("m6")]
        chain[0] = "k"
        for name, lo, bank in (("win", 7 * C, 4), ("ka", 0, 3))[::1 if COUNTS else -1]:
            for a, b in parts(C):
                vtt(at(name, lo + a, lo + b), ps(bank, a, b), at("crow", a, b), ADD)
        if COUNTS:
            scan(pl("win", 0), at("ka"), at("ka"), MAX, MAX)
            chain[0] = "t"
            scan(at("hm"), at("fold"), ps(3), MAX, MAX)
            vtt(marks[0], at("hm"), ps(3), GT)
        chain[0] = "t"
        for m in range(1 if COUNTS else 0, 7):
            scan(pl("win", m), marks[m - 1] if m else at("ones", 0, C), pl("win", 7) if m % 2 else at("ka"), MUL, MAX)
            vtt(marks[m], pl("win", m), ps(3 + m % 2), GE)
        chain[0] = "d"
        for a in (0, C):
            for b, c in parts(C):
                quant("mk", "mk", a + b, a + c)
            mm(6, "k", 128 * K3, "mk", a, a + C, not a, a > 0)
        for a, b in parts(C):
            cut("kf", a, b, ps(6, a, b))
        for a in (0, 24):
            vtt(at("u1", a, a + 24), table("kf"), at("jg", a, a + 24), ADD)
        vtt(at("u1"), at("u1"), at("jt"), MAX)
        chain[0] = "t"
        scan(at("m6f"), at("pick2"), at("m6"), ADD, MAX)
        for i in range(2):
            vts(at("u2", 24 * i, 24 * i + 24), table("m6f"), twos_of, further[i], SUB, MUL)
        last(at("oab"), at("u2"), at("u1"), ADD)
        for i in range(2):
            act(pl("ar", i), by(at("win"), at("oab", 24 * i, 24 * i + 24)))

    def orders():
        for (a, b), bank in zip(LAST, (0, 7)):
            chain[0] = "a"
            mm(bank, "uu", 0, "x", a, b)
            vtt(at("sm", a, b), ps(bank, 0, b - a), at("mb", a, b), MIN)
            scan(at("sf", a, b), at("fold", a, b), at("sm", a, b), ADD, MAX)
            chain[0] = "r"
            vtt(slot("cmp5", 3, a, b), at("sf", a, b), ps(bank, 0, b - a), GE)
        scan(at("dr"), at("foldb"), slot("cmp5", 3), MUL, ADD)
        vtt(at("rc"), at("ct0"), table("dr"), ADD)
        chain[0] = "a"
        mm(5, "uu", 0, "x", 0, C)
        for c in range(23, 0, -1):
            score, out, a = at("sf", 16 * c + 15, 16 * c + 16), slot("cmp%d" % ((c - 1) // 4), (c - 1) % 4, 0, 16 * c), C * (c % 12)
            if c > BY_VECTOR:
                chain[0] = "s"
                act(at("sig", a, a + 16 * c), ps(5, 0, 16 * c), SIGN, bias=score, scale=-1.0)
                chain[0] = "o"
                act(out, at("sig", a, a + 16 * c), RELU, accum_out=at("rs", c, c + 1))
            else:
                chain[0] = "j"
                vts(out, ps(0, 0, 16 * c), score, None, LT)
                act(pl("junk", c % 4, 0, 16 * c), out, accum_out=at("rs", c, c + 1))
        chain[0] = "o"
        for i in TILES:
            name = "cmp%d" % i
            for a, b in parts(WIDE[i]):
                quant(name, name, a, b)
            mm(2, "k", 128 * SG, name, 0, WIDE[i], i == TILES[0], i == TILES[-1])
        vtt(at("rc"), at("rs"), at("rc"), ADD)
        for a, b in parts(C):
            cut("cf2", a, b, ps(2, a, b))
        last(at("pos"), at("rc"), table("cf2"), SUB, True)
        vcp(by(at("inv"), at("pos")), at("iotaj"))

    def planes(dst, src, scale):
        for t, bank in enumerate((7, 1, 0, 5)):
            mm(bank, "k", 128 * (EB0 + t), src, 0, C)
            act(pl(dst, t), ps(bank), scale=scale)

    def reads(a, b, both):
        n, k, it = b - a, (b - a) // 16, at("it", a // 16, b // 16)
        cut("itf", a, b, at("inv", a, b))
        vts(it, table("itf", a, b), shift_of, None, SUB)
        for i in range(2):
            (vcp if both and i else act)(at("ab", 2 * a + i * n, 2 * a + i * n + n), by(pl("ar", i), it))
        cut("abf", 2 * a, 2 * b, at("ab", 2 * a, 2 * b))
        ti = at("ti", a // 8, b // 8)
        vts(ti, table("abf", 2 * a, 2 * b), 511, None, AND)
        vcp(at("at", 0, 2 * k) if a else at("ae"), ti)

    def blend(out, src, half, lists, a, b):
        k = (b - a) // 16
        for t in range(4):
            act(pl(half, t, a, b), by(pl(src, t), at(lists, 0, k)))
            vtt(out(t), by(pl(src, t), at(lists, k, 2 * k)), pl(half, t, a, b), ADD)

    nxt = T.cores[(rank + 1) % len(T.cores)]
    rid, pid = topo.addr(nxt)[:2]
    engines = len(topo.engines(core, nxt))

    def send(name, *pairs):
        def call():
            for dst, src in pairs:
                out, in_ = [x[0].bitcast(dt.uint8) if x[2][0][0][-2:] == "_q" else x[0] for x in (dst, src)]
                g.remote_dma(out, in_, T.sem["in" + name], T.sem["out" + name], pid, rid, topo.mask(core, nxt))
        add("p", regions(*[src for _, src in pairs]), [], call, "out" + name, len(pairs) * engines)
        add("p", [], regions(*[dst for dst, _ in pairs]), lambda: None, "in" + name, len(pairs) * engines)

    for r in range(ROUNDS):
        more, land, lists = r + 1 < ROUNDS, "land%d" % r, "lists%d" % r
        send("x%d" % r, (at(land + "_q", 0, C), at("x_q", 0, C)), (at(land + "_s", 0, C), at("x_s", 0, C)))
        if not r:
            late_constants()
        turning(POOL and r > 0)
        orders()
        chain[0] = "p"
        planes("fp", "x", 16.0)
        chain[0] = "n"
        planes("fq", land, 0.5)
        chain[0] = "e"
        reads(0, M, SHARE)
        send("l%d" % r, (at(lists), at("ae")))
        chain[0] = "y"
        blend(lambda t: pl("zs", t, 0, M), "fp", "ag", "ae", 0, M)
        chain[0] = "z"
        reads(M, C, BOTH)
        blend(lambda t: pl("zs", t, M, C), "fp", "ag", "at", M, C)
        chain[0] = "b"
        blend(lambda t: slot("eb", t, 0, M), "fq", "ah", lists, 0, M)
        quant("e", "eb", 0, M)
        chain[:] = "l" * more, r + 1
        for i, (a, b, c) in enumerate(((0, REST, C), (M, M, REST), (REST, 0, M))):
            select(at("wrow", a, a + c - b), at("inv", b, c), [[1, c - b]], GE, 0.0, 0, 0)
        act(at("swap"), by(at("wrow"), at("pos")))
        act(at("crow"), by(at("swap"), at("cl")), IDENT, bias=-512.0 * more)
        if more:
            for a, b in parts(C):
                cut("crf", a, b, at("crow", a, b))
            vts(at("cl"), table("crf"), shift_of, 512.0, SUB, ADD)
        else:
            dma("y", "stp", at("crow")[2], [], T.op[:], T.crow[0:128:16, :])
        chain[0] = "f"
        for b, bank in enumerate((1, 2, 6, 7)):
            mm(bank, "w", 128 * b, "e", 0, M)
            vtt(pl("zs", b, REST, C), ps(bank, 0, M), pl("zs", b, REST, C), ADD)
        for a, c in LAST:
            for b in range(4):
                out, in_ = slot("xb", b, a, c), by(pl("zs", b), at("pos", a // 16, c // 16))
                if b < 2 + (a > 0) * MORE:
                    act(out, in_, scale=0.03125)
                else:
                    vts(out, in_, 0.03125, None, MUL)
            chain[0] = "q" if more else "j"
            quant("x", "xb", a, c)
            chain[0] = "f"

    chain[:] = "", ROUNDS + 1
    for i, (a, b) in enumerate(LAST):
        mm(5 * i, "v", 0, "x", a, b)
        dma("y", "stc%d" % i, at("x_q", a, b)[2], [], T.oc[:, 4 * a:4 * b], T.x_q[:, a:b].bitcast(dt.uint8))
        (vcp if i else act)(at("yb", a, b), ps(5 * i, 0, b - a))
        dma("s", "sty%d" % i, at("yb", a, b)[2], [], T.y[:, a:b], T.yb[:, a:b])
    for k in range(4):
        dma("y", "sts%d" % k, at("x_s")[2], [], T.osc[4 * k:4 * k + 4, :], T.x_s[32 * k:32 * k + 4, 0:C])

    hist, needs = {}, []
    for i, (q, reads, writes, *_) in enumerate(calls):
        needs.append(set())
        for kind, regs in (("r", reads), ("w", writes)):
            for key, lo, hi in regs:
                for a, b, kind2, q2, j in hist.get(key, []):
                    if lo < b and a < hi and ("w" in (kind, kind2) or (key[:2] == "ps" and q != q2)) and not q == q2 == "t":
                        needs[i].add(j)
        for key, lo, hi in writes:
            hist[key] = [e for e in hist.get(key, []) if not (lo <= e[0] and e[1] <= hi)] + [(lo, hi, "w", q, i)]
        for key, lo, hi in reads:
            hist.setdefault(key, []).append((lo, hi, "r", q, i))

    line = {q: [] for q in queue}
    for r in range(ROUNDS + 2):
        for q in queue:
            line[q] += chains.pop((q, r, ""), [])
            line[q] += [chains[q, r, c].pop(0) for c in (TURNS.get(q, "") if r < ROUNDS else END) if chains.get((q, r, c))]
    assert not any(chains.values())

    count = {s: 0 for s in own.values()}
    seen, clock, event = {q: {} for q in queue}, {}, {}
    while any(line.values()):
        i = next(line[q].pop(0) for q in queue if line[q] and all(j in event for j in needs[line[q][0]]))
        q, _, _, call, sem, n = calls[i]
        need = {}
        for j in needs[i]:
            need[event[j][0]] = max(need.get(event[j][0], 0), event[j][1])
        need = {s: k for s, k in need.items() if seen[q].get(s, 0) < k}
        for s in sorted(need):
            if any(o != s and clock[(o, need[o])].get(s, 0) >= need[s] for o in need if need[o]):
                need[s] = 0
        for s, k in need.items():
            if k and seen[q].get(s, 0) < k:
                queue[q].wait_ge(T.sem[s], k)
                for s2, k2 in clock[(s, k)].items():
                    seen[q][s2] = max(seen[q].get(s2, 0), k2)
        made = call()
        if sem is None:
            sem = own[q]
            count[sem] += 1
            n = count[sem]
            made.then_inc(T.sem[sem], 1)
        elif made is not None:
            made.then_inc(T.sem[sem], n)
        event[i] = (sem, n)
        clock[event[i]] = {**(seen[q] if made is not None else {}), sem: n}
    for s, n in count.items():
        g.wait_ge(T.sem[s], n)
    for s in MOVES:
        g.wait_ge(T.sem[s], 16)
    for r in range(ROUNDS):
        g.wait_ge(T.sem["outx%d" % r], 2 * engines)
        g.wait_ge(T.sem["outl%d" % r], engines)
